import numpy as np
import ml_dtypes


def mxq(x, axis, fmt="e4m3"):
    dtype, down = {"e4m3": (ml_dtypes.float8_e4m3fn, 7), "e5m2": (ml_dtypes.float8_e5m2, 14)}[fmt]
    v = np.moveaxis(np.asarray(x, np.float32).astype(ml_dtypes.bfloat16).astype(np.float64), axis, -1)
    blocks = v.reshape(v.shape[:-1] + (-1, 32))
    amax = np.abs(blocks).max(-1, keepdims=True)
    byte = np.maximum(np.where(amax > 0, np.frexp(amax)[1] - 1 + 127, 0) - down, 1)
    scale = np.exp2(byte - 127.0)
    codes = (blocks / scale).astype(np.float32).astype(dtype).astype(np.float64)
    return np.moveaxis((codes * scale).reshape(v.shape), -1, axis)


WIDE = False


def mx_kscale(k):
    if not WIDE:
        return np.ones(k)
    levels = np.array([10, -10, 5, -5, 0])
    if k % 512:
        return np.exp2(np.random.permutation(np.resize(levels, k // 32))).repeat(32)
    a = np.empty((k // 512, 16))
    for p in range(k // 512):
        a[p, :8] = np.random.permutation(np.resize(levels, 8))
        for g in range(8):
            far = levels[np.abs(levels - a[p, g]) >= 10]
            a[p, g + 8] = far[np.random.randint(len(far))]
    return np.exp2(a.ravel()).repeat(32)


def f64(x):
    return np.asarray(x).astype(np.float64)


def striped(idx):
    return np.tile(idx.reshape(-1, 16).T, (8, 1)).astype(np.uint16)


def unstriped(offs):
    return offs[:16].T.reshape(-1).astype(np.int64)


def pack_weight(w):
    k, n = w.shape
    w = f64(np.asarray(w, np.float32).astype(ml_dtypes.bfloat16)).reshape(k // 32, 32, n)
    amax = np.abs(w).max(1)
    byte = np.clip(np.where(amax > 0, np.frexp(amax)[1] - 1 + 127 - 7, 1), 1, 254)
    scaled = (w * np.exp2(127.0 - byte)[:, None, :]).reshape(k, n).astype(np.float32)
    words = np.ascontiguousarray(scaled.reshape(k // 512, 128, 4, n).transpose(0, 1, 3, 2)).astype(ml_dtypes.float8_e4m3fn).view(np.uint8)
    return words, np.ascontiguousarray(byte.astype(np.uint8).reshape(k // 512, 16, n))


def unpack_weight(words, scales):
    g, p, n, _ = words.shape
    vals = np.ascontiguousarray(words).view(ml_dtypes.float8_e4m3fn).astype(np.float64) * np.repeat(np.exp2(scales.astype(np.float64) - 127.0), 8, axis=1)[..., None]
    return vals.transpose(0, 1, 3, 2).reshape(g * 512, n)


def relu(v):
    return np.maximum(v, 0.0)


K, T, H, N = 512, 1024, 512, 128


def setup_inputs():
    n = np.random.standard_normal
    s = mx_kscale(K)[:, None]
    u = mx_kscale(H)
    packed_xT = pack_weight(n((K, T)) * s)
    return {
        "x_words": packed_xT[0],
        "x_scales": packed_xT[1],
        "w1": (n((K, H)) / np.sqrt(K) / s * u).astype(np.float32),
        "w2": (n((H, N)) / np.sqrt(2 * H) / u[:, None]).astype(np.float32),
        "w3": (n((H, N)) / np.sqrt(2 * H) / u[:, None]).astype(np.float32),
        "pos1": striped(np.random.permutation(T)),
        "pos2": striped(np.random.permutation(T)),
    }


def reference(x_words, x_scales, w1, w2, w3, pos1, pos2):
    xq = unpack_weight(x_words, x_scales)
    h = relu(mxq(f64(w1), 0, "e4m3").T @ xq)
    z = np.maximum(h[:, unstriped(pos1)], h[:, unstriped(pos2)])
    return mxq(f64(w2), 0, "e4m3").T @ mxq(h, 0, "e4m3") + mxq(f64(w3), 0, "e4m3").T @ mxq(z, 0, "e4m3")

@@ -1,0 +1,249 @@
+from contextlib import ExitStack
+
+import concourse.mybir as mybir
+
+K, T, H, N = 512, 1024, 512, 128
+FLOPS = 2 * K * H * T + 2 * 2 * H * N * T
+
+F32 = mybir.dt.float32
+BF16 = mybir.dt.bfloat16
+I32 = mybir.dt.int32
+U32 = mybir.dt.uint32
+U16 = mybir.dt.uint16
+U8 = mybir.dt.uint8
+FP8X4 = mybir.dt.float8_e4m3fn_x4
+MAX = mybir.AluOpType.max
+RELU = mybir.ActivationFunctionType.Relu
+
+P = 128
+PACK = 4
+BANK = 512
+RUN = 4
+GAP = 8
+CHUNKS = (512, 256, 128, 128)
+
+
+def tile_picked_wsagecat_max_l_kernel(
+    tc, x_words, x_scales, w1, w2, w3, pos1, pos2, out
+):
+    nc = tc.nc
+    with ExitStack() as ctx:
+        keep = ctx.enter_context(tc.tile_pool(name="keep", bufs=1))
+        raw = ctx.enter_context(tc.tile_pool(name="raw", bufs=2))
+        psum_h = ctx.enter_context(tc.psum_pool(name="psum_h", bufs=6))
+        psum_o = ctx.enter_context(tc.psum_pool(name="psum_o", bufs=2))
+
+        lists = [keep.tile([P, T // 16], U16, name="list%d" % d) for d in range(2)]
+        x_codes = keep.tile([P, T], U32, align_bytes=64)
+        x_plane = keep.tile([P, T], U8, align_bytes=64)
+
+        w1_rows = w1.rearrange("(p j) c -> p j c", j=PACK)
+        half = H // 2
+        w1_raw = []
+        for u in range(2):
+            w_half = raw.tile([P, PACK, half], F32, name="w_half", tag="raw")
+            nc.sync.dma_start(out=w_half[:], in_=w1_rows[:, :, u * half : (u + 1) * half])
+            w1_raw.append(w_half)
+        nc.sync.dma_start(
+            out=x_codes[:].bitcast(I32),
+            in_=x_words[0].rearrange("p n t -> p (n t)").bitcast(I32),
+        )
+        nc.vector.memset(x_plane[:].bitcast(I32), 0)
+        for q in range(4):
+            nc.scalar.dma_start(
+                out=x_plane[32 * q : 32 * q + 4, :].bitcast(I32),
+                in_=x_scales[0, 4 * q : 4 * q + 4, :].bitcast(I32),
+            )
+        nc.sync.dma_start(lists[0][:], pos1)
+        nc.sync.dma_start(lists[1][:], pos2)
+
+        w1_bf = keep.tile([P, PACK, P, PACK], BF16, align_bytes=64)
+        w1_codes = keep.tile([P, PACK, P], U32, align_bytes=64)
+        w1_plane = keep.tile([P, PACK, P], U8, align_bytes=64)
+        mh = P // 2
+
+        def cast_w1(u, t0, t1):
+            nc.vector.tensor_copy(
+                out=w1_bf[:, t0:t1, u * mh : (u + 1) * mh, :].rearrange("p t m j -> p m j t"),
+                in_=w1_raw[u][:].rearrange("p j (m t) -> p m j t", t=PACK)[:, :, :, t0:t1],
+            )
+
+        def quant_w1(t):
+            nc.vector.quantize_mx(
+                out=w1_codes[:, t, :].bitcast(FP8X4),
+                scales=w1_plane[:, t, :],
+                in_=w1_bf[:, t, :, :].rearrange("p m j -> p (m j)"),
+            )
+
+        cast_w1(0, 0, 4)
+        cast_w1(1, 0, 1)
+        cast_w1(1, 1, 2)
+        quant_w1(0)
+        quant_w1(1)
+        cast_w1(1, 2, 4)
+        quant_w1(2)
+        quant_w1(3)
+
+        h = keep.tile([P, PACK * T], F32, align_bytes=64)
+
+        def h_piece(t, c0, c1, on_vector):
+            acc = psum_h.tile([P, BANK], F32, name="acc_h")
+            nc.tensor.matmul_mx(
+                out=acc[:, : c1 - c0],
+                lhsT=w1_codes[:, t, :].bitcast(FP8X4),
+                lhsT_scale=w1_plane[:, t, :],
+                rhs=x_codes[:, c0:c1].bitcast(FP8X4),
+                rhs_scale=x_plane[:, c0:c1],
+                start=True,
+                stop=True,
+            )
+            dst = h[:, t * T + c0 : t * T + c1]
+            if on_vector:
+                nc.vector.tensor_scalar_max(dst, acc[:, : c1 - c0], 0.0)
+            else:
+                nc.scalar.activation(dst, acc[:, : c1 - c0], RELU)
+
+        h_piece(0, 0, 512, False)
+        h_piece(0, 512, 768, True)
+        h_piece(0, 768, 1024, False)
+        for t in (1, 2, 3):
+            h_piece(t, 0, 512, False)
+            h_piece(t, 512, 1024, False)
+
+        w23_bf = keep.tile([P, 2, N, PACK], BF16, align_bytes=64)
+        w23_codes = keep.tile([P, 2 * N], U32, align_bytes=64)
+        w23_plane = keep.tile([P, 2 * N], U8, align_bytes=64)
+        for s, w in enumerate((w2, w3)):
+            w_out = raw.tile([P, PACK, N], F32, name="w_out", tag="raw")
+            nc.sync.dma_start(out=w_out[:], in_=w.rearrange("(p j) n -> p j n", j=PACK))
+            nc.scalar.copy(
+                out=w23_bf[:, s, :, :].rearrange("p (c i) j -> p c j i", i=RUN),
+                in_=w_out[:].rearrange("p j (c i) -> p c j i", i=RUN),
+            )
+        nc.vector.quantize_mx(
+            out=w23_codes[:].bitcast(FP8X4),
+            scales=w23_plane[:],
+            in_=w23_bf[:].rearrange("p s n j -> p (s n j)"),
+        )
+
+        h_planes = h[:].rearrange("p (t c) -> p t c", t=PACK)
+
+        HB = 0
+        G0 = HB + PACK * T
+        STEP0 = 2 * (512 + 2 * GAP)
+        ZB = [G0 + PACK * STEP0]
+        for n in CHUNKS:
+            ZB.append(ZB[-1] + PACK * n)
+        work = keep.tile([P, ZB[-1]], BF16, align_bytes=64)
+        h_codes = keep.tile([P, T], U32, align_bytes=64)
+        h_plane = keep.tile([P, T], U8, align_bytes=64)
+        z_codes = keep.tile([P, T], U32, align_bytes=64)
+        z_plane = keep.tile([P, T], U8, align_bytes=64)
+
+        def rows(base, n, steps=1, pitch=None):
+            width = n + 2 * GAP
+            if pitch is None:
+                pitch = width
+            block = work[:, base : base + steps * pitch].rearrange("p (s r) -> p s r", s=steps)
+            return block[:, :, :width].rearrange("p s (u c) -> p s u c", u=2)[:, :, :, : n // 2]
+
+        def gather(t, d, c0, n, base):
+            nc.vector.tensor_copy(
+                rows(base, n)[:, 0, :, :],
+                h[:, t * T : (t + 1) * T].indirect(lists[d][:, c0 // 16 : (c0 + n) // 16]),
+            )
+
+        def largest(z_base, n, t0, steps, base_a, base_b, pitch):
+            dst = work[:, z_base + t0 * n : z_base + (t0 + steps) * n]
+            nc.vector.tensor_tensor(
+                dst.rearrange("p (s u c) -> p s u c", s=steps, u=2),
+                rows(base_a, n, steps, pitch),
+                rows(base_b, n, steps, pitch),
+                MAX,
+            )
+
+        def weave(engine_copy, dst_base, src, n):
+            engine_copy(
+                out=work[:, dst_base : dst_base + PACK * n].rearrange("p (c i t) -> p c t i", i=RUN, t=PACK),
+                in_=src.rearrange("p t (c i) -> p c t i", i=RUN),
+            )
+
+        def z_planes(z_base, n):
+            return work[:, z_base : z_base + PACK * n].rearrange("p (t c) -> p t c", t=PACK)
+
+        def quantise(codes, plane, c0, n, base):
+            nc.vector.quantize_mx(
+                out=codes[:, c0 : c0 + n].bitcast(FP8X4),
+                scales=plane[:, c0 : c0 + n],
+                in_=work[:, base : base + PACK * n],
+            )
+
+        def quantise_halves(codes, plane, c0, n, base):
+            quantise(codes, plane, c0, n // 2, base)
+            quantise(codes, plane, c0 + n // 2, n // 2, base + PACK * n // 2)
+
+        def finish(c0, n):
+            acc = psum_o.tile([P, BANK], F32, name="acc_o")
+            for s, (codes, plane) in enumerate(((h_codes, h_plane), (z_codes, z_plane))):
+                nc.tensor.matmul_mx(
+                    out=acc[:, :n],
+                    lhsT=w23_codes[:, s * N : (s + 1) * N].bitcast(FP8X4),
+                    lhsT_scale=w23_plane[:, s * N : (s + 1) * N],
+                    rhs=codes[:, c0 : c0 + n].bitcast(FP8X4),
+                    rhs_scale=plane[:, c0 : c0 + n],
+                    start=(s == 0),
+                    stop=(s == 1),
+                )
+            result = keep.tile([P, n], F32, name="result%d" % c0)
+            nc.scalar.copy(out=result[:], in_=acc[:, :n])
+            nc.sync.dma_start(out=out[:, c0 : c0 + n], in_=result[:])
+
+        for u in range(2):
+            weave(nc.scalar.copy, HB + u * 2048, h_planes[:, :, u * 512 : (u + 1) * 512], 512)
+
+        half0 = STEP0 // 2
+        for t in range(PACK):
+            for d in range(2):
+                gather(t, d, 0, 512, G0 + t * STEP0 + d * half0)
+        quantise_halves(h_codes, h_plane, 0, 512, HB)
+        for t0 in (0, 2):
+            largest(HB, 512, t0, 2, G0 + t0 * STEP0, G0 + t0 * STEP0 + half0, STEP0)
+        weave(nc.scalar.copy, ZB[0], z_planes(HB, 512), 512)
+
+        for t in range(PACK):
+            for d in range(2):
+                gather(t, d, 512, 256, G0 + t * STEP0 + d * half0)
+        quantise_halves(h_codes, h_plane, 512, 512, HB + 2048)
+        for t0 in (0, 2):
+            largest(HB + 2048, 256, t0, 2, G0 + t0 * STEP0, G0 + t0 * STEP0 + half0, STEP0)
+        weave(nc.scalar.copy, ZB[1], z_planes(HB + 2048, 256), 256)
+        quantise_halves(z_codes, z_plane, 0, 512, ZB[0])
+        finish(0, 512)
+
+        one = 128 + 2 * GAP
+        step = 2 * one
+        for t in range(PACK):
+            for d in range(2):
+                gather(t, d, 768, 128, ZB[0] + t * step + d * one)
+        quantise_halves(z_codes, z_plane, 512, 256, ZB[1])
+        for t0 in (0, 2):
+            largest(ZB[1], 128, t0, 2, ZB[0] + t0 * step, ZB[0] + t0 * step + one, step)
+        weave(nc.scalar.copy, ZB[2], z_planes(ZB[1], 128), 128)
+        finish(512, 256)
+
+        z3 = HB + 3072
+        for t in range(2):
+            for d in range(2):
+                gather(t, d, 896, 128, ZB[0] + t * step + d * one)
+        gather(2, 0, 896, 128, ZB[0] + 2 * step)
+        largest(z3, 128, 0, 2, ZB[0], ZB[0] + one, step)
+        quantise_halves(z_codes, z_plane, 768, 128, ZB[2])
+        finish(768, 128)
+        gather(2, 1, 896, 128, ZB[2])
+        gather(3, 0, 896, 128, ZB[2] + one)
+        largest(z3, 128, 2, 1, ZB[0] + 2 * step, ZB[2], None)
+        gather(3, 1, 896, 128, ZB[2] + 2 * one)
+        largest(z3, 128, 3, 1, ZB[2] + one, ZB[2] + 2 * one, None)
+        weave(nc.vector.tensor_copy, ZB[3], z_planes(z3, 128), 128)
+        quantise(z_codes, z_plane, 896, 128, ZB[3])
+        finish(896, 128)

@@ -18,9 +18,24 @@ RELU = mybir.ActivationFunctionType.Relu
 P = 128
 PACK = 4
 BANK = 512
-RUN = 4
-GAP = 8
-CHUNKS = (512, 256, 128, 128)
+NEAR = 4
+QUARTER = T // 4
+RUN = 64
+PITCH = RUN + 8
+SPARE = 384
+CHUNKS = ((0, 640), (640, 256), (896, 128))
+
+
+def pieces(n, widest):
+    cut = []
+    start = 0
+    while start < n:
+        width = widest
+        while width > n - start:
+            width = width // 2
+        cut.append((start, width))
+        start = start + width
+    return cut
 
 
 def tile_picked_wsagecat_max_l_kernel(
@@ -30,13 +45,16 @@ def tile_picked_wsagecat_max_l_kernel(
     with ExitStack() as ctx:
         keep = ctx.enter_context(tc.tile_pool(name="keep", bufs=1))
         raw = ctx.enter_context(tc.tile_pool(name="raw", bufs=2))
-        psum_h = ctx.enter_context(tc.psum_pool(name="psum_h", bufs=6))
-        psum_o = ctx.enter_context(tc.psum_pool(name="psum_o", bufs=2))
+        psum_h = ctx.enter_context(tc.psum_pool(name="psum_h", bufs=5))
+        psum_o = ctx.enter_context(tc.psum_pool(name="psum_o", bufs=3))
 
         lists = [keep.tile([P, T // 16], U16, name="list%d" % d) for d in range(2)]
         x_codes = keep.tile([P, T], U32, align_bytes=64)
-        x_plane = keep.tile([P, T], U8, align_bytes=64)
+        x_plane = keep.tile([P, QUARTER], U8, align_bytes=64)
+        h = keep.tile([P, PACK * T + SPARE], F32, align_bytes=64)
 
+        nc.vector.memset(x_plane[:].bitcast(I32), 0)
+        nc.vector.memset(h[:, PACK * T :], 0.0)
         w1_rows = w1.rearrange("(p j) c -> p j c", j=PACK)
         half = H // 2
         w1_raw = []
@@ -44,16 +62,16 @@ def tile_picked_wsagecat_max_l_kernel(
             w_half = raw.tile([P, PACK, half], F32, name="w_half", tag="raw")
             nc.sync.dma_start(out=w_half[:], in_=w1_rows[:, :, u * half : (u + 1) * half])
             w1_raw.append(w_half)
-        nc.sync.dma_start(
-            out=x_codes[:].bitcast(I32),
-            in_=x_words[0].rearrange("p n t -> p (n t)").bitcast(I32),
-        )
-        nc.vector.memset(x_plane[:].bitcast(I32), 0)
-        for q in range(4):
-            nc.scalar.dma_start(
-                out=x_plane[32 * q : 32 * q + 4, :].bitcast(I32),
-                in_=x_scales[0, 4 * q : 4 * q + 4, :].bitcast(I32),
-            )
+            if u == 0:
+                for q in range(4):
+                    nc.sync.dma_start(
+                        out=x_plane[32 * q : 32 * q + 16, :].bitcast(I32),
+                        in_=x_scales[0, 4 * q : 4 * q + 4, :].bitcast(I32).rearrange("r (a c) -> a r c", a=4),
+                    )
+        x_rows = x_words[0].rearrange("p n t -> p (n t)").bitcast(I32)
+        for u in range(2):
+            cols = slice(u * T // 2, (u + 1) * T // 2)
+            nc.sync.dma_start(out=x_codes[:, cols].bitcast(I32), in_=x_rows[:, cols])
         nc.sync.dma_start(lists[0][:], pos1)
         nc.sync.dma_start(lists[1][:], pos2)
 
@@ -61,52 +79,45 @@ def tile_picked_wsagecat_max_l_kernel(
         w1_codes = keep.tile([P, PACK, P], U32, align_bytes=64)
         w1_plane = keep.tile([P, PACK, P], U8, align_bytes=64)
         mh = P // 2
-
-        def cast_w1(u, t0, t1):
-            nc.vector.tensor_copy(
-                out=w1_bf[:, t0:t1, u * mh : (u + 1) * mh, :].rearrange("p t m j -> p m j t"),
-                in_=w1_raw[u][:].rearrange("p j (m t) -> p m j t", t=PACK)[:, :, :, t0:t1],
-            )
-
-        def quant_w1(t):
+        for u in range(2):
+            for t0 in (2, 0):
+                nc.vector.tensor_copy(
+                    out=w1_bf[:, t0 : t0 + 2, u * mh : (u + 1) * mh, :].rearrange("p t m j -> p m j t"),
+                    in_=w1_raw[u][:].rearrange("p j (m t) -> p m j t", t=PACK)[:, :, :, t0 : t0 + 2],
+                )
+        for t in (3, 2, 1, 0):
             nc.vector.quantize_mx(
                 out=w1_codes[:, t, :].bitcast(FP8X4),
                 scales=w1_plane[:, t, :],
                 in_=w1_bf[:, t, :, :].rearrange("p m j -> p (m j)"),
             )
 
-        cast_w1(0, 0, 4)
-        cast_w1(1, 0, 1)
-        cast_w1(1, 1, 2)
-        quant_w1(0)
-        quant_w1(1)
-        cast_w1(1, 2, 4)
-        quant_w1(2)
-        quant_w1(3)
-
-        h = keep.tile([P, PACK * T], F32, align_bytes=64)
-
         def h_piece(t, c0, c1, on_vector):
             acc = psum_h.tile([P, BANK], F32, name="acc_h")
-            nc.tensor.matmul_mx(
-                out=acc[:, : c1 - c0],
-                lhsT=w1_codes[:, t, :].bitcast(FP8X4),
-                lhsT_scale=w1_plane[:, t, :],
-                rhs=x_codes[:, c0:c1].bitcast(FP8X4),
-                rhs_scale=x_plane[:, c0:c1],
-                start=True,
-                stop=True,
-            )
+            for b0 in range(c0, c1, QUARTER):
+                b1 = min(b0 + QUARTER, c1)
+                a, r = divmod(b0, QUARTER)
+                nc.tensor.matmul_mx(
+                    out=acc[:, b0 - c0 : b1 - c0],
+                    lhsT=w1_codes[:, t, :].bitcast(FP8X4),
+                    lhsT_scale=w1_plane[:, t, :],
+                    rhs=x_codes[:, b0:b1].bitcast(FP8X4),
+                    rhs_scale=x_plane[4 * a :, r : r + b1 - b0],
+                    start=True,
+                    stop=True,
+                )
             dst = h[:, t * T + c0 : t * T + c1]
             if on_vector:
                 nc.vector.tensor_scalar_max(dst, acc[:, : c1 - c0], 0.0)
             else:
                 nc.scalar.activation(dst, acc[:, : c1 - c0], RELU)
 
-        h_piece(0, 0, 512, False)
-        h_piece(0, 512, 768, True)
-        h_piece(0, 768, 1024, False)
-        for t in (1, 2, 3):
+        h_piece(3, 0, 256, False)
+        h_piece(3, 256, 512, True)
+        h_piece(3, 512, 768, False)
+        h_piece(3, 768, 896, True)
+        h_piece(3, 896, 1024, False)
+        for t in (2, 1, 0):
             h_piece(t, 0, 512, False)
             h_piece(t, 512, 1024, False)
 
@@ -117,8 +128,8 @@ def tile_picked_wsagecat_max_l_kernel(
             w_out = raw.tile([P, PACK, N], F32, name="w_out", tag="raw")
             nc.sync.dma_start(out=w_out[:], in_=w.rearrange("(p j) n -> p j n", j=PACK))
             nc.scalar.copy(
-                out=w23_bf[:, s, :, :].rearrange("p (c i) j -> p c j i", i=RUN),
-                in_=w_out[:].rearrange("p j (c i) -> p c j i", i=RUN),
+                out=w23_bf[:, s, :, :].rearrange("p (c i) j -> p c j i", i=NEAR),
+                in_=w_out[:].rearrange("p j (c i) -> p c j i", i=NEAR),
             )
         nc.vector.quantize_mx(
             out=w23_codes[:].bitcast(FP8X4),
@@ -126,124 +137,120 @@ def tile_picked_wsagecat_max_l_kernel(
             in_=w23_bf[:].rearrange("p s n j -> p (s n j)"),
         )
 
-        h_planes = h[:].rearrange("p (t c) -> p t c", t=PACK)
+        def span(n):
+            return n // RUN * PITCH
 
         HB = 0
-        G0 = HB + PACK * T
-        STEP0 = 2 * (512 + 2 * GAP)
-        ZB = [G0 + PACK * STEP0]
-        for n in CHUNKS:
-            ZB.append(ZB[-1] + PACK * n)
-        work = keep.tile([P, ZB[-1]], BF16, align_bytes=64)
+        ZB = HB + PACK * T
+        G_HIGH = ZB + PACK * T
+        G_LOW = G_HIGH + 4 * span(T)
+        WIDTH = G_LOW + 4 * span(640) + span(T)
+        work = keep.tile([P, WIDTH], BF16, align_bytes=64)
         h_codes = keep.tile([P, T], U32, align_bytes=64)
         h_plane = keep.tile([P, T], U8, align_bytes=64)
         z_codes = keep.tile([P, T], U32, align_bytes=64)
         z_plane = keep.tile([P, T], U8, align_bytes=64)
 
-        def rows(base, n, steps=1, pitch=None):
-            width = n + 2 * GAP
-            if pitch is None:
-                pitch = width
-            block = work[:, base : base + steps * pitch].rearrange("p (s r) -> p s r", s=steps)
-            return block[:, :, :width].rearrange("p s (u c) -> p s u c", u=2)[:, :, :, : n // 2]
+        def runs(base, n, planes, pitch):
+            block = work[:, base : base + planes * pitch].rearrange("p (t r) -> p t r", t=planes)
+            return block[:, :, : span(n)].rearrange("p t (u c) -> p t u c", c=PITCH)[:, :, :, :RUN]
 
         def gather(t, d, c0, n, base):
+            window = T + SPARE if n == T else T
             nc.vector.tensor_copy(
-                rows(base, n)[:, 0, :, :],
-                h[:, t * T : (t + 1) * T].indirect(lists[d][:, c0 // 16 : (c0 + n) // 16]),
+                runs(base, n, 1, span(n))[:, 0, :, :],
+                h[:, t * T : t * T + window].indirect(lists[d][:, c0 // 16 : (c0 + n) // 16]),
             )
 
-        def largest(z_base, n, t0, steps, base_a, base_b, pitch):
-            dst = work[:, z_base + t0 * n : z_base + (t0 + steps) * n]
+        def largest(c0, n, t0, planes, base_a, base_b, pitch):
+            start = HB + PACK * c0 + t0 * n
             nc.vector.tensor_tensor(
-                dst.rearrange("p (s u c) -> p s u c", s=steps, u=2),
-                rows(base_a, n, steps, pitch),
-                rows(base_b, n, steps, pitch),
+                work[:, start : start + planes * n].rearrange("p (t u c) -> p t u c", t=planes, c=RUN),
+                runs(base_a, n, planes, pitch),
+                runs(base_b, n, planes, pitch),
                 MAX,
             )
 
-        def weave(engine_copy, dst_base, src, n):
+        def largest_high(c0, n):
+            largest(c0, n, 2, 2, G_HIGH + span(c0), G_HIGH + span(T) + span(c0), 2 * span(T))
+
+        def weave(engine_copy, base, src, n):
             engine_copy(
-                out=work[:, dst_base : dst_base + PACK * n].rearrange("p (c i t) -> p c t i", i=RUN, t=PACK),
-                in_=src.rearrange("p t (c i) -> p c t i", i=RUN),
+                out=work[:, base : base + PACK * n].rearrange("p (c i t) -> p c t i", i=NEAR, t=PACK),
+                in_=src.rearrange("p t (c i) -> p c t i", i=NEAR),
             )
 
-        def z_planes(z_base, n):
-            return work[:, z_base : z_base + PACK * n].rearrange("p (t c) -> p t c", t=PACK)
+        def weave_z(engine_copy, c0, n):
+            src = work[:, HB + PACK * c0 : HB + PACK * (c0 + n)].rearrange("p (t c) -> p t c", t=PACK)
+            weave(engine_copy, ZB + PACK * c0, src, n)
 
-        def quantise(codes, plane, c0, n, base):
-            nc.vector.quantize_mx(
-                out=codes[:, c0 : c0 + n].bitcast(FP8X4),
-                scales=plane[:, c0 : c0 + n],
-                in_=work[:, base : base + PACK * n],
-            )
-
-        def quantise_halves(codes, plane, c0, n, base):
-            quantise(codes, plane, c0, n // 2, base)
-            quantise(codes, plane, c0 + n // 2, n // 2, base + PACK * n // 2)
+        def quantise(codes, plane, base, c0, n, widest):
+            for start, width in pieces(n, widest):
+                b0 = c0 + start
+                nc.vector.quantize_mx(
+                    out=codes[:, b0 : b0 + width].bitcast(FP8X4),
+                    scales=plane[:, b0 : b0 + width],
+                    in_=work[:, base + PACK * b0 : base + PACK * (b0 + width)],
+                )
 
         def finish(c0, n):
-            acc = psum_o.tile([P, BANK], F32, name="acc_o")
-            for s, (codes, plane) in enumerate(((h_codes, h_plane), (z_codes, z_plane))):
-                nc.tensor.matmul_mx(
-                    out=acc[:, :n],
-                    lhsT=w23_codes[:, s * N : (s + 1) * N].bitcast(FP8X4),
-                    lhsT_scale=w23_plane[:, s * N : (s + 1) * N],
-                    rhs=codes[:, c0 : c0 + n].bitcast(FP8X4),
-                    rhs_scale=plane[:, c0 : c0 + n],
-                    start=(s == 0),
-                    stop=(s == 1),
-                )
-            result = keep.tile([P, n], F32, name="result%d" % c0)
-            nc.scalar.copy(out=result[:], in_=acc[:, :n])
-            nc.sync.dma_start(out=out[:, c0 : c0 + n], in_=result[:])
+            for start, width in pieces(n, BANK):
+                cols = slice(c0 + start, c0 + start + width)
+                acc = psum_o.tile([P, BANK], F32, name="acc_o")
+                for s, (codes, plane) in enumerate(((h_codes, h_plane), (z_codes, z_plane))):
+                    nc.tensor.matmul_mx(
+                        out=acc[:, :width],
+                        lhsT=w23_codes[:, s * N : (s + 1) * N].bitcast(FP8X4),
+                        lhsT_scale=w23_plane[:, s * N : (s + 1) * N],
+                        rhs=codes[:, cols].bitcast(FP8X4),
+                        rhs_scale=plane[:, cols],
+                        start=(s == 0),
+                        stop=(s == 1),
+                    )
+                result = keep.tile([P, width], F32, name="result%d" % (c0 + start))
+                nc.scalar.copy(out=result[:], in_=acc[:, :width])
+                nc.sync.dma_start(out=out[:, cols], in_=result[:])
 
-        for u in range(2):
-            weave(nc.scalar.copy, HB + u * 2048, h_planes[:, :, u * 512 : (u + 1) * 512], 512)
+        h_planes = h[:, : PACK * T].rearrange("p (t c) -> p t c", t=PACK)
+        for c0, n in CHUNKS:
+            weave(nc.scalar.copy, HB + PACK * c0, h_planes[:, :, c0 : c0 + n], n)
 
-        half0 = STEP0 // 2
-        for t in range(PACK):
+        for t in (3, 2):
             for d in range(2):
-                gather(t, d, 0, 512, G0 + t * STEP0 + d * half0)
-        quantise_halves(h_codes, h_plane, 0, 512, HB)
-        for t0 in (0, 2):
-            largest(HB, 512, t0, 2, G0 + t0 * STEP0, G0 + t0 * STEP0 + half0, STEP0)
-        weave(nc.scalar.copy, ZB[0], z_planes(HB, 512), 512)
+                gather(t, d, 0, T, G_HIGH + (2 * (t - 2) + d) * span(T))
 
-        for t in range(PACK):
+        c0, n = CHUNKS[0]
+        for t in (1, 0):
             for d in range(2):
-                gather(t, d, 512, 256, G0 + t * STEP0 + d * half0)
-        quantise_halves(h_codes, h_plane, 512, 512, HB + 2048)
-        for t0 in (0, 2):
-            largest(HB + 2048, 256, t0, 2, G0 + t0 * STEP0, G0 + t0 * STEP0 + half0, STEP0)
-        weave(nc.scalar.copy, ZB[1], z_planes(HB + 2048, 256), 256)
-        quantise_halves(z_codes, z_plane, 0, 512, ZB[0])
-        finish(0, 512)
+                gather(t, d, c0, n, G_LOW + (2 * t + d) * span(n))
+        quantise(h_codes, h_plane, HB, c0, n, 256)
+        largest(c0, n, 0, 2, G_LOW, G_LOW + span(n), 2 * span(n))
+        largest_high(c0, n)
+        weave_z(nc.scalar.copy, c0, n)
 
-        one = 128 + 2 * GAP
-        step = 2 * one
-        for t in range(PACK):
+        c1, n1 = CHUNKS[1]
+        c2, n2 = CHUNKS[2]
+        for t in (1, 0):
             for d in range(2):
-                gather(t, d, 768, 128, ZB[0] + t * step + d * one)
-        quantise_halves(z_codes, z_plane, 512, 256, ZB[1])
-        for t0 in (0, 2):
-            largest(ZB[1], 128, t0, 2, ZB[0] + t0 * step, ZB[0] + t0 * step + one, step)
-        weave(nc.scalar.copy, ZB[2], z_planes(ZB[1], 128), 128)
-        finish(512, 256)
+                gather(t, d, c1, n1, G_LOW + (2 * t + d) * span(n1))
+        quantise(h_codes, h_plane, HB, c1, n1, 256)
+        quantise(h_codes, h_plane, HB, c2, n2, 256)
+        largest(c1, n1, 0, 2, G_LOW, G_LOW + span(n1), 2 * span(n1))
+        largest_high(c1, n1)
+        largest_high(c2, n2)
+        weave_z(nc.scalar.copy, c1, n1)
+        quantise(z_codes, z_plane, ZB, c0, n, 256)
+        finish(c0, n)
 
-        z3 = HB + 3072
-        for t in range(2):
-            for d in range(2):
-                gather(t, d, 896, 128, ZB[0] + t * step + d * one)
-        gather(2, 0, 896, 128, ZB[0] + 2 * step)
-        largest(z3, 128, 0, 2, ZB[0], ZB[0] + one, step)
-        quantise_halves(z_codes, z_plane, 768, 128, ZB[2])
-        finish(768, 128)
-        gather(2, 1, 896, 128, ZB[2])
-        gather(3, 0, 896, 128, ZB[2] + one)
-        largest(z3, 128, 2, 1, ZB[0] + 2 * step, ZB[2], None)
-        gather(3, 1, 896, 128, ZB[2] + 2 * one)
-        largest(z3, 128, 3, 1, ZB[2] + one, ZB[2] + 2 * one, None)
-        weave(nc.vector.tensor_copy, ZB[3], z_planes(z3, 128), 128)
-        quantise(z_codes, z_plane, 896, 128, ZB[3])
-        finish(896, 128)
+        one = span(n2)
+        gather(1, 0, c2, n2, ZB)
+        gather(1, 1, c2, n2, ZB + one)
+        gather(0, 0, c2, n2, ZB + 2 * one)
+        largest(c2, n2, 1, 1, ZB, ZB + one, one)
+        quantise(z_codes, z_plane, ZB, c1, n1, 128)
+        finish(c1, n1)
+        gather(0, 1, c2, n2, ZB + PACK * c1)
+        largest(c2, n2, 0, 1, ZB + 2 * one, ZB + PACK * c1, one)
+        weave_z(nc.vector.tensor_copy, c2, n2)
+        quantise(z_codes, z_plane, ZB, c2, n2, 128)
+        finish(c2, n2)

@@ -22,8 +22,8 @@ NEAR = 4
 QUARTER = T // 4
 RUN = 64
 PITCH = RUN + 8
-SPARE = 384
-CHUNKS = ((0, 640), (640, 256), (896, 128))
+SPARE = 256
+CHUNKS = ((0, 512), (512, 384), (896, 128))
 
 
 def pieces(n, widest):
@@ -140,11 +140,16 @@ def tile_picked_wsagecat_max_l_kernel(
         def span(n):
             return n // RUN * PITCH
 
+        (c0, n0), (c1, n1), (c2, n2) = CHUNKS
         HB = 0
-        ZB = HB + PACK * T
-        G_HIGH = ZB + PACK * T
-        G_LOW = G_HIGH + 4 * span(T)
-        WIDTH = G_LOW + 4 * span(640) + span(T)
+        Z1 = HB + PACK * T
+        Z0 = Z1 + PACK * n1
+        Z2 = Z0 + PACK * n0
+        G_HIGH = Z2 + PACK * n2
+        G_LOW = G_HIGH + 6 * span(c2)
+        WIDTH = G_LOW + 3 * span(c2)
+        LAST_B = Z0 - span(n2)
+        LAST_A = LAST_B + PACK * span(n2)
         work = keep.tile([P, WIDTH], BF16, align_bytes=64)
         h_codes = keep.tile([P, T], U32, align_bytes=64)
         h_plane = keep.tile([P, T], U8, align_bytes=64)
@@ -155,51 +160,42 @@ def tile_picked_wsagecat_max_l_kernel(
             block = work[:, base : base + planes * pitch].rearrange("p (t r) -> p t r", t=planes)
             return block[:, :, : span(n)].rearrange("p t (u c) -> p t u c", c=PITCH)[:, :, :, :RUN]
 
-        def gather(t, d, c0, n, base):
-            window = T + SPARE if n == T else T
+        def gather(t, d, first, n, base):
+            window = T + SPARE if 4 * n > 3 * T else T
             nc.vector.tensor_copy(
                 runs(base, n, 1, span(n))[:, 0, :, :],
-                h[:, t * T : t * T + window].indirect(lists[d][:, c0 // 16 : (c0 + n) // 16]),
+                h[:, t * T : t * T + window].indirect(lists[d][:, first // 16 : (first + n) // 16]),
             )
 
-        def largest(c0, n, t0, planes, base_a, base_b, pitch):
-            start = HB + PACK * c0 + t0 * n
+        def largest(first, n, t0, planes, base, list_pitch):
+            start = HB + PACK * first + t0 * n
             nc.vector.tensor_tensor(
                 work[:, start : start + planes * n].rearrange("p (t u c) -> p t u c", t=planes, c=RUN),
-                runs(base_a, n, planes, pitch),
-                runs(base_b, n, planes, pitch),
+                runs(base, n, planes, 2 * list_pitch),
+                runs(base + list_pitch, n, planes, 2 * list_pitch),
                 MAX,
             )
 
-        def largest_high(c0, n):
-            largest(c0, n, 2, 2, G_HIGH + span(c0), G_HIGH + span(T) + span(c0), 2 * span(T))
+        def woven(base, n):
+            return work[:, base : base + PACK * n].rearrange("p (c i t) -> p c t i", i=NEAR, t=PACK)
 
-        def weave(engine_copy, base, src, n):
-            engine_copy(
-                out=work[:, base : base + PACK * n].rearrange("p (c i t) -> p c t i", i=NEAR, t=PACK),
-                in_=src.rearrange("p t (c i) -> p c t i", i=NEAR),
+        def near(planes):
+            return planes.rearrange("p t (c i) -> p c t i", i=NEAR)
+
+        def quantise(codes, plane, first, n, base):
+            nc.vector.quantize_mx(
+                out=codes[:, first : first + n].bitcast(FP8X4),
+                scales=plane[:, first : first + n],
+                in_=work[:, base : base + PACK * n],
             )
 
-        def weave_z(engine_copy, c0, n):
-            src = work[:, HB + PACK * c0 : HB + PACK * (c0 + n)].rearrange("p (t c) -> p t c", t=PACK)
-            weave(engine_copy, ZB + PACK * c0, src, n)
-
-        def quantise(codes, plane, base, c0, n, widest):
-            for start, width in pieces(n, widest):
-                b0 = c0 + start
-                nc.vector.quantize_mx(
-                    out=codes[:, b0 : b0 + width].bitcast(FP8X4),
-                    scales=plane[:, b0 : b0 + width],
-                    in_=work[:, base + PACK * b0 : base + PACK * (b0 + width)],
-                )
-
-        def finish(c0, n):
+        def finish(first, n):
+            acc = psum_o.tile([P, BANK], F32, name="acc_o")
             for start, width in pieces(n, BANK):
-                cols = slice(c0 + start, c0 + start + width)
-                acc = psum_o.tile([P, BANK], F32, name="acc_o")
+                cols = slice(first + start, first + start + width)
                 for s, (codes, plane) in enumerate(((h_codes, h_plane), (z_codes, z_plane))):
                     nc.tensor.matmul_mx(
-                        out=acc[:, :width],
+                        out=acc[:, start : start + width],
                         lhsT=w23_codes[:, s * N : (s + 1) * N].bitcast(FP8X4),
                         lhsT_scale=w23_plane[:, s * N : (s + 1) * N],
                         rhs=codes[:, cols].bitcast(FP8X4),
@@ -207,50 +203,57 @@ def tile_picked_wsagecat_max_l_kernel(
                         start=(s == 0),
                         stop=(s == 1),
                     )
-                result = keep.tile([P, width], F32, name="result%d" % (c0 + start))
-                nc.scalar.copy(out=result[:], in_=acc[:, :width])
-                nc.sync.dma_start(out=out[:, cols], in_=result[:])
+            result = keep.tile([P, n], F32, name="result%d" % first)
+            nc.scalar.copy(out=result[:], in_=acc[:, :n])
+            nc.sync.dma_start(out=out[:, first : first + n], in_=result[:])
+
+        def low_planes(first, n):
+            for d in range(2):
+                gather(0, d, first, n, G_LOW + d * span(n))
+
+        def make_z(first, n, base):
+            largest(first, n, 0, 1, G_LOW, span(n))
+            largest(first, n, 1, 3, G_HIGH + span(first), span(c2))
+            z_planes = work[:, HB + PACK * first : HB + PACK * (first + n)].rearrange("p (t c) -> p t c", t=PACK)
+            nc.scalar.copy(out=woven(base, n), in_=near(z_planes))
 
         h_planes = h[:, : PACK * T].rearrange("p (t c) -> p t c", t=PACK)
-        for c0, n in CHUNKS:
-            weave(nc.scalar.copy, HB + PACK * c0, h_planes[:, :, c0 : c0 + n], n)
+        for first, n in CHUNKS:
+            nc.scalar.copy(out=woven(HB + PACK * first, n), in_=near(h_planes[:, :, first : first + n]))
 
-        for t in (3, 2):
+        for t in (3, 2, 1):
             for d in range(2):
-                gather(t, d, 0, T, G_HIGH + (2 * (t - 2) + d) * span(T))
+                gather(t, d, 0, c2, G_HIGH + (2 * (t - 1) + d) * span(c2))
 
-        c0, n = CHUNKS[0]
-        for t in (1, 0):
-            for d in range(2):
-                gather(t, d, c0, n, G_LOW + (2 * t + d) * span(n))
-        quantise(h_codes, h_plane, HB, c0, n, 256)
-        largest(c0, n, 0, 2, G_LOW, G_LOW + span(n), 2 * span(n))
-        largest_high(c0, n)
-        weave_z(nc.scalar.copy, c0, n)
+        low_planes(c0, n0)
+        for first in (0, 256):
+            quantise(h_codes, h_plane, first, 256, HB + PACK * first)
+        make_z(c0, n0, Z0)
 
-        c1, n1 = CHUNKS[1]
-        c2, n2 = CHUNKS[2]
-        for t in (1, 0):
-            for d in range(2):
-                gather(t, d, c1, n1, G_LOW + (2 * t + d) * span(n1))
-        quantise(h_codes, h_plane, HB, c1, n1, 256)
-        quantise(h_codes, h_plane, HB, c2, n2, 256)
-        largest(c1, n1, 0, 2, G_LOW, G_LOW + span(n1), 2 * span(n1))
-        largest_high(c1, n1)
-        largest_high(c2, n2)
-        weave_z(nc.scalar.copy, c1, n1)
-        quantise(z_codes, z_plane, ZB, c0, n, 256)
-        finish(c0, n)
+        low_planes(c1, n1)
+        for first, n in ((512, 256), (768, 128), (896, 128)):
+            quantise(h_codes, h_plane, first, n, HB + PACK * first)
+        make_z(c1, n1, Z1)
+        for first in (0, 256):
+            quantise(z_codes, z_plane, first, 256, Z0 + PACK * first)
+        finish(c0, n0)
 
         one = span(n2)
-        gather(1, 0, c2, n2, ZB)
-        gather(1, 1, c2, n2, ZB + one)
-        gather(0, 0, c2, n2, ZB + 2 * one)
-        largest(c2, n2, 1, 1, ZB, ZB + one, one)
-        quantise(z_codes, z_plane, ZB, c1, n1, 128)
+        for t in (3, 2, 1, 0):
+            gather(t, 0, c2, n2, LAST_A + t * one)
+            if t > 0:
+                gather(t, 1, c2, n2, LAST_B + t * one)
+        quantise(z_codes, z_plane, c1 + 256, 128, Z1 + PACK * 256)
+        quantise(z_codes, z_plane, c1, 256, Z1)
         finish(c1, n1)
-        gather(0, 1, c2, n2, ZB + PACK * c1)
-        largest(c2, n2, 0, 1, ZB + 2 * one, ZB + PACK * c1, one)
-        weave_z(nc.vector.tensor_copy, c2, n2)
-        quantise(z_codes, z_plane, ZB, c2, n2, 128)
+        gather(0, 1, c2, n2, LAST_B)
+        for u in range(2):
+            nc.vector.tensor_tensor(
+                woven(Z2 + u * PACK * RUN, RUN),
+                near(runs(LAST_A, n2, PACK, one)[:, :, u, :]),
+                near(runs(LAST_B, n2, PACK, one)[:, :, u, :]),
+                MAX,
+            )
+        for u in range(2):
+            quantise(z_codes, z_plane, c2 + u * RUN, RUN, Z2 + u * PACK * RUN)
         finish(c2, n2)

@@ -13,29 +13,37 @@ U16 = mybir.dt.uint16
 U8 = mybir.dt.uint8
 FP8X4 = mybir.dt.float8_e4m3fn_x4
 MAX = mybir.AluOpType.max
+ADD = mybir.AluOpType.add
+SUB = mybir.AluOpType.subtract
 RELU = mybir.ActivationFunctionType.Relu
 
 P = 128
 PACK = 4
 BANK = 512
-NEAR = 4
 QUARTER = T // 4
-RUN = 64
-PITCH = RUN + 8
+NEAR = 4
+RUN = 128
+LAST_RUN = 64
+GAP = 8
 SPARE = 256
+
 CHUNKS = ((0, 512), (512, 384), (896, 128))
 
 
-def pieces(n, widest):
+def powers_of_two(n):
     cut = []
     start = 0
     while start < n:
-        width = widest
+        width = BANK
         while width > n - start:
             width = width // 2
         cut.append((start, width))
         start = start + width
     return cut
+
+
+def span(n, run):
+    return n // run * (run + GAP)
 
 
 def tile_picked_wsagecat_max_l_kernel(
@@ -50,210 +58,240 @@ def tile_picked_wsagecat_max_l_kernel(
 
         lists = [keep.tile([P, T // 16], U16, name="list%d" % d) for d in range(2)]
         x_codes = keep.tile([P, T], U32, align_bytes=64)
-        x_plane = keep.tile([P, QUARTER], U8, align_bytes=64)
+        x_scale = keep.tile([P, QUARTER], U8, align_bytes=64)
         h = keep.tile([P, PACK * T + SPARE], F32, align_bytes=64)
 
-        nc.vector.memset(x_plane[:].bitcast(I32), 0)
+        nc.vector.memset(x_scale[:].bitcast(I32), 0)
         nc.vector.memset(h[:, PACK * T :], 0.0)
+
         w1_rows = w1.rearrange("(p j) c -> p j c", j=PACK)
         half = H // 2
         w1_raw = []
         for u in range(2):
-            w_half = raw.tile([P, PACK, half], F32, name="w_half", tag="raw")
-            nc.sync.dma_start(out=w_half[:], in_=w1_rows[:, :, u * half : (u + 1) * half])
-            w1_raw.append(w_half)
+            w1_half = raw.tile([P, PACK, half], F32, name="w1_half", tag="raw")
+            nc.sync.dma_start(out=w1_half[:], in_=w1_rows[:, :, u * half : (u + 1) * half])
+            w1_raw.append(w1_half)
             if u == 0:
                 for q in range(4):
                     nc.sync.dma_start(
-                        out=x_plane[32 * q : 32 * q + 16, :].bitcast(I32),
+                        out=x_scale[32 * q : 32 * q + 16, :].bitcast(I32),
                         in_=x_scales[0, 4 * q : 4 * q + 4, :].bitcast(I32).rearrange("r (a c) -> a r c", a=4),
                     )
         x_rows = x_words[0].rearrange("p n t -> p (n t)").bitcast(I32)
         for u in range(2):
-            cols = slice(u * T // 2, (u + 1) * T // 2)
-            nc.sync.dma_start(out=x_codes[:, cols].bitcast(I32), in_=x_rows[:, cols])
+            nodes = slice(u * T // 2, (u + 1) * T // 2)
+            nc.sync.dma_start(out=x_codes[:, nodes].bitcast(I32), in_=x_rows[:, nodes])
         nc.sync.dma_start(lists[0][:], pos1)
         nc.sync.dma_start(lists[1][:], pos2)
 
-        w1_bf = keep.tile([P, PACK, P, PACK], BF16, align_bytes=64)
+        w1_woven = keep.tile([P, PACK, P, PACK], BF16, align_bytes=64)
         w1_codes = keep.tile([P, PACK, P], U32, align_bytes=64)
-        w1_plane = keep.tile([P, PACK, P], U8, align_bytes=64)
-        mh = P // 2
+        w1_scale = keep.tile([P, PACK, P], U8, align_bytes=64)
+        m_half = P // 2
         for u in range(2):
             for t0 in (2, 0):
                 nc.vector.tensor_copy(
-                    out=w1_bf[:, t0 : t0 + 2, u * mh : (u + 1) * mh, :].rearrange("p t m j -> p m j t"),
+                    out=w1_woven[:, t0 : t0 + 2, u * m_half : (u + 1) * m_half, :].rearrange("p t m j -> p m j t"),
                     in_=w1_raw[u][:].rearrange("p j (m t) -> p m j t", t=PACK)[:, :, :, t0 : t0 + 2],
                 )
         for t in (3, 2, 1, 0):
             nc.vector.quantize_mx(
                 out=w1_codes[:, t, :].bitcast(FP8X4),
-                scales=w1_plane[:, t, :],
-                in_=w1_bf[:, t, :, :].rearrange("p m j -> p (m j)"),
+                scales=w1_scale[:, t, :],
+                in_=w1_woven[:, t, :, :].rearrange("p m j -> p (m j)"),
             )
 
-        def h_piece(t, c0, c1, on_vector):
-            acc = psum_h.tile([P, BANK], F32, name="acc_h")
-            for b0 in range(c0, c1, QUARTER):
-                b1 = min(b0 + QUARTER, c1)
-                a, r = divmod(b0, QUARTER)
+        def h_piece(t, start, stop, on_vector):
+            acc_h = psum_h.tile([P, BANK], F32, name="acc_h")
+            for b0 in range(start, stop, QUARTER):
+                b1 = min(b0 + QUARTER, stop)
+                a, within = divmod(b0, QUARTER)
                 nc.tensor.matmul_mx(
-                    out=acc[:, b0 - c0 : b1 - c0],
+                    out=acc_h[:, b0 - start : b1 - start],
                     lhsT=w1_codes[:, t, :].bitcast(FP8X4),
-                    lhsT_scale=w1_plane[:, t, :],
+                    lhsT_scale=w1_scale[:, t, :],
                     rhs=x_codes[:, b0:b1].bitcast(FP8X4),
-                    rhs_scale=x_plane[4 * a :, r : r + b1 - b0],
+                    rhs_scale=x_scale[4 * a :, within : within + b1 - b0],
                     start=True,
                     stop=True,
                 )
-            dst = h[:, t * T + c0 : t * T + c1]
+            dst = h[:, t * T + start : t * T + stop]
             if on_vector:
-                nc.vector.tensor_scalar_max(dst, acc[:, : c1 - c0], 0.0)
+                nc.vector.tensor_scalar_max(dst, acc_h[:, : stop - start], 0.0)
             else:
-                nc.scalar.activation(dst, acc[:, : c1 - c0], RELU)
+                nc.scalar.activation(dst, acc_h[:, : stop - start], RELU)
 
-        h_piece(3, 0, 256, False)
-        h_piece(3, 256, 512, True)
-        h_piece(3, 512, 768, False)
-        h_piece(3, 768, 896, True)
-        h_piece(3, 896, 1024, False)
+        edges = (0, QUARTER, 2 * QUARTER, 3 * QUARTER, 3 * QUARTER + QUARTER // 2, T)
+        for piece in range(len(edges) - 1):
+            h_piece(3, edges[piece], edges[piece + 1], piece % 2 == 1)
         for t in (2, 1, 0):
-            h_piece(t, 0, 512, False)
-            h_piece(t, 512, 1024, False)
+            h_piece(t, 0, BANK, False)
+            h_piece(t, BANK, T, False)
 
-        w23_bf = keep.tile([P, 2, N, PACK], BF16, align_bytes=64)
+        def near(rows):
+            return rows.rearrange("p t (c i) -> p c t i", i=NEAR)
+
+        w23_woven = keep.tile([P, 2, N, PACK], BF16, align_bytes=64)
         w23_codes = keep.tile([P, 2 * N], U32, align_bytes=64)
-        w23_plane = keep.tile([P, 2 * N], U8, align_bytes=64)
+        w23_scale = keep.tile([P, 2 * N], U8, align_bytes=64)
         for s, w in enumerate((w2, w3)):
             w_out = raw.tile([P, PACK, N], F32, name="w_out", tag="raw")
             nc.sync.dma_start(out=w_out[:], in_=w.rearrange("(p j) n -> p j n", j=PACK))
             nc.scalar.copy(
-                out=w23_bf[:, s, :, :].rearrange("p (c i) j -> p c j i", i=NEAR),
-                in_=w_out[:].rearrange("p j (c i) -> p c j i", i=NEAR),
+                out=w23_woven[:, s, :, :].rearrange("p (c i) j -> p c j i", i=NEAR), in_=near(w_out[:])
             )
         nc.vector.quantize_mx(
             out=w23_codes[:].bitcast(FP8X4),
-            scales=w23_plane[:],
-            in_=w23_bf[:].rearrange("p s n j -> p (s n j)"),
+            scales=w23_scale[:],
+            in_=w23_woven[:].rearrange("p s n j -> p (s n j)"),
         )
 
-        def span(n):
-            return n // RUN * PITCH
-
         (c0, n0), (c1, n1), (c2, n2) = CHUNKS
-        HB = 0
-        Z1 = HB + PACK * T
-        Z0 = Z1 + PACK * n1
-        Z2 = Z0 + PACK * n0
-        G_HIGH = Z2 + PACK * n2
-        G_LOW = G_HIGH + 6 * span(c2)
-        WIDTH = G_LOW + 3 * span(c2)
-        LAST_B = Z0 - span(n2)
-        LAST_A = LAST_B + PACK * span(n2)
-        work = keep.tile([P, WIDTH], BF16, align_bytes=64)
+        last_span = span(n2, LAST_RUN)
+        long_span = span(c2, RUN)
+        h_woven0 = 0
+        z_planes0 = h_woven0 + n0
+        h_woven1 = z_planes0 + PACK * n0
+        z_planes1 = h_woven1 + n1
+        h_woven2 = z_planes1 + PACK * n1
+        z_woven1 = h_woven2 + PACK * n2
+        z_woven0 = z_woven1 + PACK * n1
+        z_woven2 = z_woven0 + PACK * n0
+        picked_long = z_woven2 + PACK * n2
+        picked_plane0 = picked_long + 2 * (PACK - 1) * long_span
+        last_b = z_woven0 - last_span
+        last_a = last_b + PACK * last_span
+        work = keep.tile([P, picked_plane0 + 2 * long_span], BF16, align_bytes=64)
         h_codes = keep.tile([P, T], U32, align_bytes=64)
-        h_plane = keep.tile([P, T], U8, align_bytes=64)
+        h_scale = keep.tile([P, T], U8, align_bytes=64)
         z_codes = keep.tile([P, T], U32, align_bytes=64)
-        z_plane = keep.tile([P, T], U8, align_bytes=64)
+        z_scale = keep.tile([P, T], U8, align_bytes=64)
 
-        def runs(base, n, planes, pitch):
+        def runs(base, n, run, planes, pitch):
             block = work[:, base : base + planes * pitch].rearrange("p (t r) -> p t r", t=planes)
-            return block[:, :, : span(n)].rearrange("p t (u c) -> p t u c", c=PITCH)[:, :, :, :RUN]
+            return block[:, :, : span(n, run)].rearrange("p t (u c) -> p t u c", c=run + GAP)[:, :, :, :run]
 
-        def gather(t, d, first, n, base):
-            window = T + SPARE if 4 * n > 3 * T else T
+        def one_plane(base, n, run):
+            return runs(base, n, run, 1, span(n, run))[:, 0, :, :]
+
+        def gather(t, d, first, n, run, base):
+            window = T + SPARE if n == c2 else T
             nc.vector.tensor_copy(
-                runs(base, n, 1, span(n))[:, 0, :, :],
+                one_plane(base, n, run),
                 h[:, t * T : t * T + window].indirect(lists[d][:, first // 16 : (first + n) // 16]),
             )
 
-        def largest(first, n, t0, planes, base, list_pitch):
-            start = HB + PACK * first + t0 * n
-            nc.vector.tensor_tensor(
-                work[:, start : start + planes * n].rearrange("p (t u c) -> p t u c", t=planes, c=RUN),
-                runs(base, n, planes, 2 * list_pitch),
-                runs(base + list_pitch, n, planes, 2 * list_pitch),
-                MAX,
-            )
+        def long_base(t, d, first):
+            return picked_long + (2 * (t - 1) + d) * long_span + span(first, RUN)
+
+        def z_rows(z_planes, n, t0, planes):
+            rows = work[:, z_planes + t0 * n : z_planes + (t0 + planes) * n]
+            return rows.rearrange("p (t u c) -> p t u c", t=planes, c=RUN)
 
         def woven(base, n):
             return work[:, base : base + PACK * n].rearrange("p (c i t) -> p c t i", i=NEAR, t=PACK)
 
-        def near(planes):
-            return planes.rearrange("p t (c i) -> p c t i", i=NEAR)
+        def weave_h(first, n, base):
+            h_planes = h[:, : PACK * T].rearrange("p (t c) -> p t c", t=PACK)
+            nc.scalar.copy(out=woven(base, n), in_=near(h_planes[:, :, first : first + n]))
 
-        def quantise(codes, plane, first, n, base):
+        def gather_plane0(first, n):
+            for d in range(2):
+                gather(0, d, first, n, RUN, picked_plane0 + d * span(n, RUN))
+
+        def finish_z(first, n, z_planes, z_woven):
+            for t0, planes, base, list_pitch in (
+                (0, 1, picked_plane0, span(n, RUN)),
+                (1, 2, long_base(1, 0, first), long_span),
+            ):
+                nc.vector.tensor_tensor(
+                    z_rows(z_planes, n, t0, planes),
+                    runs(base, n, RUN, planes, planes * list_pitch),
+                    runs(base + list_pitch, n, RUN, planes, planes * list_pitch),
+                    MAX,
+                )
+            planes_of_z = work[:, z_planes : z_planes + PACK * n].rearrange("p (t c) -> p t c", t=PACK)
+            nc.scalar.copy(out=woven(z_woven, n), in_=near(planes_of_z))
+
+        def quantise(codes, scale, first, n, base):
             nc.vector.quantize_mx(
                 out=codes[:, first : first + n].bitcast(FP8X4),
-                scales=plane[:, first : first + n],
+                scales=scale[:, first : first + n],
                 in_=work[:, base : base + PACK * n],
             )
 
-        def finish(first, n):
-            acc = psum_o.tile([P, BANK], F32, name="acc_o")
-            for start, width in pieces(n, BANK):
+        def finish_out(first, n):
+            acc_o = psum_o.tile([P, BANK], F32, name="acc_o")
+            for start, width in powers_of_two(n):
                 cols = slice(first + start, first + start + width)
-                for s, (codes, plane) in enumerate(((h_codes, h_plane), (z_codes, z_plane))):
+                for s, (codes, scale) in enumerate(((h_codes, h_scale), (z_codes, z_scale))):
                     nc.tensor.matmul_mx(
-                        out=acc[:, start : start + width],
+                        out=acc_o[:, start : start + width],
                         lhsT=w23_codes[:, s * N : (s + 1) * N].bitcast(FP8X4),
-                        lhsT_scale=w23_plane[:, s * N : (s + 1) * N],
+                        lhsT_scale=w23_scale[:, s * N : (s + 1) * N],
                         rhs=codes[:, cols].bitcast(FP8X4),
-                        rhs_scale=plane[:, cols],
+                        rhs_scale=scale[:, cols],
                         start=(s == 0),
                         stop=(s == 1),
                     )
             result = keep.tile([P, n], F32, name="result%d" % first)
-            nc.scalar.copy(out=result[:], in_=acc[:, :n])
+            nc.scalar.copy(out=result[:], in_=acc_o[:, :n])
             nc.sync.dma_start(out=out[:, first : first + n], in_=result[:])
 
-        def low_planes(first, n):
-            for d in range(2):
-                gather(0, d, first, n, G_LOW + d * span(n))
-
-        def make_z(first, n, base):
-            largest(first, n, 0, 1, G_LOW, span(n))
-            largest(first, n, 1, 3, G_HIGH + span(first), span(c2))
-            z_planes = work[:, HB + PACK * first : HB + PACK * (first + n)].rearrange("p (t c) -> p t c", t=PACK)
-            nc.scalar.copy(out=woven(base, n), in_=near(z_planes))
-
-        h_planes = h[:, : PACK * T].rearrange("p (t c) -> p t c", t=PACK)
-        for first, n in CHUNKS:
-            nc.scalar.copy(out=woven(HB + PACK * first, n), in_=near(h_planes[:, :, first : first + n]))
+        weave_h(c0, n0, h_woven0)
 
         for t in (3, 2, 1):
             for d in range(2):
-                gather(t, d, 0, c2, G_HIGH + (2 * (t - 1) + d) * span(c2))
+                gather(t, d, 0, c2, RUN, long_base(t, d, 0))
 
-        low_planes(c0, n0)
-        for first in (0, 256):
-            quantise(h_codes, h_plane, first, 256, HB + PACK * first)
-        make_z(c0, n0, Z0)
+        diff = keep.tile([P, c2], F32)
+        nc.gpsimd.tensor_tensor(
+            diff[:].rearrange("p (u c) -> p u c", c=RUN),
+            one_plane(long_base(3, 0, 0), c2, RUN),
+            one_plane(long_base(3, 1, 0), c2, RUN),
+            SUB,
+        )
+        excess = raw.tile([P, c2], F32, name="excess", tag="raw")
+        nc.scalar.activation(excess[:], diff[:], RELU)
+        for first, n, z_planes in ((c0, n0, z_planes0), (c1, n1, z_planes1)):
+            nc.gpsimd.tensor_tensor(
+                z_rows(z_planes, n, 3, 1)[:, 0, :, :],
+                excess[:, first : first + n].rearrange("p (u c) -> p u c", c=RUN),
+                one_plane(long_base(3, 1, first), n, RUN),
+                ADD,
+            )
+        weave_h(c1, n1, h_woven1)
+        weave_h(c2, n2, h_woven2)
 
-        low_planes(c1, n1)
-        for first, n in ((512, 256), (768, 128), (896, 128)):
-            quantise(h_codes, h_plane, first, n, HB + PACK * first)
-        make_z(c1, n1, Z1)
-        for first in (0, 256):
-            quantise(z_codes, z_plane, first, 256, Z0 + PACK * first)
-        finish(c0, n0)
+        gather_plane0(c0, n0)
+        for first in (c0, c0 + QUARTER):
+            quantise(h_codes, h_scale, first, QUARTER, h_woven0 + PACK * first)
+        finish_z(c0, n0, z_planes0, z_woven0)
 
-        one = span(n2)
+        gather_plane0(c1, n1)
+        for start, width in powers_of_two(n1):
+            quantise(h_codes, h_scale, c1 + start, width, h_woven1 + PACK * start)
+        quantise(h_codes, h_scale, c2, n2, h_woven2)
+        finish_z(c1, n1, z_planes1, z_woven1)
+        for first in (c0, c0 + QUARTER):
+            quantise(z_codes, z_scale, first, QUARTER, z_woven0 + PACK * first)
+        finish_out(c0, n0)
+
         for t in (3, 2, 1, 0):
-            gather(t, 0, c2, n2, LAST_A + t * one)
+            gather(t, 0, c2, n2, LAST_RUN, last_a + t * last_span)
             if t > 0:
-                gather(t, 1, c2, n2, LAST_B + t * one)
-        quantise(z_codes, z_plane, c1 + 256, 128, Z1 + PACK * 256)
-        quantise(z_codes, z_plane, c1, 256, Z1)
-        finish(c1, n1)
-        gather(0, 1, c2, n2, LAST_B)
-        for u in range(2):
+                gather(t, 1, c2, n2, LAST_RUN, last_b + t * last_span)
+        for start, width in reversed(powers_of_two(n1)):
+            quantise(z_codes, z_scale, c1 + start, width, z_woven1 + PACK * start)
+        finish_out(c1, n1)
+        gather(0, 1, c2, n2, LAST_RUN, last_b)
+        for u in range(n2 // LAST_RUN):
             nc.vector.tensor_tensor(
-                woven(Z2 + u * PACK * RUN, RUN),
-                near(runs(LAST_A, n2, PACK, one)[:, :, u, :]),
-                near(runs(LAST_B, n2, PACK, one)[:, :, u, :]),
+                woven(z_woven2 + u * PACK * LAST_RUN, LAST_RUN),
+                near(runs(last_a, n2, LAST_RUN, PACK, last_span)[:, :, u, :]),
+                near(runs(last_b, n2, LAST_RUN, PACK, last_span)[:, :, u, :]),
                 MAX,
             )
-        for u in range(2):
-            quantise(z_codes, z_plane, c2 + u * RUN, RUN, Z2 + u * PACK * RUN)
-        finish(c2, n2)
+        for u in range(n2 // LAST_RUN):
+            quantise(z_codes, z_scale, c2 + u * LAST_RUN, LAST_RUN, z_woven2 + u * PACK * LAST_RUN)
+        finish_out(c2, n2)

@@ -22,19 +22,20 @@ PACK = 4
 BANK = 512
 QUARTER = T // 4
 NEAR = 4
-RUN = 128
-LAST_RUN = 64
+RUN = 64
 GAP = 8
-SPARE = 256
+SPARE = 352
+PIECE = 128
 
 CHUNKS = ((0, 512), (512, 384), (896, 128))
+GROUPS = ((0, 512), (512, 256), (768, 128), (896, 128))
 
 
-def powers_of_two(n):
+def powers_of_two(n, widest):
     cut = []
     start = 0
     while start < n:
-        width = BANK
+        width = widest
         while width > n - start:
             width = width // 2
         cut.append((start, width))
@@ -42,8 +43,8 @@ def powers_of_two(n):
     return cut
 
 
-def span(n, run):
-    return n // run * (run + GAP)
+def span(n):
+    return n // RUN * (RUN + GAP)
 
 
 def tile_picked_wsagecat_max_l_kernel(
@@ -53,8 +54,7 @@ def tile_picked_wsagecat_max_l_kernel(
     with ExitStack() as ctx:
         keep = ctx.enter_context(tc.tile_pool(name="keep", bufs=1))
         raw = ctx.enter_context(tc.tile_pool(name="raw", bufs=2))
-        psum_h = ctx.enter_context(tc.psum_pool(name="psum_h", bufs=5))
-        psum_o = ctx.enter_context(tc.psum_pool(name="psum_o", bufs=3))
+        psum = ctx.enter_context(tc.psum_pool(name="psum", bufs=8))
 
         lists = [keep.tile([P, T // 16], U16, name="list%d" % d) for d in range(2)]
         x_codes = keep.tile([P, T], U32, align_bytes=64)
@@ -89,20 +89,20 @@ def tile_picked_wsagecat_max_l_kernel(
         w1_scale = keep.tile([P, PACK, P], U8, align_bytes=64)
         m_half = P // 2
         for u in range(2):
-            for t0 in (2, 0):
-                nc.vector.tensor_copy(
+            for t0, cast in ((2, nc.vector.tensor_copy), (0, nc.scalar.copy)):
+                cast(
                     out=w1_woven[:, t0 : t0 + 2, u * m_half : (u + 1) * m_half, :].rearrange("p t m j -> p m j t"),
                     in_=w1_raw[u][:].rearrange("p j (m t) -> p m j t", t=PACK)[:, :, :, t0 : t0 + 2],
                 )
-        for t in (3, 2, 1, 0):
+        for t0, t1 in ((3, 4), (2, 3), (0, 2)):
             nc.vector.quantize_mx(
-                out=w1_codes[:, t, :].bitcast(FP8X4),
-                scales=w1_scale[:, t, :],
-                in_=w1_woven[:, t, :, :].rearrange("p m j -> p (m j)"),
+                out=w1_codes[:, t0:t1, :].rearrange("p t m -> p (t m)").bitcast(FP8X4),
+                scales=w1_scale[:, t0:t1, :].rearrange("p t m -> p (t m)"),
+                in_=w1_woven[:, t0:t1, :, :].rearrange("p t m j -> p (t m j)"),
             )
 
         def h_piece(t, start, stop, on_vector):
-            acc_h = psum_h.tile([P, BANK], F32, name="acc_h")
+            acc_h = psum.tile([P, BANK], F32, name="acc_h", tag="acc")
             for b0 in range(start, stop, QUARTER):
                 b1 = min(b0 + QUARTER, stop)
                 a, within = divmod(b0, QUARTER)
@@ -121,97 +121,59 @@ def tile_picked_wsagecat_max_l_kernel(
             else:
                 nc.scalar.activation(dst, acc_h[:, : stop - start], RELU)
 
-        edges = (0, QUARTER, 2 * QUARTER, 3 * QUARTER, 3 * QUARTER + QUARTER // 2, T)
-        for piece in range(len(edges) - 1):
-            h_piece(3, edges[piece], edges[piece + 1], piece % 2 == 1)
-        for t in (2, 1, 0):
-            h_piece(t, 0, BANK, False)
-            h_piece(t, BANK, T, False)
-
-        def near(rows):
-            return rows.rearrange("p t (c i) -> p c t i", i=NEAR)
-
-        w23_woven = keep.tile([P, 2, N, PACK], BF16, align_bytes=64)
-        w23_codes = keep.tile([P, 2 * N], U32, align_bytes=64)
-        w23_scale = keep.tile([P, 2 * N], U8, align_bytes=64)
-        for s, w in enumerate((w2, w3)):
-            w_out = raw.tile([P, PACK, N], F32, name="w_out", tag="raw")
-            nc.sync.dma_start(out=w_out[:], in_=w.rearrange("(p j) n -> p j n", j=PACK))
-            nc.scalar.copy(
-                out=w23_woven[:, s, :, :].rearrange("p (c i) j -> p c j i", i=NEAR), in_=near(w_out[:])
-            )
-        nc.vector.quantize_mx(
-            out=w23_codes[:].bitcast(FP8X4),
-            scales=w23_scale[:],
-            in_=w23_woven[:].rearrange("p s n j -> p (s n j)"),
-        )
-
         (c0, n0), (c1, n1), (c2, n2) = CHUNKS
-        last_span = span(n2, LAST_RUN)
-        long_span = span(c2, RUN)
-        h_woven0 = 0
-        z_planes0 = h_woven0 + n0
-        h_woven1 = z_planes0 + PACK * n0
-        z_planes1 = h_woven1 + n1
-        h_woven2 = z_planes1 + PACK * n1
-        z_woven1 = h_woven2 + PACK * n2
-        z_woven0 = z_woven1 + PACK * n1
-        z_woven2 = z_woven0 + PACK * n0
-        picked_long = z_woven2 + PACK * n2
-        picked_plane0 = picked_long + 2 * (PACK - 1) * long_span
-        last_b = z_woven0 - last_span
-        last_a = last_b + PACK * last_span
-        work = keep.tile([P, picked_plane0 + 2 * long_span], BF16, align_bytes=64)
+        whole = span(T)
+        woven_piece = PACK * PIECE
+        z_planes0 = 0
+        h_woven0 = z_planes0 + 2 * n0 - 2 * woven_piece
+        z_planes1 = z_planes0 + PACK * n0 + 2 * woven_piece - 2 * n1
+        h_woven2 = z_planes1 + 2 * n1 - 2 * woven_piece
+        h_woven3 = z_planes1 + PACK * n1
+        z_woven1 = h_woven3 + 2 * woven_piece
+        z_woven2 = z_woven1
+        picked0_c0 = z_woven1 + PACK * n1
+        picked0_c1 = picked0_c0 + 2 * span(n0)
+        h_woven1 = (picked0_c1 + 2 * span(n1) - woven_piece + 31) // 32 * 32
+        picked = h_woven1 + 2 * woven_piece
+        z_woven0 = picked + 128
+        work = keep.tile([P, picked + 2 * (PACK + 1) * whole], BF16, align_bytes=64)
         h_codes = keep.tile([P, T], U32, align_bytes=64)
         h_scale = keep.tile([P, T], U8, align_bytes=64)
         z_codes = keep.tile([P, T], U32, align_bytes=64)
         z_scale = keep.tile([P, T], U8, align_bytes=64)
+        w23_codes = keep.tile([P, 2 * N], U32, align_bytes=64)
+        w23_scale = keep.tile([P, 2 * N], U8, align_bytes=64)
 
-        def runs(base, n, run, planes, pitch):
+        def place(t, d, first):
+            if t == 0 and first == c0:
+                return picked0_c0 + d * span(n0)
+            if t == 0 and first == c1:
+                return picked0_c1 + d * span(n1)
+            return picked + (2 * t + d) * whole + span(first)
+
+        def runs(d, first, n, planes):
+            base = place(0, d, first)
+            pitch = place(1, d, first) - base
             block = work[:, base : base + planes * pitch].rearrange("p (t r) -> p t r", t=planes)
-            return block[:, :, : span(n, run)].rearrange("p t (u c) -> p t u c", c=run + GAP)[:, :, :, :run]
+            return block[:, :, : span(n)].rearrange("p t (u c) -> p t u c", c=RUN + GAP)[:, :, :, :RUN]
 
-        def one_plane(base, n, run):
-            return runs(base, n, run, 1, span(n, run))[:, 0, :, :]
+        def one_plane(t, d, first, n):
+            base = place(t, d, first)
+            return work[:, base : base + span(n)].rearrange("p (u c) -> p u c", c=RUN + GAP)[:, :, :RUN]
 
-        def gather(t, d, first, n, run, base):
-            window = T + SPARE if n == c2 else T
-            nc.vector.tensor_copy(
-                one_plane(base, n, run),
-                h[:, t * T : t * T + window].indirect(lists[d][:, first // 16 : (first + n) // 16]),
-            )
+        def gather(t, first, n):
+            window = T + SPARE if n == T else T
+            for d in range(2):
+                nc.vector.tensor_copy(
+                    one_plane(t, d, first, n),
+                    h[:, t * T : t * T + window].indirect(lists[d][:, first // 16 : (first + n) // 16]),
+                )
 
-        def long_base(t, d, first):
-            return picked_long + (2 * (t - 1) + d) * long_span + span(first, RUN)
-
-        def z_rows(z_planes, n, t0, planes):
-            rows = work[:, z_planes + t0 * n : z_planes + (t0 + planes) * n]
-            return rows.rearrange("p (t u c) -> p t u c", t=planes, c=RUN)
+        def near(rows):
+            return rows.rearrange("p t (c i) -> p c t i", i=NEAR)
 
         def woven(base, n):
             return work[:, base : base + PACK * n].rearrange("p (c i t) -> p c t i", i=NEAR, t=PACK)
-
-        def weave_h(first, n, base):
-            h_planes = h[:, : PACK * T].rearrange("p (t c) -> p t c", t=PACK)
-            nc.scalar.copy(out=woven(base, n), in_=near(h_planes[:, :, first : first + n]))
-
-        def gather_plane0(first, n):
-            for d in range(2):
-                gather(0, d, first, n, RUN, picked_plane0 + d * span(n, RUN))
-
-        def finish_z(first, n, z_planes, z_woven):
-            for t0, planes, base, list_pitch in (
-                (0, 1, picked_plane0, span(n, RUN)),
-                (1, 2, long_base(1, 0, first), long_span),
-            ):
-                nc.vector.tensor_tensor(
-                    z_rows(z_planes, n, t0, planes),
-                    runs(base, n, RUN, planes, planes * list_pitch),
-                    runs(base + list_pitch, n, RUN, planes, planes * list_pitch),
-                    MAX,
-                )
-            planes_of_z = work[:, z_planes : z_planes + PACK * n].rearrange("p (t c) -> p t c", t=PACK)
-            nc.scalar.copy(out=woven(z_woven, n), in_=near(planes_of_z))
 
         def quantise(codes, scale, first, n, base):
             nc.vector.quantize_mx(
@@ -220,78 +182,125 @@ def tile_picked_wsagecat_max_l_kernel(
                 in_=work[:, base : base + PACK * n],
             )
 
-        def finish_out(first, n):
-            acc_o = psum_o.tile([P, BANK], F32, name="acc_o")
-            for start, width in powers_of_two(n):
-                cols = slice(first + start, first + start + width)
-                for s, (codes, scale) in enumerate(((h_codes, h_scale), (z_codes, z_scale))):
-                    nc.tensor.matmul_mx(
-                        out=acc_o[:, start : start + width],
-                        lhsT=w23_codes[:, s * N : (s + 1) * N].bitcast(FP8X4),
-                        lhsT_scale=w23_scale[:, s * N : (s + 1) * N],
-                        rhs=codes[:, cols].bitcast(FP8X4),
-                        rhs_scale=scale[:, cols],
-                        start=(s == 0),
-                        stop=(s == 1),
-                    )
-            result = keep.tile([P, n], F32, name="result%d" % first)
-            nc.scalar.copy(out=result[:], in_=acc_o[:, :n])
-            nc.sync.dma_start(out=out[:, first : first + n], in_=result[:])
+        edges = (0, QUARTER, 2 * QUARTER, 3 * QUARTER, 3 * QUARTER + QUARTER // 2, T)
+        for piece in range(len(edges) - 1):
+            h_piece(3, edges[piece], edges[piece + 1], piece % 2 == 1)
+        gather(3, 0, T)
 
-        weave_h(c0, n0, h_woven0)
+        for s, w in enumerate((w2, w3)):
+            w_out = raw.tile([P, PACK, N], F32, name="w_out", tag="raw")
+            nc.sync.dma_start(out=w_out[:], in_=w.rearrange("(p j) n -> p j n", j=PACK))
+            base = place(2 - s, 1, 0) - PACK * N // 2
+            nc.scalar.copy(out=woven(base, N), in_=near(w_out[:]))
+            quantise(w23_codes, w23_scale, s * N, N, base)
 
-        for t in (3, 2, 1):
-            for d in range(2):
-                gather(t, d, 0, c2, RUN, long_base(t, d, 0))
+        for t in (2, 1, 0):
+            h_piece(t, 0, BANK, False)
+            h_piece(t, BANK, T, False)
+        for t in (2, 1):
+            gather(t, 0, T)
 
-        diff = keep.tile([P, c2], F32)
-        nc.gpsimd.tensor_tensor(
-            diff[:].rearrange("p (u c) -> p u c", c=RUN),
-            one_plane(long_base(3, 0, 0), c2, RUN),
-            one_plane(long_base(3, 1, 0), c2, RUN),
-            SUB,
-        )
-        excess = raw.tile([P, c2], F32, name="excess", tag="raw")
-        nc.scalar.activation(excess[:], diff[:], RELU)
-        for first, n, z_planes in ((c0, n0, z_planes0), (c1, n1, z_planes1)):
-            nc.gpsimd.tensor_tensor(
-                z_rows(z_planes, n, 3, 1)[:, 0, :, :],
-                excess[:, first : first + n].rearrange("p (u c) -> p u c", c=RUN),
-                one_plane(long_base(3, 1, first), n, RUN),
-                ADD,
-            )
-        weave_h(c1, n1, h_woven1)
-        weave_h(c2, n2, h_woven2)
+        def weave_h(first, base):
+            h_planes = h[:, : PACK * T].rearrange("p (t c) -> p t c", t=PACK)
+            nc.scalar.copy(out=woven(base, 2 * PIECE), in_=near(h_planes[:, :, first : first + 2 * PIECE]))
 
-        gather_plane0(c0, n0)
-        for first in (c0, c0 + QUARTER):
-            quantise(h_codes, h_scale, first, QUARTER, h_woven0 + PACK * first)
+        def quantise_h(first, base, order):
+            for k in order:
+                quantise(h_codes, h_scale, first + k * PIECE, PIECE, base + k * woven_piece)
+
+        def z_rows(z_planes, n, t0, planes):
+            rows = work[:, z_planes + t0 * n : z_planes + (t0 + planes) * n]
+            return rows.rearrange("p (t u c) -> p t u c", t=planes, c=RUN)
+
+        scratch = [keep.tile([P, n0], F32, name="scratch%d" % k) for k in range(4)]
+
+        def side_max(t, diffs, excesses):
+            parts = ((c0, n0, z_planes0), (c1, n1, z_planes1))
+            for (first, n, z_planes), diff in zip(parts, diffs):
+                nc.gpsimd.tensor_tensor(
+                    diff[:, :n].rearrange("p (u c) -> p u c", c=RUN),
+                    one_plane(t, 0, first, n),
+                    one_plane(t, 1, first, n),
+                    SUB,
+                )
+            for (first, n, z_planes), diff, excess in zip(parts, diffs, excesses):
+                nc.scalar.activation(excess[:, :n], diff[:, :n], RELU)
+                nc.gpsimd.tensor_tensor(
+                    z_rows(z_planes, n, t, 1)[:, 0, :, :],
+                    excess[:, :n].rearrange("p (u c) -> p u c", c=RUN),
+                    one_plane(t, 1, first, n),
+                    ADD,
+                )
+
+        weave_h(0, h_woven0)
+        side_max(3, scratch[0:2], scratch[2:4])
+        weave_h(2 * PIECE, h_woven1)
+        side_max(2, (scratch[3], scratch[2]), scratch[0:2])
+        weave_h(4 * PIECE, h_woven2)
+        weave_h(6 * PIECE, h_woven3)
+
+        def finish_z(first, n, z_planes, z_woven):
+            for t in (1, 0):
+                nc.vector.tensor_tensor(
+                    z_rows(z_planes, n, t, 1)[:, 0, :, :], one_plane(t, 0, first, n), one_plane(t, 1, first, n), MAX
+                )
+            planes_of_z = work[:, z_planes : z_planes + PACK * n].rearrange("p (t c) -> p t c", t=PACK)
+            nc.scalar.copy(out=woven(z_woven, n), in_=near(planes_of_z))
+
+        result = keep.tile([P, T], F32)
+        result0 = work[:, z_planes1 : z_planes1 + 2 * n0].bitcast(F32)
+
+        def finish_out(first, n, on_vector):
+            acc_o = psum.tile([P, BANK], F32, name="acc_o", tag="acc")
+            cols = slice(first, first + n)
+            for s, (codes, scale) in enumerate(((h_codes, h_scale), (z_codes, z_scale))):
+                nc.tensor.matmul_mx(
+                    out=acc_o[:, :n],
+                    lhsT=w23_codes[:, s * N : (s + 1) * N].bitcast(FP8X4),
+                    lhsT_scale=w23_scale[:, s * N : (s + 1) * N],
+                    rhs=codes[:, cols].bitcast(FP8X4),
+                    rhs_scale=scale[:, cols],
+                    start=(s == 0),
+                    stop=(s == 1),
+                )
+            dst = result0 if first == 0 else result[:, cols]
+            if on_vector:
+                nc.vector.tensor_copy(out=dst, in_=acc_o[:, :n])
+            else:
+                nc.scalar.copy(out=dst, in_=acc_o[:, :n])
+
+        def store(first, stop):
+            nc.sync.dma_start(out=out[:, first:stop], in_=result0 if first == 0 else result[:, first:stop])
+
+        gather(0, c0, n0)
+        quantise_h(0, h_woven0, (1, 0))
         finish_z(c0, n0, z_planes0, z_woven0)
+        quantise_h(2 * PIECE, h_woven1, (0, 1))
 
-        gather_plane0(c1, n1)
-        for start, width in powers_of_two(n1):
-            quantise(h_codes, h_scale, c1 + start, width, h_woven1 + PACK * start)
-        quantise(h_codes, h_scale, c2, n2, h_woven2)
+        gather(0, c1, n1)
+        quantise_h(4 * PIECE, h_woven2, (1, 0))
         finish_z(c1, n1, z_planes1, z_woven1)
-        for first in (c0, c0 + QUARTER):
-            quantise(z_codes, z_scale, first, QUARTER, z_woven0 + PACK * first)
-        finish_out(c0, n0)
+        quantise_h(6 * PIECE, h_woven3, (0, 1))
+        for start, width in powers_of_two(n0, QUARTER):
+            quantise(z_codes, z_scale, c0 + start, width, z_woven0 + PACK * start)
+        finish_out(*GROUPS[0], False)
+        store(0, GROUPS[1][0])
 
-        for t in (3, 2, 1, 0):
-            gather(t, 0, c2, n2, LAST_RUN, last_a + t * last_span)
-            if t > 0:
-                gather(t, 1, c2, n2, LAST_RUN, last_b + t * last_span)
-        for start, width in reversed(powers_of_two(n1)):
-            quantise(z_codes, z_scale, c1 + start, width, z_woven1 + PACK * start)
-        finish_out(c1, n1)
-        gather(0, 1, c2, n2, LAST_RUN, last_b)
-        for u in range(n2 // LAST_RUN):
+        gather(0, c2, n2)
+        quantise(z_codes, z_scale, c1, n2, z_woven1)
+        for start, width in powers_of_two(n1 - n2, QUARTER):
+            quantise(z_codes, z_scale, c1 + n2 + start, width, z_woven1 + PACK * (n2 + start))
+        finish_out(*GROUPS[1], False)
+        store(GROUPS[1][0], GROUPS[2][0])
+        finish_out(*GROUPS[2], False)
+        for u in range(n2 // RUN):
             nc.vector.tensor_tensor(
-                woven(z_woven2 + u * PACK * LAST_RUN, LAST_RUN),
-                near(runs(last_a, n2, LAST_RUN, PACK, last_span)[:, :, u, :]),
-                near(runs(last_b, n2, LAST_RUN, PACK, last_span)[:, :, u, :]),
+                woven(z_woven2 + u * PACK * RUN, RUN),
+                near(runs(0, c2, n2, PACK)[:, :, u, :]),
+                near(runs(1, c2, n2, PACK)[:, :, u, :]),
                 MAX,
             )
-        for u in range(n2 // LAST_RUN):
-            quantise(z_codes, z_scale, c2 + u * LAST_RUN, LAST_RUN, z_woven2 + u * PACK * LAST_RUN)
-        finish_out(c2, n2)
+        for u in range(n2 // RUN):
+            quantise(z_codes, z_scale, c2 + u * RUN, RUN, z_woven2 + u * PACK * RUN)
+        finish_out(*GROUPS[3], True)
+        store(GROUPS[2][0], T)

@@ -83,6 +83,10 @@ def tile_picked_wsagecat_max_l_kernel(
             nc.sync.dma_start(out=x_codes[:, nodes].bitcast(I32), in_=x_rows[:, nodes])
         nc.sync.dma_start(lists[0][:], pos1)
         nc.sync.dma_start(lists[1][:], pos2)
+        halves = h[:, : (PACK - 1) * T].rearrange("p (b c) -> p b c", c=BANK)
+        w23_raw = (halves[:, 2:6, 0:N], halves[:, 0:4, N : 2 * N])
+        for s, w in enumerate((w2, w3)):
+            nc.sync.dma_start(out=w23_raw[s], in_=w.rearrange("(p j) n -> p j n", j=PACK))
 
         w1_woven = keep.tile([P, PACK, P, PACK], BF16, align_bytes=64)
         w1_codes = keep.tile([P, PACK, P], U32, align_bytes=64)
@@ -124,19 +128,21 @@ def tile_picked_wsagecat_max_l_kernel(
         (c0, n0), (c1, n1), (c2, n2) = CHUNKS
         whole = span(T)
         woven_piece = PACK * PIECE
-        z_planes0 = 0
-        h_woven0 = z_planes0 + 2 * n0 - 2 * woven_piece
-        z_planes1 = z_planes0 + PACK * n0 + 2 * woven_piece - 2 * n1
-        h_woven2 = z_planes1 + 2 * n1 - 2 * woven_piece
-        h_woven3 = z_planes1 + PACK * n1
-        z_woven1 = h_woven3 + 2 * woven_piece
+        h_woven1 = 0
+        z_planes1 = h_woven1 + woven_piece
+        h_woven2 = z_planes1 + PACK * n1
+        z_woven1 = h_woven2 + 4 * woven_piece
         z_woven2 = z_woven1
-        picked0_c0 = z_woven1 + PACK * n1
-        picked0_c1 = picked0_c0 + 2 * span(n0)
-        h_woven1 = (picked0_c1 + 2 * span(n1) - woven_piece + 31) // 32 * 32
-        picked = h_woven1 + 2 * woven_piece
-        z_woven0 = picked + 128
-        work = keep.tile([P, picked + 2 * (PACK + 1) * whole], BF16, align_bytes=64)
+        z_woven0 = z_woven1 + PACK * n1
+        h_woven0 = z_woven0 + PACK * n0
+        z_planes0 = h_woven0 + woven_piece
+        first0 = [z_planes0 + PACK * n0 + d * (span(n0) + whole + woven_piece // 2) for d in range(2)]
+        second0 = [h_woven0, first0[1]]
+        last0 = [z_woven0 + (d + 1) * PACK * n0 // 2 - span(n2) for d in range(2)]
+        plane1 = [first0[d] + span(n0) for d in range(2)]
+        pitch = [plane1[d] + span(c2) - last0[d] for d in range(2)]
+        w23_woven = plane1[1] + pitch[1] - 2 * c2
+        work = keep.tile([P, last0[1] + PACK * pitch[1]], BF16, align_bytes=64)
         h_codes = keep.tile([P, T], U32, align_bytes=64)
         h_scale = keep.tile([P, T], U8, align_bytes=64)
         z_codes = keep.tile([P, T], U32, align_bytes=64)
@@ -146,15 +152,15 @@ def tile_picked_wsagecat_max_l_kernel(
 
         def place(t, d, first):
             if t == 0 and first == c0:
-                return picked0_c0 + d * span(n0)
+                return first0[d]
             if t == 0 and first == c1:
-                return picked0_c1 + d * span(n1)
-            return picked + (2 * t + d) * whole + span(first)
+                return second0[d]
+            return plane1[d] + (t - 1) * pitch[d] + span(first)
 
         def runs(d, first, n, planes):
             base = place(0, d, first)
-            pitch = place(1, d, first) - base
-            block = work[:, base : base + planes * pitch].rearrange("p (t r) -> p t r", t=planes)
+            step = place(1, d, first) - base
+            block = work[:, base : base + planes * step].rearrange("p (t r) -> p t r", t=planes)
             return block[:, :, : span(n)].rearrange("p t (u c) -> p t u c", c=RUN + GAP)[:, :, :, :RUN]
 
         def one_plane(t, d, first, n):
@@ -187,12 +193,9 @@ def tile_picked_wsagecat_max_l_kernel(
             h_piece(3, edges[piece], edges[piece + 1], piece % 2 == 1)
         gather(3, 0, T)
 
-        for s, w in enumerate((w2, w3)):
-            w_out = raw.tile([P, PACK, N], F32, name="w_out", tag="raw")
-            nc.sync.dma_start(out=w_out[:], in_=w.rearrange("(p j) n -> p j n", j=PACK))
-            base = place(2 - s, 1, 0) - PACK * N // 2
-            nc.scalar.copy(out=woven(base, N), in_=near(w_out[:]))
-            quantise(w23_codes, w23_scale, s * N, N, base)
+        for s in range(2):
+            nc.scalar.copy(out=woven(w23_woven + s * PACK * N, N), in_=near(w23_raw[s]))
+        quantise(w23_codes, w23_scale, 0, 2 * N, w23_woven)
 
         for t in (2, 1, 0):
             h_piece(t, 0, BANK, False)
@@ -200,50 +203,42 @@ def tile_picked_wsagecat_max_l_kernel(
         for t in (2, 1):
             gather(t, 0, T)
 
-        def weave_h(first, base):
+        def weave_h(first, n, base):
             h_planes = h[:, : PACK * T].rearrange("p (t c) -> p t c", t=PACK)
-            nc.scalar.copy(out=woven(base, 2 * PIECE), in_=near(h_planes[:, :, first : first + 2 * PIECE]))
+            nc.scalar.copy(out=woven(base, n), in_=near(h_planes[:, :, first : first + n]))
 
-        def quantise_h(first, base, order):
-            for k in order:
+        def quantise_pair(first, base):
+            for k in (1, 0):
                 quantise(h_codes, h_scale, first + k * PIECE, PIECE, base + k * woven_piece)
 
         def z_rows(z_planes, n, t0, planes):
             rows = work[:, z_planes + t0 * n : z_planes + (t0 + planes) * n]
             return rows.rearrange("p (t u c) -> p t u c", t=planes, c=RUN)
 
-        scratch = [keep.tile([P, n0], F32, name="scratch%d" % k) for k in range(4)]
+        scratch = [work[:, w23_woven : w23_woven + 2 * c2].bitcast(F32)]
+        scratch.append(keep.tile([P, c2], F32, name="scratch1")[:])
 
-        def side_max(t, diffs, excesses):
-            parts = ((c0, n0, z_planes0), (c1, n1, z_planes1))
-            for (first, n, z_planes), diff in zip(parts, diffs):
-                nc.gpsimd.tensor_tensor(
-                    diff[:, :n].rearrange("p (u c) -> p u c", c=RUN),
-                    one_plane(t, 0, first, n),
-                    one_plane(t, 1, first, n),
-                    SUB,
-                )
-            for (first, n, z_planes), diff, excess in zip(parts, diffs, excesses):
-                nc.scalar.activation(excess[:, :n], diff[:, :n], RELU)
+        def side_max(t, diff, excess):
+            nc.gpsimd.tensor_tensor(
+                diff.rearrange("p (u c) -> p u c", c=RUN), one_plane(t, 0, 0, c2), one_plane(t, 1, 0, c2), SUB
+            )
+            for first, n, z_planes in ((c0, n0, z_planes0), (c1, n1, z_planes1)):
+                nc.scalar.activation(excess[:, first : first + n], diff[:, first : first + n], RELU)
                 nc.gpsimd.tensor_tensor(
                     z_rows(z_planes, n, t, 1)[:, 0, :, :],
-                    excess[:, :n].rearrange("p (u c) -> p u c", c=RUN),
+                    excess[:, first : first + n].rearrange("p (u c) -> p u c", c=RUN),
                     one_plane(t, 1, first, n),
                     ADD,
                 )
 
-        weave_h(0, h_woven0)
-        side_max(3, scratch[0:2], scratch[2:4])
-        weave_h(2 * PIECE, h_woven1)
-        side_max(2, (scratch[3], scratch[2]), scratch[0:2])
-        weave_h(4 * PIECE, h_woven2)
-        weave_h(6 * PIECE, h_woven3)
+        weave_h(0, 2 * PIECE, h_woven0)
+        side_max(3, scratch[0], scratch[1])
+        weave_h(2 * PIECE, 2 * PIECE, h_woven1)
+        weave_h(4 * PIECE, 4 * PIECE, h_woven2)
+        side_max(2, scratch[1], h[:, PACK * T - c2 : PACK * T])
 
         def finish_z(first, n, z_planes, z_woven):
-            for t in (1, 0):
-                nc.vector.tensor_tensor(
-                    z_rows(z_planes, n, t, 1)[:, 0, :, :], one_plane(t, 0, first, n), one_plane(t, 1, first, n), MAX
-                )
+            nc.vector.tensor_tensor(z_rows(z_planes, n, 0, 2), runs(0, first, n, 2), runs(1, first, n, 2), MAX)
             planes_of_z = work[:, z_planes : z_planes + PACK * n].rearrange("p (t c) -> p t c", t=PACK)
             nc.scalar.copy(out=woven(z_woven, n), in_=near(planes_of_z))
 
@@ -273,14 +268,13 @@ def tile_picked_wsagecat_max_l_kernel(
             nc.sync.dma_start(out=out[:, first:stop], in_=result0 if first == 0 else result[:, first:stop])
 
         gather(0, c0, n0)
-        quantise_h(0, h_woven0, (1, 0))
+        quantise_pair(0, h_woven0)
         finish_z(c0, n0, z_planes0, z_woven0)
-        quantise_h(2 * PIECE, h_woven1, (0, 1))
 
         gather(0, c1, n1)
-        quantise_h(4 * PIECE, h_woven2, (1, 0))
+        quantise_pair(2 * PIECE, h_woven1)
         finish_z(c1, n1, z_planes1, z_woven1)
-        quantise_h(6 * PIECE, h_woven3, (0, 1))
+        quantise(h_codes, h_scale, 4 * PIECE, 4 * PIECE, h_woven2)
         for start, width in powers_of_two(n0, QUARTER):
             quantise(z_codes, z_scale, c0 + start, width, z_woven0 + PACK * start)
         finish_out(*GROUPS[0], False)

@@ -83,27 +83,36 @@ def tile_picked_wsagecat_max_l_kernel(
             nc.sync.dma_start(out=x_codes[:, nodes].bitcast(I32), in_=x_rows[:, nodes])
         nc.sync.dma_start(lists[0][:], pos1)
         nc.sync.dma_start(lists[1][:], pos2)
-        halves = h[:, : (PACK - 1) * T].rearrange("p (b c) -> p b c", c=BANK)
-        w23_raw = (halves[:, 2:6, 0:N], halves[:, 0:4, N : 2 * N])
+        w23_raw = keep.tile([P, 2, PACK, N], F32)
         for s, w in enumerate((w2, w3)):
-            nc.sync.dma_start(out=w23_raw[s], in_=w.rearrange("(p j) n -> p j n", j=PACK))
+            nc.sync.dma_start(out=w23_raw[:, s], in_=w.rearrange("(p j) n -> p j n", j=PACK))
 
         w1_woven = keep.tile([P, PACK, P, PACK], BF16, align_bytes=64)
         w1_codes = keep.tile([P, PACK, P], U32, align_bytes=64)
         w1_scale = keep.tile([P, PACK, P], U8, align_bytes=64)
         m_half = P // 2
-        for u in range(2):
-            for t0, cast in ((2, nc.vector.tensor_copy), (0, nc.scalar.copy)):
-                cast(
-                    out=w1_woven[:, t0 : t0 + 2, u * m_half : (u + 1) * m_half, :].rearrange("p t m j -> p m j t"),
-                    in_=w1_raw[u][:].rearrange("p j (m t) -> p m j t", t=PACK)[:, :, :, t0 : t0 + 2],
-                )
-        for t0, t1 in ((3, 4), (2, 3), (0, 2)):
-            nc.vector.quantize_mx(
-                out=w1_codes[:, t0:t1, :].rearrange("p t m -> p (t m)").bitcast(FP8X4),
-                scales=w1_scale[:, t0:t1, :].rearrange("p t m -> p (t m)"),
-                in_=w1_woven[:, t0:t1, :, :].rearrange("p t m j -> p (t m j)"),
+
+        def cast_w1(cast, u, t0, t1):
+            cast(
+                out=w1_woven[:, t0:t1, u * m_half : (u + 1) * m_half, :].rearrange("p t m j -> p m j t"),
+                in_=w1_raw[u][:].rearrange("p j (m t) -> p m j t", t=PACK)[:, :, :, t0:t1],
             )
+
+        def quantise_w1(t0, t1, m0, m1):
+            nc.vector.quantize_mx(
+                out=w1_codes[:, t0:t1, m0:m1].rearrange("p t m -> p (t m)").bitcast(FP8X4),
+                scales=w1_scale[:, t0:t1, m0:m1].rearrange("p t m -> p (t m)"),
+                in_=w1_woven[:, t0:t1, m0:m1, :].rearrange("p t m j -> p (t m j)"),
+            )
+
+        cast_w1(nc.vector.tensor_copy, 0, 2, 4)
+        cast_w1(nc.scalar.copy, 0, 0, 2)
+        quantise_w1(3, 4, 0, m_half)
+        cast_w1(nc.vector.tensor_copy, 1, 3, 4)
+        cast_w1(nc.scalar.copy, 1, 0, 3)
+        quantise_w1(3, 4, m_half, P)
+        quantise_w1(2, 3, 0, P)
+        quantise_w1(0, 2, 0, P)
 
         def h_piece(t, start, stop, on_vector):
             acc_h = psum.tile([P, BANK], F32, name="acc_h", tag="acc")
@@ -136,12 +145,11 @@ def tile_picked_wsagecat_max_l_kernel(
         z_woven0 = z_woven1 + PACK * n1
         h_woven0 = z_woven0 + PACK * n0
         z_planes0 = h_woven0 + woven_piece
-        first0 = [z_planes0 + PACK * n0 + d * (span(n0) + whole + woven_piece // 2) for d in range(2)]
+        first0 = [z_planes0 + PACK * n0 + d * (span(n0) + whole) for d in range(2)]
         second0 = [h_woven0, first0[1]]
         last0 = [z_woven0 + (d + 1) * PACK * n0 // 2 - span(n2) for d in range(2)]
         plane1 = [first0[d] + span(n0) for d in range(2)]
         pitch = [plane1[d] + span(c2) - last0[d] for d in range(2)]
-        w23_woven = plane1[1] + pitch[1] - 2 * c2
         work = keep.tile([P, last0[1] + PACK * pitch[1]], BF16, align_bytes=64)
         h_codes = keep.tile([P, T], U32, align_bytes=64)
         h_scale = keep.tile([P, T], U8, align_bytes=64)
@@ -193,10 +201,6 @@ def tile_picked_wsagecat_max_l_kernel(
             h_piece(3, edges[piece], edges[piece + 1], piece % 2 == 1)
         gather(3, 0, T)
 
-        for s in range(2):
-            nc.scalar.copy(out=woven(w23_woven + s * PACK * N, N), in_=near(w23_raw[s]))
-        quantise(w23_codes, w23_scale, 0, 2 * N, w23_woven)
-
         for t in (2, 1, 0):
             h_piece(t, 0, BANK, False)
             h_piece(t, BANK, T, False)
@@ -215,14 +219,20 @@ def tile_picked_wsagecat_max_l_kernel(
             rows = work[:, z_planes + t0 * n : z_planes + (t0 + planes) * n]
             return rows.rearrange("p (t u c) -> p t u c", t=planes, c=RUN)
 
-        scratch = [work[:, w23_woven : w23_woven + 2 * c2].bitcast(F32)]
-        scratch.append(keep.tile([P, c2], F32, name="scratch1")[:])
+        shift = n0 // 2
+        first_diff = keep.tile([P, c2], F32)
+        shared = keep.tile([P, shift + c2], F32, align_bytes=64)
 
         def side_max(t, diff, excess):
-            nc.gpsimd.tensor_tensor(
-                diff.rearrange("p (u c) -> p u c", c=RUN), one_plane(t, 0, 0, c2), one_plane(t, 1, 0, c2), SUB
-            )
-            for first, n, z_planes in ((c0, n0, z_planes0), (c1, n1, z_planes1)):
+            parts = ((c0, n0, z_planes0), (c1, n1, z_planes1))
+            for first, n, z_planes in parts:
+                nc.gpsimd.tensor_tensor(
+                    diff[:, first : first + n].rearrange("p (u c) -> p u c", c=RUN),
+                    one_plane(t, 0, first, n),
+                    one_plane(t, 1, first, n),
+                    SUB,
+                )
+            for first, n, z_planes in parts:
                 nc.scalar.activation(excess[:, first : first + n], diff[:, first : first + n], RELU)
                 nc.gpsimd.tensor_tensor(
                     z_rows(z_planes, n, t, 1)[:, 0, :, :],
@@ -232,10 +242,17 @@ def tile_picked_wsagecat_max_l_kernel(
                 )
 
         weave_h(0, 2 * PIECE, h_woven0)
-        side_max(3, scratch[0], scratch[1])
+        side_max(3, first_diff[:], shared[:, :c2])
         weave_h(2 * PIECE, 2 * PIECE, h_woven1)
         weave_h(4 * PIECE, 4 * PIECE, h_woven2)
-        side_max(2, scratch[1], h[:, PACK * T - c2 : PACK * T])
+        side_max(2, shared[:, shift:], h[:, PACK * T - c2 : PACK * T])
+
+        w23_woven = shared[:, n0 : 2 * n0].bitcast(BF16)
+        for s in range(2):
+            nc.scalar.copy(
+                out=w23_woven[:, s * PACK * N : (s + 1) * PACK * N].rearrange("p (c i t) -> p c t i", i=NEAR, t=PACK),
+                in_=near(w23_raw[:, s]),
+            )
 
         def finish_z(first, n, z_planes, z_woven):
             nc.vector.tensor_tensor(z_rows(z_planes, n, 0, 2), runs(0, first, n, 2), runs(1, first, n, 2), MAX)
@@ -275,6 +292,7 @@ def tile_picked_wsagecat_max_l_kernel(
         quantise_pair(2 * PIECE, h_woven1)
         finish_z(c1, n1, z_planes1, z_woven1)
         quantise(h_codes, h_scale, 4 * PIECE, 4 * PIECE, h_woven2)
+        nc.vector.quantize_mx(out=w23_codes[:].bitcast(FP8X4), scales=w23_scale[:], in_=w23_woven)
         for start, width in powers_of_two(n0, QUARTER):
             quantise(z_codes, z_scale, c0 + start, width, z_woven0 + PACK * start)
         finish_out(*GROUPS[0], False)

@@ -28,7 +28,7 @@ SPARE = 352
 PIECE = 128
 
 CHUNKS = ((0, 512), (512, 384), (896, 128))
-GROUPS = ((0, 512), (512, 256), (768, 128), (896, 128))
+BANKS = ((0, 384), (384, 384), (768, 128), (896, 128))
 
 
 def powers_of_two(n, widest):
@@ -139,15 +139,15 @@ def tile_picked_wsagecat_max_l_kernel(
         woven_piece = PACK * PIECE
         h_woven1 = 0
         z_planes1 = h_woven1 + woven_piece
-        h_woven2 = z_planes1 + PACK * n1
-        z_woven1 = h_woven2 + 4 * woven_piece
-        z_woven2 = z_woven1
-        z_woven0 = z_woven1 + PACK * n1
+        z_planes2 = z_planes1 + PACK * n1
+        z_woven1 = z_planes2 + PACK * n2
+        z_woven2 = z_woven1 + PACK * n1
+        z_woven0 = z_woven2 + PACK * n2
         h_woven0 = z_woven0 + PACK * n0
         z_planes0 = h_woven0 + woven_piece
         first0 = [z_planes0 + PACK * n0 + d * (span(n0) + whole) for d in range(2)]
         second0 = [h_woven0, first0[1]]
-        last0 = [z_woven0 + (d + 1) * PACK * n0 // 2 - span(n2) for d in range(2)]
+        last0 = [z_woven0 + d * woven_piece // 2 for d in range(2)]
         plane1 = [first0[d] + span(n0) for d in range(2)]
         pitch = [plane1[d] + span(c2) - last0[d] for d in range(2)]
         work = keep.tile([P, last0[1] + PACK * pitch[1]], BF16, align_bytes=64)
@@ -186,14 +186,15 @@ def tile_picked_wsagecat_max_l_kernel(
         def near(rows):
             return rows.rearrange("p t (c i) -> p c t i", i=NEAR)
 
-        def woven(base, n):
-            return work[:, base : base + PACK * n].rearrange("p (c i t) -> p c t i", i=NEAR, t=PACK)
+        def region(base, n):
+            return work[:, base : base + PACK * n]
 
-        def quantise(codes, scale, first, n, base):
+        def woven(values):
+            return values.rearrange("p (c i t) -> p c t i", i=NEAR, t=PACK)
+
+        def quantise(codes, scale, first, n, values):
             nc.vector.quantize_mx(
-                out=codes[:, first : first + n].bitcast(FP8X4),
-                scales=scale[:, first : first + n],
-                in_=work[:, base : base + PACK * n],
+                out=codes[:, first : first + n].bitcast(FP8X4), scales=scale[:, first : first + n], in_=values
             )
 
         edges = (0, QUARTER, 2 * QUARTER, 3 * QUARTER, 3 * QUARTER + QUARTER // 2, T)
@@ -207,75 +208,82 @@ def tile_picked_wsagecat_max_l_kernel(
         for t in (2, 1):
             gather(t, 0, T)
 
-        def weave_h(first, n, base):
+        def weave_h(first, n, values):
             h_planes = h[:, : PACK * T].rearrange("p (t c) -> p t c", t=PACK)
-            nc.scalar.copy(out=woven(base, n), in_=near(h_planes[:, :, first : first + n]))
+            nc.scalar.copy(out=woven(values), in_=near(h_planes[:, :, first : first + n]))
 
         def quantise_pair(first, base):
             for k in (1, 0):
-                quantise(h_codes, h_scale, first + k * PIECE, PIECE, base + k * woven_piece)
+                quantise(h_codes, h_scale, first + k * PIECE, PIECE, region(base + k * woven_piece, PIECE))
 
         def z_rows(z_planes, n, t0, planes):
             rows = work[:, z_planes + t0 * n : z_planes + (t0 + planes) * n]
             return rows.rearrange("p (t u c) -> p t u c", t=planes, c=RUN)
 
-        shift = n0 // 2
-        first_diff = keep.tile([P, c2], F32)
-        shared = keep.tile([P, shift + c2], F32, align_bytes=64)
+        parts = ((c0, n0, z_planes0), (c1, n1, z_planes1))
 
-        def side_max(t, diff, excess):
-            parts = ((c0, n0, z_planes0), (c1, n1, z_planes1))
-            for first, n, z_planes in parts:
+        def side_max(t, diffs, excesses):
+            for (first, n, z_planes), diff in zip(parts, diffs):
                 nc.gpsimd.tensor_tensor(
-                    diff[:, first : first + n].rearrange("p (u c) -> p u c", c=RUN),
+                    diff.rearrange("p (u c) -> p u c", c=RUN),
                     one_plane(t, 0, first, n),
                     one_plane(t, 1, first, n),
                     SUB,
                 )
-            for first, n, z_planes in parts:
-                nc.scalar.activation(excess[:, first : first + n], diff[:, first : first + n], RELU)
+            for (first, n, z_planes), diff, excess in zip(parts, diffs, excesses):
+                nc.scalar.activation(excess, diff, RELU)
                 nc.gpsimd.tensor_tensor(
                     z_rows(z_planes, n, t, 1)[:, 0, :, :],
-                    excess[:, first : first + n].rearrange("p (u c) -> p u c", c=RUN),
+                    excess.rearrange("p (u c) -> p u c", c=RUN),
                     one_plane(t, 1, first, n),
                     ADD,
                 )
 
-        weave_h(0, 2 * PIECE, h_woven0)
-        side_max(3, first_diff[:], shared[:, :c2])
-        weave_h(2 * PIECE, 2 * PIECE, h_woven1)
+        def both_parts(tile, start):
+            return (tile[:, start : start + n0], tile[:, start + n0 : start + c2])
+
+        diff3 = keep.tile([P, c2], F32)
+        shared = keep.tile([P, 2 * c2], F32, align_bytes=64)
+        excess3_at = 192
+        diff2_at = excess3_at + n0 // 2
+        h_woven2 = shared[:, : 2 * BANK].bitcast(BF16)
+        w23_woven = shared[:, 2 * c2 - BANK :].bitcast(BF16)
+
+        weave_h(0, 2 * PIECE, region(h_woven0, 2 * PIECE))
+        side_max(3, both_parts(diff3, 0), both_parts(shared, excess3_at))
+        weave_h(2 * PIECE, 2 * PIECE, region(h_woven1, 2 * PIECE))
+        side_max(2, both_parts(shared, diff2_at), (h[:, 3 * T : 3 * T + n0], diff3[:, :n1]))
         weave_h(4 * PIECE, 4 * PIECE, h_woven2)
-        side_max(2, shared[:, shift:], h[:, PACK * T - c2 : PACK * T])
-
-        w23_woven = shared[:, n0 : 2 * n0].bitcast(BF16)
         for s in range(2):
-            nc.scalar.copy(
-                out=w23_woven[:, s * PACK * N : (s + 1) * PACK * N].rearrange("p (c i t) -> p c t i", i=NEAR, t=PACK),
-                in_=near(w23_raw[:, s]),
-            )
+            nc.scalar.copy(out=woven(w23_woven[:, s * PACK * N : (s + 1) * PACK * N]), in_=near(w23_raw[:, s]))
 
-        def finish_z(first, n, z_planes, z_woven):
-            nc.vector.tensor_tensor(z_rows(z_planes, n, 0, 2), runs(0, first, n, 2), runs(1, first, n, 2), MAX)
-            planes_of_z = work[:, z_planes : z_planes + PACK * n].rearrange("p (t c) -> p t c", t=PACK)
-            nc.scalar.copy(out=woven(z_woven, n), in_=near(planes_of_z))
+        def finish_z(first, n, planes, z_planes, z_woven):
+            nc.vector.tensor_tensor(
+                z_rows(z_planes, n, 0, planes), runs(0, first, n, planes), runs(1, first, n, planes), MAX
+            )
+            planes_of_z = region(z_planes, n).rearrange("p (t c) -> p t c", t=PACK)
+            nc.scalar.copy(out=woven(region(z_woven, n)), in_=near(planes_of_z))
 
         result = keep.tile([P, T], F32)
-        result0 = work[:, z_planes1 : z_planes1 + 2 * n0].bitcast(F32)
+        result0 = work[:, z_planes1 : z_planes1 + 2 * BANKS[0][1]].bitcast(F32)
 
-        def finish_out(first, n, on_vector):
+        def finish_out(first, pieces, on_vector):
             acc_o = psum.tile([P, BANK], F32, name="acc_o", tag="acc")
-            cols = slice(first, first + n)
-            for s, (codes, scale) in enumerate(((h_codes, h_scale), (z_codes, z_scale))):
-                nc.tensor.matmul_mx(
-                    out=acc_o[:, :n],
-                    lhsT=w23_codes[:, s * N : (s + 1) * N].bitcast(FP8X4),
-                    lhsT_scale=w23_scale[:, s * N : (s + 1) * N],
-                    rhs=codes[:, cols].bitcast(FP8X4),
-                    rhs_scale=scale[:, cols],
-                    start=(s == 0),
-                    stop=(s == 1),
-                )
-            dst = result0 if first == 0 else result[:, cols]
+            n = 0
+            for width in pieces:
+                cols = slice(first + n, first + n + width)
+                for s, (codes, scale) in enumerate(((h_codes, h_scale), (z_codes, z_scale))):
+                    nc.tensor.matmul_mx(
+                        out=acc_o[:, n : n + width],
+                        lhsT=w23_codes[:, s * N : (s + 1) * N].bitcast(FP8X4),
+                        lhsT_scale=w23_scale[:, s * N : (s + 1) * N],
+                        rhs=codes[:, cols].bitcast(FP8X4),
+                        rhs_scale=scale[:, cols],
+                        start=(s == 0),
+                        stop=(s == 1),
+                    )
+                n = n + width
+            dst = result0 if first == 0 else result[:, first : first + n]
             if on_vector:
                 nc.vector.tensor_copy(out=dst, in_=acc_o[:, :n])
             else:
@@ -284,35 +292,32 @@ def tile_picked_wsagecat_max_l_kernel(
         def store(first, stop):
             nc.sync.dma_start(out=out[:, first:stop], in_=result0 if first == 0 else result[:, first:stop])
 
+        def quantise_z(first, start, n, z_woven):
+            quantise(z_codes, z_scale, first + start, n, region(z_woven + PACK * start, n))
+
         gather(0, c0, n0)
         quantise_pair(0, h_woven0)
-        finish_z(c0, n0, z_planes0, z_woven0)
+        finish_z(c0, n0, 2, z_planes0, z_woven0)
 
         gather(0, c1, n1)
         quantise_pair(2 * PIECE, h_woven1)
-        finish_z(c1, n1, z_planes1, z_woven1)
+        finish_z(c1, n1, 2, z_planes1, z_woven1)
         quantise(h_codes, h_scale, 4 * PIECE, 4 * PIECE, h_woven2)
-        nc.vector.quantize_mx(out=w23_codes[:].bitcast(FP8X4), scales=w23_scale[:], in_=w23_woven)
-        for start, width in powers_of_two(n0, QUARTER):
-            quantise(z_codes, z_scale, c0 + start, width, z_woven0 + PACK * start)
-        finish_out(*GROUPS[0], False)
-        store(0, GROUPS[1][0])
+        quantise(w23_codes, w23_scale, 0, 2 * N, w23_woven)
+        quantise_z(c0, 0, PIECE, z_woven0)
+        quantise_z(c0, PIECE, 2 * PIECE, z_woven0)
+
+        finish_out(0, (256, 128), False)
+        store(0, 384)
 
         gather(0, c2, n2)
-        quantise(z_codes, z_scale, c1, n2, z_woven1)
-        for start, width in powers_of_two(n1 - n2, QUARTER):
-            quantise(z_codes, z_scale, c1 + n2 + start, width, z_woven1 + PACK * (n2 + start))
-        finish_out(*GROUPS[1], False)
-        store(GROUPS[1][0], GROUPS[2][0])
-        finish_out(*GROUPS[2], False)
-        for u in range(n2 // RUN):
-            nc.vector.tensor_tensor(
-                woven(z_woven2 + u * PACK * RUN, RUN),
-                near(runs(0, c2, n2, PACK)[:, :, u, :]),
-                near(runs(1, c2, n2, PACK)[:, :, u, :]),
-                MAX,
-            )
-        for u in range(n2 // RUN):
-            quantise(z_codes, z_scale, c2 + u * RUN, RUN, z_woven2 + u * PACK * RUN)
-        finish_out(*GROUPS[3], True)
-        store(GROUPS[2][0], T)
+        quantise_z(c0, 3 * PIECE, PIECE, z_woven0)
+        finish_z(c2, n2, PACK, z_planes2, z_woven2)
+        for start, width in powers_of_two(n1, QUARTER):
+            quantise_z(c1, start, width, z_woven1)
+        quantise_z(c2, 0, n2, z_woven2)
+        finish_out(384, (128, 256), False)
+        store(384, 768)
+        finish_out(768, (128,), False)
+        finish_out(896, (128,), True)
+        store(768, T)

@@ -53,7 +53,6 @@ def tile_picked_wsagecat_max_l_kernel(
     nc = tc.nc
     with ExitStack() as ctx:
         keep = ctx.enter_context(tc.tile_pool(name="keep", bufs=1))
-        raw = ctx.enter_context(tc.tile_pool(name="raw", bufs=2))
         psum = ctx.enter_context(tc.psum_pool(name="psum", bufs=8))
 
         lists = [keep.tile([P, T // 16], U16, name="list%d" % d) for d in range(2)]
@@ -65,18 +64,14 @@ def tile_picked_wsagecat_max_l_kernel(
         nc.vector.memset(h[:, PACK * T :], 0.0)
 
         w1_rows = w1.rearrange("(p j) c -> p j c", j=PACK)
-        half = H // 2
-        w1_raw = []
+        w1_raw = [keep.tile([P, 2, H], F32, name="w1_raw%d" % u) for u in range(2)]
         for u in range(2):
-            w1_half = raw.tile([P, PACK, half], F32, name="w1_half", tag="raw")
-            nc.sync.dma_start(out=w1_half[:], in_=w1_rows[:, :, u * half : (u + 1) * half])
-            w1_raw.append(w1_half)
-            if u == 0:
-                for q in range(4):
-                    nc.sync.dma_start(
-                        out=x_scale[32 * q : 32 * q + 16, :].bitcast(I32),
-                        in_=x_scales[0, 4 * q : 4 * q + 4, :].bitcast(I32).rearrange("r (a c) -> a r c", a=4),
-                    )
+            nc.sync.dma_start(out=w1_raw[u][:], in_=w1_rows[:, 2 * u : 2 * u + 2, :])
+        for q in range(4):
+            nc.sync.dma_start(
+                out=x_scale[32 * q : 32 * q + 16, :].bitcast(I32),
+                in_=x_scales[0, 4 * q : 4 * q + 4, :].bitcast(I32).rearrange("r (a c) -> a r c", a=4),
+            )
         x_rows = x_words[0].rearrange("p n t -> p (n t)").bitcast(I32)
         for u in range(2):
             nodes = slice(u * T // 2, (u + 1) * T // 2)
@@ -90,29 +85,27 @@ def tile_picked_wsagecat_max_l_kernel(
         w1_woven = keep.tile([P, PACK, P, PACK], BF16, align_bytes=64)
         w1_codes = keep.tile([P, PACK, P], U32, align_bytes=64)
         w1_scale = keep.tile([P, PACK, P], U8, align_bytes=64)
-        m_half = P // 2
 
         def cast_w1(cast, u, t0, t1):
             cast(
-                out=w1_woven[:, t0:t1, u * m_half : (u + 1) * m_half, :].rearrange("p t m j -> p m j t"),
+                out=w1_woven[:, t0:t1, :, 2 * u : 2 * u + 2].rearrange("p t m j -> p m j t"),
                 in_=w1_raw[u][:].rearrange("p j (m t) -> p m j t", t=PACK)[:, :, :, t0:t1],
             )
 
-        def quantise_w1(t0, t1, m0, m1):
+        def quantise_w1(t0, t1):
             nc.vector.quantize_mx(
-                out=w1_codes[:, t0:t1, m0:m1].rearrange("p t m -> p (t m)").bitcast(FP8X4),
-                scales=w1_scale[:, t0:t1, m0:m1].rearrange("p t m -> p (t m)"),
-                in_=w1_woven[:, t0:t1, m0:m1, :].rearrange("p t m j -> p (t m j)"),
+                out=w1_codes[:, t0:t1, :].rearrange("p t m -> p (t m)").bitcast(FP8X4),
+                scales=w1_scale[:, t0:t1, :].rearrange("p t m -> p (t m)"),
+                in_=w1_woven[:, t0:t1, :, :].rearrange("p t m j -> p (t m j)"),
             )
 
         cast_w1(nc.vector.tensor_copy, 0, 2, 4)
         cast_w1(nc.scalar.copy, 0, 0, 2)
-        quantise_w1(3, 4, 0, m_half)
         cast_w1(nc.vector.tensor_copy, 1, 3, 4)
         cast_w1(nc.scalar.copy, 1, 0, 3)
-        quantise_w1(3, 4, m_half, P)
-        quantise_w1(2, 3, 0, P)
-        quantise_w1(0, 2, 0, P)
+        quantise_w1(3, 4)
+        quantise_w1(2, 3)
+        quantise_w1(0, 2)
 
         def h_piece(t, start, stop, on_vector):
             acc_h = psum.tile([P, BANK], F32, name="acc_h", tag="acc")

@@ -26,9 +26,11 @@ RUN = 64
 GAP = 8
 SPARE = 352
 PIECE = 128
+SHORT, LONG = 64, 256
+PAIR = SHORT + LONG
 
-CHUNKS = ((0, 512), (512, 384), (896, 128))
-BANKS = ((0, 384), (384, 384), (768, 128), (896, 128))
+CHUNKS = ((512, 512), (128, 384), (0, 128))
+BANKS = ((640, 384), (256, 384), (128, 128), (0, 128))
 
 
 def powers_of_two(n, widest):
@@ -102,7 +104,8 @@ def tile_picked_wsagecat_max_l_kernel(
         cast_w1(nc.vector.tensor_copy, 0, 2, 4)
         cast_w1(nc.scalar.copy, 0, 0, 2)
         cast_w1(nc.vector.tensor_copy, 1, 3, 4)
-        cast_w1(nc.scalar.copy, 1, 0, 3)
+        cast_w1(nc.vector.tensor_copy, 1, 2, 3)
+        cast_w1(nc.scalar.copy, 1, 0, 2)
         quantise_w1(3, 4)
         quantise_w1(2, 3)
         quantise_w1(0, 2)
@@ -128,19 +131,20 @@ def tile_picked_wsagecat_max_l_kernel(
                 nc.scalar.activation(dst, acc_h[:, : stop - start], RELU)
 
         (c0, n0), (c1, n1), (c2, n2) = CHUNKS
+        n01 = n0 + n1
         whole = span(T)
         woven_piece = PACK * PIECE
         h_woven1 = 0
-        z_planes1 = h_woven1 + woven_piece
+        z_planes1 = h_woven1 + PACK * LONG
         z_planes2 = z_planes1 + PACK * n1
         z_woven1 = z_planes2 + PACK * n2
         z_woven2 = z_woven1 + PACK * n1
         z_woven0 = z_woven2 + PACK * n2
         h_woven0 = z_woven0 + PACK * n0
-        z_planes0 = h_woven0 + woven_piece
-        first0 = [z_planes0 + PACK * n0 + d * (span(n0) + whole) for d in range(2)]
+        z_planes0 = h_woven0 + PACK * LONG
+        first0 = [z_planes0 + PACK * n0 + d * (span(n0) + 2 * whole) for d in range(2)]
         second0 = [h_woven0, first0[1]]
-        last0 = [z_woven0 + d * woven_piece // 2 for d in range(2)]
+        last0 = [h_woven0 - woven_piece + d * woven_piece // 2 for d in range(2)]
         plane1 = [first0[d] + span(n0) for d in range(2)]
         pitch = [plane1[d] + span(c2) - last0[d] for d in range(2)]
         work = keep.tile([P, last0[1] + PACK * pitch[1]], BF16, align_bytes=64)
@@ -185,6 +189,8 @@ def tile_picked_wsagecat_max_l_kernel(
         def woven(values):
             return values.rearrange("p (c i t) -> p c t i", i=NEAR, t=PACK)
 
+        late = 2 * PIECE
+
         def quantise(codes, scale, first, n, values):
             nc.vector.quantize_mx(
                 out=codes[:, first : first + n].bitcast(FP8X4), scales=scale[:, first : first + n], in_=values
@@ -192,7 +198,7 @@ def tile_picked_wsagecat_max_l_kernel(
 
         edges = (0, QUARTER, 2 * QUARTER, 3 * QUARTER, 3 * QUARTER + QUARTER // 2, T)
         for piece in range(len(edges) - 1):
-            h_piece(3, edges[piece], edges[piece + 1], piece % 2 == 1)
+            h_piece(3, edges[piece], edges[piece + 1], piece == 3)
         gather(3, 0, T)
 
         for t in (2, 1, 0):
@@ -206,8 +212,8 @@ def tile_picked_wsagecat_max_l_kernel(
             nc.scalar.copy(out=woven(values), in_=near(h_planes[:, :, first : first + n]))
 
         def quantise_pair(first, base):
-            for k in (1, 0):
-                quantise(h_codes, h_scale, first + k * PIECE, PIECE, region(base + k * woven_piece, PIECE))
+            quantise(h_codes, h_scale, first + LONG, SHORT, region(base + PACK * LONG, SHORT))
+            quantise(h_codes, h_scale, first, LONG, region(base, LONG))
 
         def z_rows(z_planes, n, t0, planes):
             rows = work[:, z_planes + t0 * n : z_planes + (t0 + planes) * n]
@@ -232,21 +238,22 @@ def tile_picked_wsagecat_max_l_kernel(
                     ADD,
                 )
 
-        def both_parts(tile, start):
-            return (tile[:, start : start + n0], tile[:, start + n0 : start + c2])
+        rest = T - 2 * PAIR
+        excess2 = (h[:, 3 * T + rest : 3 * T + rest + n0], h[:, 3 * T + rest + n0 : 3 * T + rest + n01])
+        excess3a = keep.tile([P, n0], F32)
+        diff3 = [work[:, base : base + 2 * n].bitcast(F32) for base, n in ((h_woven0, n0), (h_woven1, n1))]
+        shared = keep.tile([P, 2 * n01], F32, align_bytes=64)
+        diff2_at = 448
+        excess3b = shared[:, diff2_at + n0 - n1 // 2 : diff2_at + n0 + n1 // 2]
+        diff2 = (shared[:, diff2_at : diff2_at + n0], shared[:, diff2_at + n0 : diff2_at + n01])
+        h_woven2 = shared[:, 2 * BANK - 2 * rest : 2 * BANK].bitcast(BF16)
+        w23_woven = shared[:, 2 * n01 - BANK :].bitcast(BF16)
 
-        diff3 = keep.tile([P, c2], F32)
-        shared = keep.tile([P, 2 * c2], F32, align_bytes=64)
-        excess3_at = 192
-        diff2_at = excess3_at + n0 // 2
-        h_woven2 = shared[:, : 2 * BANK].bitcast(BF16)
-        w23_woven = shared[:, 2 * c2 - BANK :].bitcast(BF16)
-
-        weave_h(0, 2 * PIECE, region(h_woven0, 2 * PIECE))
-        side_max(3, both_parts(diff3, 0), both_parts(shared, excess3_at))
-        weave_h(2 * PIECE, 2 * PIECE, region(h_woven1, 2 * PIECE))
-        side_max(2, both_parts(shared, diff2_at), (h[:, 3 * T : 3 * T + n0], diff3[:, :n1]))
-        weave_h(4 * PIECE, 4 * PIECE, h_woven2)
+        side_max(3, diff3, (excess3a[:], excess3b))
+        weave_h(rest, PAIR, region(h_woven0, PAIR))
+        weave_h(T - PAIR, PAIR, region(h_woven1, PAIR))
+        side_max(2, diff2, excess2)
+        weave_h(0, rest, h_woven2)
         for s in range(2):
             nc.scalar.copy(out=woven(w23_woven[:, s * PACK * N : (s + 1) * PACK * N]), in_=near(w23_raw[:, s]))
 
@@ -255,62 +262,69 @@ def tile_picked_wsagecat_max_l_kernel(
                 z_rows(z_planes, n, 0, planes), runs(0, first, n, planes), runs(1, first, n, planes), MAX
             )
             planes_of_z = region(z_planes, n).rearrange("p (t c) -> p t c", t=PACK)
-            nc.scalar.copy(out=woven(region(z_woven, n)), in_=near(planes_of_z))
+            for start, stop, values in z_woven:
+                nc.scalar.copy(out=woven(values), in_=near(planes_of_z[:, :, start:stop]))
 
         result = keep.tile([P, T], F32)
         result0 = work[:, z_planes1 : z_planes1 + 2 * BANKS[0][1]].bitcast(F32)
 
-        def finish_out(first, pieces, on_vector):
+        def finish_out(first, pieces, on_vector, h_codes):
             acc_o = psum.tile([P, BANK], F32, name="acc_o", tag="acc")
-            n = 0
-            for width in pieces:
-                cols = slice(first + n, first + n + width)
-                for s, (codes, scale) in enumerate(((h_codes, h_scale), (z_codes, z_scale))):
+            n = sum(pieces)
+            for s, (codes, scale) in enumerate(((h_codes, h_scale), (z_codes, z_scale))):
+                start = 0
+                for width in pieces:
+                    cols = slice(first + start, first + start + width)
                     nc.tensor.matmul_mx(
-                        out=acc_o[:, n : n + width],
+                        out=acc_o[:, start : start + width],
                         lhsT=w23_codes[:, s * N : (s + 1) * N].bitcast(FP8X4),
                         lhsT_scale=w23_scale[:, s * N : (s + 1) * N],
                         rhs=codes[:, cols].bitcast(FP8X4),
                         rhs_scale=scale[:, cols],
-                        start=(s == 0),
-                        stop=(s == 1),
+                        start=(s == 0 and start == 0),
+                        stop=(s == 1 and start + width == n),
                     )
-                n = n + width
-            dst = result0 if first == 0 else result[:, first : first + n]
+                    start = start + width
+            dst = result0 if first == BANKS[0][0] else result[:, first : first + n]
             if on_vector:
                 nc.vector.tensor_copy(out=dst, in_=acc_o[:, :n])
             else:
                 nc.scalar.copy(out=dst, in_=acc_o[:, :n])
 
         def store(first, stop):
-            nc.sync.dma_start(out=out[:, first:stop], in_=result0 if first == 0 else result[:, first:stop])
+            nc.sync.dma_start(out=out[:, first:stop], in_=result0 if first == BANKS[0][0] else result[:, first:stop])
 
         def quantise_z(first, start, n, z_woven):
             quantise(z_codes, z_scale, first + start, n, region(z_woven + PACK * start, n))
 
         gather(0, c0, n0)
-        quantise_pair(0, h_woven0)
-        finish_z(c0, n0, 2, z_planes0, z_woven0)
+        quantise_pair(rest, h_woven0)
+        z_piece = keep.tile([P, woven_piece], BF16, tag="slot", align_bytes=64)
+        finish_z(
+            c0, n0, 2, z_planes0, ((PIECE, n0, region(z_woven0 + woven_piece, n0 - PIECE)), (0, PIECE, z_piece[:]))
+        )
 
         gather(0, c1, n1)
-        quantise_pair(2 * PIECE, h_woven1)
-        finish_z(c1, n1, 2, z_planes1, z_woven1)
-        quantise(h_codes, h_scale, 4 * PIECE, 4 * PIECE, h_woven2)
+        quantise_pair(T - PAIR, h_woven1)
+        finish_z(c1, n1, 2, z_planes1, ((0, n1, region(z_woven1, n1)),))
+        quantise(h_codes, h_scale, late, rest - late, h_woven2[:, PACK * late :])
         quantise(w23_codes, w23_scale, 0, 2 * N, w23_woven)
-        quantise_z(c0, 0, PIECE, z_woven0)
+        quantise_z(c0, 3 * PIECE, PIECE, z_woven0)
         quantise_z(c0, PIECE, 2 * PIECE, z_woven0)
 
-        finish_out(0, (256, 128), False)
-        store(0, 384)
+        finish_out(640, (256, 128), False, h_codes)
+        store(640, T)
 
         gather(0, c2, n2)
-        quantise_z(c0, 3 * PIECE, PIECE, z_woven0)
-        finish_z(c2, n2, PACK, z_planes2, z_woven2)
-        for start, width in powers_of_two(n1, QUARTER):
-            quantise_z(c1, start, width, z_woven1)
+        quantise(z_codes, z_scale, c0, PIECE, z_piece[:])
+        finish_z(c2, n2, PACK, z_planes2, ((0, n2, region(z_woven2, n2)),))
+        late_codes = keep.tile([P, late], U32, tag="slot", align_bytes=64)
+        quantise(late_codes, h_scale, 0, late, h_woven2[:, : PACK * late])
+        quantise_z(c1, PIECE, 2 * PIECE, z_woven1)
+        quantise_z(c1, 0, PIECE, z_woven1)
         quantise_z(c2, 0, n2, z_woven2)
-        finish_out(384, (128, 256), False)
-        store(384, 768)
-        finish_out(768, (128,), False)
-        finish_out(896, (128,), True)
-        store(768, T)
+        finish_out(256, (256, 128), False, h_codes)
+        store(256, 640)
+        finish_out(128, (128,), False, late_codes)
+        finish_out(0, (128,), True, late_codes)
+        store(0, 256)

@@ -270,10 +270,9 @@ def tile_picked_wsagecat_max_l_kernel(
 
         def finish_out(first, pieces, on_vector, h_codes):
             acc_o = psum.tile([P, BANK], F32, name="acc_o", tag="acc")
-            n = sum(pieces)
+            n = sum(width for start, width in pieces)
             for s, (codes, scale) in enumerate(((h_codes, h_scale), (z_codes, z_scale))):
-                start = 0
-                for width in pieces:
+                for start, width in pieces:
                     cols = slice(first + start, first + start + width)
                     nc.tensor.matmul_mx(
                         out=acc_o[:, start : start + width],
@@ -281,10 +280,9 @@ def tile_picked_wsagecat_max_l_kernel(
                         lhsT_scale=w23_scale[:, s * N : (s + 1) * N],
                         rhs=codes[:, cols].bitcast(FP8X4),
                         rhs_scale=scale[:, cols],
-                        start=(s == 0 and start == 0),
-                        stop=(s == 1 and start + width == n),
+                        start=(s == 0 and start == pieces[0][0]),
+                        stop=(s == 1 and start == pieces[-1][0]),
                     )
-                    start = start + width
             dst = result0 if first == BANKS[0][0] else result[:, first : first + n]
             if on_vector:
                 nc.vector.tensor_copy(out=dst, in_=acc_o[:, :n])
@@ -312,7 +310,7 @@ def tile_picked_wsagecat_max_l_kernel(
         quantise_z(c0, 3 * PIECE, PIECE, z_woven0)
         quantise_z(c0, PIECE, 2 * PIECE, z_woven0)
 
-        finish_out(640, (256, 128), False, h_codes)
+        finish_out(640, ((256, 128), (0, 256)), False, h_codes)
         store(640, T)
 
         gather(0, c2, n2)
@@ -323,8 +321,8 @@ def tile_picked_wsagecat_max_l_kernel(
         quantise_z(c1, PIECE, 2 * PIECE, z_woven1)
         quantise_z(c1, 0, PIECE, z_woven1)
         quantise_z(c2, 0, n2, z_woven2)
-        finish_out(256, (256, 128), False, h_codes)
+        finish_out(256, ((256, 128), (0, 256)), False, h_codes)
         store(256, 640)
-        finish_out(128, (128,), False, late_codes)
-        finish_out(0, (128,), True, late_codes)
+        finish_out(128, ((0, 128),), False, late_codes)
+        finish_out(0, ((0, 128),), True, late_codes)
         store(0, 256)

@@ -75,8 +75,7 @@ def tile_picked_wsagecat_max_l_kernel(
                 in_=x_scales[0, 4 * q : 4 * q + 4, :].bitcast(I32).rearrange("r (a c) -> a r c", a=4),
             )
         x_rows = x_words[0].rearrange("p n t -> p (n t)").bitcast(I32)
-        for u in range(2):
-            nodes = slice(u * T // 2, (u + 1) * T // 2)
+        for nodes in (slice(0, T // 2), slice(T // 2, T - QUARTER), slice(T - QUARTER, T)):
             nc.sync.dma_start(out=x_codes[:, nodes].bitcast(I32), in_=x_rows[:, nodes])
         nc.sync.dma_start(lists[0][:], pos1)
         nc.sync.dma_start(lists[1][:], pos2)

@@ -24,29 +24,8 @@ QUARTER = T // 4
 NEAR = 4
 RUN = 64
 GAP = 8
-SPARE = 352
-PIECE = 128
-SHORT, LONG = 64, 256
-PAIR = SHORT + LONG
-
-CHUNKS = ((512, 512), (128, 384), (0, 128))
-BANKS = ((640, 384), (256, 384), (128, 128), (0, 128))
-
-
-def powers_of_two(n, widest):
-    cut = []
-    start = 0
-    while start < n:
-        width = widest
-        while width > n - start:
-            width = width // 2
-        cut.append((start, width))
-        start = start + width
-    return cut
-
-
-def span(n):
-    return n // RUN * (RUN + GAP)
+HALF = T // 2
+SPAN = HALF // RUN * (RUN + GAP)
 
 
 def tile_picked_wsagecat_max_l_kernel(
@@ -55,15 +34,17 @@ def tile_picked_wsagecat_max_l_kernel(
     nc = tc.nc
     with ExitStack() as ctx:
         keep = ctx.enter_context(tc.tile_pool(name="keep", bufs=1))
-        psum = ctx.enter_context(tc.psum_pool(name="psum", bufs=8))
+        psum = ctx.enter_context(tc.psum_pool(name="psum", bufs=1))
+
+        def bank(b, role):
+            return psum.tile([P, BANK], F32, name=role, tag="bank%d" % b)
 
         lists = [keep.tile([P, T // 16], U16, name="list%d" % d) for d in range(2)]
         x_codes = keep.tile([P, T], U32, align_bytes=64)
         x_scale = keep.tile([P, QUARTER], U8, align_bytes=64)
-        h = keep.tile([P, PACK * T + SPARE], F32, align_bytes=64)
+        h = keep.tile([P, PACK * T], F32, align_bytes=64)
 
         nc.vector.memset(x_scale[:].bitcast(I32), 0)
-        nc.vector.memset(h[:, PACK * T :], 0.0)
 
         w1_rows = w1.rearrange("(p j) c -> p j c", j=PACK)
         w1_raw = [keep.tile([P, 2, H], F32, name="w1_raw%d" % u) for u in range(2)]
@@ -79,12 +60,12 @@ def tile_picked_wsagecat_max_l_kernel(
             nc.sync.dma_start(out=x_codes[:, nodes].bitcast(I32), in_=x_rows[:, nodes])
         nc.sync.dma_start(lists[0][:], pos1)
         nc.sync.dma_start(lists[1][:], pos2)
-        w23_raw = keep.tile([P, 2, PACK, N], F32)
+        w23_raw = keep.tile([P, 2, PACK, N], F32, tag="raw", align_bytes=64)
         for s, w in enumerate((w2, w3)):
             nc.sync.dma_start(out=w23_raw[:, s], in_=w.rearrange("(p j) n -> p j n", j=PACK))
 
         w1_woven = keep.tile([P, PACK, P, PACK], BF16, align_bytes=64)
-        w1_codes = keep.tile([P, PACK, P], U32, align_bytes=64)
+        w1_codes = keep.tile([P, PACK, P], U32, tag="slot", align_bytes=64)
         w1_scale = keep.tile([P, PACK, P], U8, align_bytes=64)
 
         def cast_w1(cast, u, t0, t1):
@@ -109,9 +90,9 @@ def tile_picked_wsagecat_max_l_kernel(
         quantise_w1(2, 3)
         quantise_w1(0, 2)
 
-        def h_piece(t, start, stop, on_vector):
-            acc_h = psum.tile([P, BANK], F32, name="acc_h", tag="acc")
-            for b0 in range(start, stop, QUARTER):
+        def project(b, t, start, stop):
+            acc_h = bank(b, "acc_h")
+            for b0 in reversed(range(start, stop, QUARTER)):
                 b1 = min(b0 + QUARTER, stop)
                 a, within = divmod(b0, QUARTER)
                 nc.tensor.matmul_mx(
@@ -123,205 +104,176 @@ def tile_picked_wsagecat_max_l_kernel(
                     start=True,
                     stop=True,
                 )
-            dst = h[:, t * T + start : t * T + stop]
-            if on_vector:
-                nc.vector.tensor_scalar_max(dst, acc_h[:, : stop - start], 0.0)
-            else:
-                nc.scalar.activation(dst, acc_h[:, : stop - start], RELU)
+            return acc_h
 
-        (c0, n0), (c1, n1), (c2, n2) = CHUNKS
-        n01 = n0 + n1
-        whole = span(T)
-        woven_piece = PACK * PIECE
-        h_woven1 = 0
-        z_planes1 = h_woven1 + PACK * LONG
-        z_planes2 = z_planes1 + PACK * n1
-        z_woven1 = z_planes2 + PACK * n2
-        z_woven2 = z_woven1 + PACK * n1
-        z_woven0 = z_woven2 + PACK * n2
-        h_woven0 = z_woven0 + PACK * n0
-        z_planes0 = h_woven0 + PACK * LONG
-        first0 = [z_planes0 + PACK * n0 + d * (span(n0) + 2 * whole) for d in range(2)]
-        second0 = [h_woven0, first0[1]]
-        last0 = [h_woven0 - woven_piece + d * woven_piece // 2 for d in range(2)]
-        plane1 = [first0[d] + span(n0) for d in range(2)]
-        pitch = [plane1[d] + span(c2) - last0[d] for d in range(2)]
-        work = keep.tile([P, last0[1] + PACK * pitch[1]], BF16, align_bytes=64)
+        def plane(t, start, stop):
+            return h[:, t * T + start : t * T + stop]
+
+        edges = (0, QUARTER, 2 * QUARTER, 3 * QUARTER, 3 * QUARTER + QUARTER // 2, T)
+        for piece, b in enumerate((2, 3, 4, 5, 0)):
+            start, stop = edges[piece], edges[piece + 1]
+            acc_h = project(b, 3, start, stop)
+            if piece == 3:
+                nc.vector.tensor_scalar_max(plane(3, start, stop), acc_h[:, : stop - start], 0.0)
+            else:
+                nc.scalar.activation(plane(3, start, stop), acc_h[:, : stop - start], RELU)
+        for start, b in ((BANK, 1), (0, 0)):
+            acc_h = project(b, 2, start, start + BANK)
+            nc.scalar.activation(plane(2, start, start + BANK), acc_h[:], RELU)
+        for t, b in ((1, 6), (0, 7)):
+            acc_h = project(b, t, BANK, T)
+            nc.scalar.activation(plane(t, BANK, T), acc_h[:], RELU)
+        lower = [(t, project(b, t, 0, BANK)) for t, b in ((1, 1), (0, 0))]
+        for start, stop in ((0, BANK - P), (BANK - P, BANK)):
+            for t, acc_h in lower:
+                nc.scalar.activation(plane(t, start, stop), acc_h[:, start:stop], RELU)
+
+        def near(rows):
+            return rows.rearrange("p t (c i) -> p c t i", i=NEAR)
+
+        def woven(values):
+            return values.rearrange("p (c i t) -> p c t i", i=NEAR, t=PACK)
+
+        w23_woven = keep.tile([P, 2 * PACK * N], BF16, tag="slot", align_bytes=64)
+        h_woven_upper = keep.tile([P, PACK * HALF], BF16, align_bytes=64)
+        h_planes = h[:].rearrange("p (t c) -> p t c", t=PACK)
+        picked = [None, keep.tile([P, 2 * PACK * SPAN], BF16, name="picked_upper", align_bytes=64)]
+
+        h_woven = (picked[1][:, HALF : HALF + PACK * HALF], h_woven_upper[:])
+
+        def runs(d, half, t0, t1):
+            base = (d * PACK + t0) * SPAN
+            rows = picked[half][:, base : base + (t1 - t0) * SPAN]
+            return rows.rearrange("p (t u c) -> p t u c", t=t1 - t0, c=RUN + GAP)[:, :, :, :RUN]
+
+        def gather(t, half):
+            for d in range(2):
+                nc.vector.tensor_copy(
+                    runs(d, half, t, t + 1)[:, 0],
+                    plane(t, 0, T).indirect(lists[d][:, half * HALF // 16 : (half + 1) * HALF // 16]),
+                )
+
+        scratch = keep.tile([P, 11 * HALF], F32, align_bytes=64)
+
+        def row(r):
+            return scratch[:, r * HALF : (r + 1) * HALF]
+
+        diff = {(3, 1): row(0), (2, 1): row(1), (1, 1): row(4), (0, 1): row(5), (3, 0): row(7)[:, :QUARTER]}
+        excess = {(3, 1): row(4), (2, 1): row(5), (1, 1): row(6), (0, 1): row(7), (3, 0): row(2)[:, :QUARTER]}
+        z_upper = keep.tile([P, PACK * HALF], BF16, align_bytes=64)
+        z_lower = scratch[:, 8 * HALF : 10 * HALF].bitcast(BF16)
+        per = QUARTER // RUN
+
+        def in_runs(values):
+            return values.rearrange("p (u c) -> p u c", c=RUN)
+
+        def side(d, t, half):
+            return runs(d, half, t, t + 1)[:, 0, : (1 + half) * per, :]
+
+        def subtract(t, half):
+            nc.gpsimd.tensor_tensor(in_runs(diff[t, half]), side(0, t, half), side(1, t, half), SUB)
+
+        def relu(t, half):
+            nc.scalar.activation(excess[t, half], diff[t, half], RELU)
+
+        def add_back(t, half):
+            dst = (z_lower, z_upper)[half][:, t * HALF : t * HALF + (1 + half) * QUARTER]
+            nc.gpsimd.tensor_tensor(in_runs(dst), in_runs(excess[t, half]), side(1, t, half), ADD)
+
+        def weave_h(j):
+            nc.scalar.copy(
+                out=woven(h_woven[j // 2][:, j % 2 * T : (j % 2 + 1) * T]),
+                in_=near(h_planes[:, :, j * QUARTER : (j + 1) * QUARTER]),
+            )
+
+        for t in (3, 2, 1, 0):
+            gather(t, 1)
+        subtract(3, 1)
+        relu(3, 1)
+        for s in range(2):
+            nc.scalar.copy(out=woven(w23_woven[:, s * PACK * N : (s + 1) * PACK * N]), in_=near(w23_raw[:, s]))
+        picked[0] = keep.tile([P, 2 * PACK * SPAN], BF16, name="picked_lower", tag="raw", align_bytes=64)
+        for t in (3, 2, 1, 0):
+            gather(t, 0)
+        subtract(2, 1)
+        relu(2, 1)
+        add_back(3, 1)
+        weave_h(3)
+        weave_h(2)
+        subtract(1, 1)
+        relu(1, 1)
+        add_back(2, 1)
+        subtract(0, 1)
+        relu(0, 1)
+        weave_h(0)
+        add_back(1, 1)
+        add_back(0, 1)
+        subtract(3, 0)
+        woven_upper = keep.tile([P, PACK * HALF], BF16, align_bytes=64)
+        woven_lower = z_upper
+
+        def weave_z(planes, dst, first, n):
+            rows = planes.rearrange("p (t c) -> p t c", t=PACK)[:, :, first : first + n]
+            nc.scalar.copy(out=woven(dst[:, PACK * first : PACK * (first + n)]), in_=near(rows))
+
+        weave_z(z_upper[:], woven_upper, 0, QUARTER)
+        relu(3, 0)
+        add_back(3, 0)
+        weave_z(z_upper[:], woven_upper, QUARTER, QUARTER)
+        weave_h(1)
+
+        def largest(planes, first, n):
+            within = slice(first // RUN, (first + n) // RUN)
+            nc.vector.tensor_tensor(
+                z_lower.rearrange("p (t u c) -> p t u c", t=PACK, c=RUN)[:, :planes, within, :],
+                runs(0, 0, 0, planes)[:, :, within, :],
+                runs(1, 0, 0, planes)[:, :, within, :],
+                MAX,
+            )
+            weave_z(z_lower, woven_lower, first, n)
+
         h_codes = keep.tile([P, T], U32, align_bytes=64)
         h_scale = keep.tile([P, T], U8, align_bytes=64)
         z_codes = keep.tile([P, T], U32, align_bytes=64)
         z_scale = keep.tile([P, T], U8, align_bytes=64)
         w23_codes = keep.tile([P, 2 * N], U32, align_bytes=64)
         w23_scale = keep.tile([P, 2 * N], U8, align_bytes=64)
+        result = keep.tile([P, HALF], F32)
+        result_upper = scratch[:, 8 * HALF - 3 * P : 8 * HALF + P]
 
-        def place(t, d, first):
-            if t == 0 and first == c0:
-                return first0[d]
-            if t == 0 and first == c1:
-                return second0[d]
-            return plane1[d] + (t - 1) * pitch[d] + span(first)
-
-        def runs(d, first, n, planes):
-            base = place(0, d, first)
-            step = place(1, d, first) - base
-            block = work[:, base : base + planes * step].rearrange("p (t r) -> p t r", t=planes)
-            return block[:, :, : span(n)].rearrange("p t (u c) -> p t u c", c=RUN + GAP)[:, :, :, :RUN]
-
-        def one_plane(t, d, first, n):
-            base = place(t, d, first)
-            return work[:, base : base + span(n)].rearrange("p (u c) -> p u c", c=RUN + GAP)[:, :, :RUN]
-
-        def gather(t, first, n):
-            window = T + SPARE if n == T else T
-            for d in range(2):
-                nc.vector.tensor_copy(
-                    one_plane(t, d, first, n),
-                    h[:, t * T : t * T + window].indirect(lists[d][:, first // 16 : (first + n) // 16]),
-                )
-
-        def near(rows):
-            return rows.rearrange("p t (c i) -> p c t i", i=NEAR)
-
-        def region(base, n):
-            return work[:, base : base + PACK * n]
-
-        def woven(values):
-            return values.rearrange("p (c i t) -> p c t i", i=NEAR, t=PACK)
-
-        late = 2 * PIECE
-
-        def quantise(codes, scale, first, n, values):
+        def quantise(codes, scale, first, n, source):
             nc.vector.quantize_mx(
-                out=codes[:, first : first + n].bitcast(FP8X4), scales=scale[:, first : first + n], in_=values
+                out=codes[:, first : first + n].bitcast(FP8X4), scales=scale[:, first : first + n], in_=source
             )
 
-        edges = (0, QUARTER, 2 * QUARTER, 3 * QUARTER, 3 * QUARTER + QUARTER // 2, T)
-        for piece in range(len(edges) - 1):
-            h_piece(3, edges[piece], edges[piece + 1], piece == 3)
-        gather(3, 0, T)
-
-        for t in (2, 1, 0):
-            h_piece(t, 0, BANK, False)
-            h_piece(t, BANK, T, False)
-        for t in (2, 1):
-            gather(t, 0, T)
-
-        def weave_h(first, n, values):
-            h_planes = h[:, : PACK * T].rearrange("p (t c) -> p t c", t=PACK)
-            nc.scalar.copy(out=woven(values), in_=near(h_planes[:, :, first : first + n]))
-
-        def quantise_pair(first, base):
-            quantise(h_codes, h_scale, first + LONG, SHORT, region(base + PACK * LONG, SHORT))
-            quantise(h_codes, h_scale, first, LONG, region(base, LONG))
-
-        def z_rows(z_planes, n, t0, planes):
-            rows = work[:, z_planes + t0 * n : z_planes + (t0 + planes) * n]
-            return rows.rearrange("p (t u c) -> p t u c", t=planes, c=RUN)
-
-        parts = ((c0, n0, z_planes0), (c1, n1, z_planes1))
-
-        def side_max(t, diffs, excesses):
-            for (first, n, z_planes), diff in zip(parts, diffs):
-                nc.gpsimd.tensor_tensor(
-                    diff.rearrange("p (u c) -> p u c", c=RUN),
-                    one_plane(t, 0, first, n),
-                    one_plane(t, 1, first, n),
-                    SUB,
+        def finish(b, base, total, z_pieces, copy, dst):
+            acc_o = bank(b, "acc_o")
+            steps = [(0, base, total)] + [(1, first, n) for first, n in z_pieces]
+            for i, (s, first, n) in enumerate(steps):
+                codes, scale = ((h_codes, h_scale), (z_codes, z_scale))[s]
+                nc.tensor.matmul_mx(
+                    out=acc_o[:, first - base : first - base + n],
+                    lhsT=w23_codes[:, s * N : (s + 1) * N].bitcast(FP8X4),
+                    lhsT_scale=w23_scale[:, s * N : (s + 1) * N],
+                    rhs=codes[:, first : first + n].bitcast(FP8X4),
+                    rhs_scale=scale[:, first : first + n],
+                    start=(i == 0),
+                    stop=(i == len(steps) - 1),
                 )
-            for (first, n, z_planes), diff, excess in zip(parts, diffs, excesses):
-                nc.scalar.activation(excess, diff, RELU)
-                nc.gpsimd.tensor_tensor(
-                    z_rows(z_planes, n, t, 1)[:, 0, :, :],
-                    excess.rearrange("p (u c) -> p u c", c=RUN),
-                    one_plane(t, 1, first, n),
-                    ADD,
-                )
+            copy(out=dst, in_=acc_o[:, :total])
 
-        rest = T - 2 * PAIR
-        excess2 = (h[:, 3 * T + rest : 3 * T + rest + n0], h[:, 3 * T + rest + n0 : 3 * T + rest + n01])
-        excess3a = keep.tile([P, n0], F32)
-        diff3 = [work[:, base : base + 2 * n].bitcast(F32) for base, n in ((h_woven0, n0), (h_woven1, n1))]
-        shared = keep.tile([P, 2 * n01], F32, align_bytes=64)
-        diff2_at = 448
-        excess3b = shared[:, diff2_at + n0 - n1 // 2 : diff2_at + n0 + n1 // 2]
-        diff2 = (shared[:, diff2_at : diff2_at + n0], shared[:, diff2_at + n0 : diff2_at + n01])
-        h_woven2 = shared[:, 2 * BANK - 2 * rest : 2 * BANK].bitcast(BF16)
-        w23_woven = shared[:, 2 * n01 - BANK :].bitcast(BF16)
-
-        side_max(3, diff3, (excess3a[:], excess3b))
-        weave_h(rest, PAIR, region(h_woven0, PAIR))
-        weave_h(T - PAIR, PAIR, region(h_woven1, PAIR))
-        side_max(2, diff2, excess2)
-        weave_h(0, rest, h_woven2)
-        for s in range(2):
-            nc.scalar.copy(out=woven(w23_woven[:, s * PACK * N : (s + 1) * PACK * N]), in_=near(w23_raw[:, s]))
-
-        def finish_z(first, n, planes, z_planes, z_woven):
-            nc.vector.tensor_tensor(
-                z_rows(z_planes, n, 0, planes), runs(0, first, n, planes), runs(1, first, n, planes), MAX
-            )
-            planes_of_z = region(z_planes, n).rearrange("p (t c) -> p t c", t=PACK)
-            for start, stop, values in z_woven:
-                nc.scalar.copy(out=woven(values), in_=near(planes_of_z[:, :, start:stop]))
-
-        result = keep.tile([P, T], F32)
-        result0 = work[:, z_planes1 : z_planes1 + 2 * BANKS[0][1]].bitcast(F32)
-
-        def finish_out(first, pieces, on_vector, h_codes):
-            acc_o = psum.tile([P, BANK], F32, name="acc_o", tag="acc")
-            n = sum(width for start, width in pieces)
-            for s, (codes, scale) in enumerate(((h_codes, h_scale), (z_codes, z_scale))):
-                for start, width in pieces:
-                    cols = slice(first + start, first + start + width)
-                    nc.tensor.matmul_mx(
-                        out=acc_o[:, start : start + width],
-                        lhsT=w23_codes[:, s * N : (s + 1) * N].bitcast(FP8X4),
-                        lhsT_scale=w23_scale[:, s * N : (s + 1) * N],
-                        rhs=codes[:, cols].bitcast(FP8X4),
-                        rhs_scale=scale[:, cols],
-                        start=(s == 0 and start == pieces[0][0]),
-                        stop=(s == 1 and start == pieces[-1][0]),
-                    )
-            dst = result0 if first == BANKS[0][0] else result[:, first : first + n]
-            if on_vector:
-                nc.vector.tensor_copy(out=dst, in_=acc_o[:, :n])
-            else:
-                nc.scalar.copy(out=dst, in_=acc_o[:, :n])
-
-        def store(first, stop):
-            nc.sync.dma_start(out=out[:, first:stop], in_=result0 if first == BANKS[0][0] else result[:, first:stop])
-
-        def quantise_z(first, start, n, z_woven):
-            quantise(z_codes, z_scale, first + start, n, region(z_woven + PACK * start, n))
-
-        gather(0, c0, n0)
-        quantise_pair(rest, h_woven0)
-        z_piece = keep.tile([P, woven_piece], BF16, tag="slot", align_bytes=64)
-        finish_z(
-            c0, n0, 2, z_planes0, ((PIECE, n0, region(z_woven0 + woven_piece, n0 - PIECE)), (0, PIECE, z_piece[:]))
-        )
-
-        gather(0, c1, n1)
-        quantise_pair(T - PAIR, h_woven1)
-        finish_z(c1, n1, 2, z_planes1, ((0, n1, region(z_woven1, n1)),))
-        quantise(h_codes, h_scale, late, rest - late, h_woven2[:, PACK * late :])
-        quantise(w23_codes, w23_scale, 0, 2 * N, w23_woven)
-        quantise_z(c0, 3 * PIECE, PIECE, z_woven0)
-        quantise_z(c0, PIECE, 2 * PIECE, z_woven0)
-
-        finish_out(640, ((256, 128), (0, 256)), False, h_codes)
-        store(640, T)
-
-        gather(0, c2, n2)
-        quantise(z_codes, z_scale, c0, PIECE, z_piece[:])
-        finish_z(c2, n2, PACK, z_planes2, ((0, n2, region(z_woven2, n2)),))
-        late_codes = keep.tile([P, late], U32, tag="slot", align_bytes=64)
-        quantise(late_codes, h_scale, 0, late, h_woven2[:, : PACK * late])
-        quantise_z(c1, PIECE, 2 * PIECE, z_woven1)
-        quantise_z(c1, 0, PIECE, z_woven1)
-        quantise_z(c2, 0, n2, z_woven2)
-        finish_out(256, ((256, 128), (0, 256)), False, h_codes)
-        store(256, 640)
-        finish_out(128, ((0, 128),), False, late_codes)
-        finish_out(0, ((0, 128),), True, late_codes)
-        store(0, 256)
+        quantise(w23_codes, w23_scale, 0, 2 * N, w23_woven[:])
+        largest(3, 0, P)
+        largest(3, P, P)
+        largest(4, 2 * P, 2 * P)
+        quantise(h_codes, h_scale, HALF, HALF, h_woven[1])
+        quantise(z_codes, z_scale, HALF, HALF, woven_upper[:])
+        finish(2, HALF, HALF, ((HALF, HALF),), nc.scalar.copy, result_upper)
+        nc.sync.dma_start(out=out[:, HALF:], in_=result_upper)
+        quantise(h_codes, h_scale, 0, HALF, h_woven[0])
+        for first, n in ((0, 2 * P), (2 * P, P), (3 * P, P)):
+            quantise(z_codes, z_scale, first, n, woven_lower[:, PACK * first : PACK * (first + n)])
+        finish(3, 0, 2 * P, ((0, 2 * P),), nc.scalar.copy, result[:, : 2 * P])
+        nc.sync.dma_start(out=out[:, : 2 * P], in_=result[:, : 2 * P])
+        finish(4, 2 * P, 2 * P, ((2 * P, P), (3 * P, P)), nc.vector.tensor_copy, result[:, 2 * P :])
+        nc.sync.dma_start(out=out[:, 2 * P : HALF], in_=result[:, 2 * P :])

@@ -135,25 +135,27 @@ def tile_picked_wsagecat_max_l_kernel(
             return values.rearrange("p (c i t) -> p c t i", i=NEAR, t=PACK)
 
         w23_woven = keep.tile([P, 2 * PACK * N], BF16, tag="slot", align_bytes=64)
-        h_woven_upper = keep.tile([P, PACK * HALF], BF16, align_bytes=64)
+        h_woven = [keep.tile([P, PACK * HALF], BF16, name="h_woven%d" % half, align_bytes=64) for half in range(2)]
         h_planes = h[:].rearrange("p (t c) -> p t c", t=PACK)
         picked = [None, keep.tile([P, 2 * PACK * SPAN], BF16, name="picked_upper", align_bytes=64)]
-
-        h_woven = (picked[1][:, HALF : HALF + PACK * HALF], h_woven_upper[:])
 
         def runs(d, half, t0, t1):
             base = (d * PACK + t0) * SPAN
             rows = picked[half][:, base : base + (t1 - t0) * SPAN]
             return rows.rearrange("p (t u c) -> p t u c", t=t1 - t0, c=RUN + GAP)[:, :, :, :RUN]
 
+        def gather_part(t, half, d, first, n):
+            entry = half * HALF + first
+            nc.vector.tensor_copy(
+                runs(d, half, t, t + 1)[:, 0, first // RUN : (first + n) // RUN, :],
+                plane(t, 0, T).indirect(lists[d][:, entry // 16 : (entry + n) // 16]),
+            )
+
         def gather(t, half):
             for d in range(2):
-                nc.vector.tensor_copy(
-                    runs(d, half, t, t + 1)[:, 0],
-                    plane(t, 0, T).indirect(lists[d][:, half * HALF // 16 : (half + 1) * HALF // 16]),
-                )
+                gather_part(t, half, d, 0, HALF)
 
-        scratch = keep.tile([P, 11 * HALF], F32, align_bytes=64)
+        scratch = keep.tile([P, 8 * HALF], F32, align_bytes=64)
 
         def row(r):
             return scratch[:, r * HALF : (r + 1) * HALF]
@@ -161,7 +163,10 @@ def tile_picked_wsagecat_max_l_kernel(
         diff = {(3, 1): row(0), (2, 1): row(1), (1, 1): row(4), (0, 1): row(5), (3, 0): row(7)[:, :QUARTER]}
         excess = {(3, 1): row(4), (2, 1): row(5), (1, 1): row(6), (0, 1): row(7), (3, 0): row(2)[:, :QUARTER]}
         z_upper = keep.tile([P, PACK * HALF], BF16, align_bytes=64)
-        z_lower = scratch[:, 8 * HALF : 10 * HALF].bitcast(BF16)
+        z_lower = [
+            keep.tile([P, PACK * QUARTER], BF16, name="z_lower0", tag="late", align_bytes=64),
+            keep.tile([P, PACK * QUARTER], BF16, name="z_lower1", align_bytes=64),
+        ]
         per = QUARTER // RUN
 
         def in_runs(values):
@@ -177,7 +182,8 @@ def tile_picked_wsagecat_max_l_kernel(
             nc.scalar.activation(excess[t, half], diff[t, half], RELU)
 
         def add_back(t, half):
-            dst = (z_lower, z_upper)[half][:, t * HALF : t * HALF + (1 + half) * QUARTER]
+            n = (1 + half) * QUARTER
+            dst = (z_lower[0], z_upper)[half][:, t * n : (t + 1) * n]
             nc.gpsimd.tensor_tensor(in_runs(dst), in_runs(excess[t, half]), side(1, t, half), ADD)
 
         def weave_h(j):
@@ -193,8 +199,11 @@ def tile_picked_wsagecat_max_l_kernel(
         for s in range(2):
             nc.scalar.copy(out=woven(w23_woven[:, s * PACK * N : (s + 1) * PACK * N]), in_=near(w23_raw[:, s]))
         picked[0] = keep.tile([P, 2 * PACK * SPAN], BF16, name="picked_lower", tag="raw", align_bytes=64)
-        for t in (3, 2, 1, 0):
+        for t in (3, 2, 1):
             gather(t, 0)
+        gather_part(0, 0, 0, 0, HALF)
+        gather_part(0, 0, 1, 0, QUARTER)
+        gather_part(0, 0, 1, QUARTER, QUARTER)
         subtract(2, 1)
         relu(2, 1)
         add_back(3, 1)
@@ -203,9 +212,10 @@ def tile_picked_wsagecat_max_l_kernel(
         subtract(1, 1)
         relu(1, 1)
         add_back(2, 1)
+        weave_h(1)
+        weave_h(0)
         subtract(0, 1)
         relu(0, 1)
-        weave_h(0)
         add_back(1, 1)
         add_back(0, 1)
         subtract(3, 0)
@@ -220,17 +230,16 @@ def tile_picked_wsagecat_max_l_kernel(
         relu(3, 0)
         add_back(3, 0)
         weave_z(z_upper[:], woven_upper, QUARTER, QUARTER)
-        weave_h(1)
 
-        def largest(planes, first, n):
-            within = slice(first // RUN, (first + n) // RUN)
+        def largest(planes, j):
+            within = slice(j * per, (j + 1) * per)
             nc.vector.tensor_tensor(
-                z_lower.rearrange("p (t u c) -> p t u c", t=PACK, c=RUN)[:, :planes, within, :],
+                z_lower[j][:].rearrange("p (t u c) -> p t u c", t=PACK, c=RUN)[:, :planes],
                 runs(0, 0, 0, planes)[:, :, within, :],
                 runs(1, 0, 0, planes)[:, :, within, :],
                 MAX,
             )
-            weave_z(z_lower, woven_lower, first, n)
+            weave_z(z_lower[j][:], woven_lower[:, j * T : (j + 1) * T], 0, QUARTER)
 
         h_codes = keep.tile([P, T], U32, align_bytes=64)
         h_scale = keep.tile([P, T], U8, align_bytes=64)
@@ -238,15 +247,14 @@ def tile_picked_wsagecat_max_l_kernel(
         z_scale = keep.tile([P, T], U8, align_bytes=64)
         w23_codes = keep.tile([P, 2 * N], U32, align_bytes=64)
         w23_scale = keep.tile([P, 2 * N], U8, align_bytes=64)
-        result = keep.tile([P, HALF], F32)
-        result_upper = scratch[:, 8 * HALF - 3 * P : 8 * HALF + P]
+        result = keep.tile([P, T], F32)
 
         def quantise(codes, scale, first, n, source):
             nc.vector.quantize_mx(
                 out=codes[:, first : first + n].bitcast(FP8X4), scales=scale[:, first : first + n], in_=source
             )
 
-        def finish(b, base, total, z_pieces, copy, dst):
+        def finish(b, base, total, z_pieces, copy, h_codes):
             acc_o = bank(b, "acc_o")
             steps = [(0, base, total)] + [(1, first, n) for first, n in z_pieces]
             for i, (s, first, n) in enumerate(steps):
@@ -260,20 +268,18 @@ def tile_picked_wsagecat_max_l_kernel(
                     start=(i == 0),
                     stop=(i == len(steps) - 1),
                 )
-            copy(out=dst, in_=acc_o[:, :total])
+            copy(out=result[:, base : base + total], in_=acc_o[:, :total])
+            nc.sync.dma_start(out=out[:, base : base + total], in_=result[:, base : base + total])
 
+        largest(3, 0)
+        largest(4, 1)
         quantise(w23_codes, w23_scale, 0, 2 * N, w23_woven[:])
-        largest(3, 0, P)
-        largest(3, P, P)
-        largest(4, 2 * P, 2 * P)
-        quantise(h_codes, h_scale, HALF, HALF, h_woven[1])
+        quantise(h_codes, h_scale, HALF, HALF, h_woven[1][:])
         quantise(z_codes, z_scale, HALF, HALF, woven_upper[:])
-        finish(2, HALF, HALF, ((HALF, HALF),), nc.scalar.copy, result_upper)
-        nc.sync.dma_start(out=out[:, HALF:], in_=result_upper)
-        quantise(h_codes, h_scale, 0, HALF, h_woven[0])
+        finish(2, HALF, HALF, ((HALF, HALF),), nc.scalar.copy, h_codes)
+        late_codes = keep.tile([P, HALF], U32, tag="late", align_bytes=64)
+        quantise(late_codes, h_scale, 0, HALF, h_woven[0][:])
         for first, n in ((0, 2 * P), (2 * P, P), (3 * P, P)):
             quantise(z_codes, z_scale, first, n, woven_lower[:, PACK * first : PACK * (first + n)])
-        finish(3, 0, 2 * P, ((0, 2 * P),), nc.scalar.copy, result[:, : 2 * P])
-        nc.sync.dma_start(out=out[:, : 2 * P], in_=result[:, : 2 * P])
-        finish(4, 2 * P, 2 * P, ((2 * P, P), (3 * P, P)), nc.vector.tensor_copy, result[:, 2 * P :])
-        nc.sync.dma_start(out=out[:, 2 * P : HALF], in_=result[:, 2 * P :])
+        finish(3, 0, 2 * P, ((0, 2 * P),), nc.scalar.copy, late_codes)
+        finish(4, 2 * P, 2 * P, ((2 * P, P), (3 * P, P)), nc.vector.tensor_copy, late_codes)

@@ -160,7 +160,7 @@ def tile_picked_wsagecat_max_l_kernel(
         def row(r):
             return scratch[:, r * HALF : (r + 1) * HALF]
 
-        diff = {(3, 1): row(0), (2, 1): row(1), (1, 1): row(4), (0, 1): row(5), (3, 0): row(7)[:, :QUARTER]}
+        diff = {(3, 1): row(0), (2, 1): row(1), (1, 1): row(4), (0, 1): row(5), (3, 0): picked[1][:, (PACK + 2) * SPAN : (PACK + 2) * SPAN + HALF].bitcast(F32)}
         excess = {(3, 1): row(4), (2, 1): row(5), (1, 1): row(6), (0, 1): row(7), (3, 0): row(2)[:, :QUARTER]}
         z_upper = keep.tile([P, PACK * HALF], BF16, align_bytes=64)
         z_lower = [
@@ -215,10 +215,12 @@ def tile_picked_wsagecat_max_l_kernel(
         weave_h(1)
         weave_h(0)
         subtract(0, 1)
+        subtract(3, 0)
         relu(0, 1)
+        relu(3, 0)
         add_back(1, 1)
         add_back(0, 1)
-        subtract(3, 0)
+        add_back(3, 0)
         woven_upper = keep.tile([P, PACK * HALF], BF16, align_bytes=64)
         woven_lower = z_upper
 
@@ -227,8 +229,6 @@ def tile_picked_wsagecat_max_l_kernel(
             nc.scalar.copy(out=woven(dst[:, PACK * first : PACK * (first + n)]), in_=near(rows))
 
         weave_z(z_upper[:], woven_upper, 0, QUARTER)
-        relu(3, 0)
-        add_back(3, 0)
         weave_z(z_upper[:], woven_upper, QUARTER, QUARTER)
 
         def largest(planes, j):

@@ -81,14 +81,14 @@ def tile_picked_wsagecat_max_l_kernel(
                 in_=w1_woven[:, t0:t1, :, :].rearrange("p t m j -> p (t m j)"),
             )
 
-        cast_w1(nc.vector.tensor_copy, 0, 2, 4)
-        cast_w1(nc.scalar.copy, 0, 0, 2)
-        cast_w1(nc.vector.tensor_copy, 1, 3, 4)
-        cast_w1(nc.vector.tensor_copy, 1, 2, 3)
-        cast_w1(nc.scalar.copy, 1, 0, 2)
-        quantise_w1(3, 4)
-        quantise_w1(2, 3)
-        quantise_w1(0, 2)
+        cast_w1(nc.vector.tensor_copy, 0, 0, 2)
+        cast_w1(nc.scalar.copy, 0, 2, 4)
+        cast_w1(nc.vector.tensor_copy, 1, 0, 1)
+        cast_w1(nc.vector.tensor_copy, 1, 1, 2)
+        cast_w1(nc.scalar.copy, 1, 2, 4)
+        quantise_w1(0, 1)
+        quantise_w1(1, 2)
+        quantise_w1(2, 4)
 
         def project(b, t, start, stop):
             acc_h = bank(b, "acc_h")
@@ -112,18 +112,18 @@ def tile_picked_wsagecat_max_l_kernel(
         edges = (0, QUARTER, 2 * QUARTER, 3 * QUARTER, 3 * QUARTER + QUARTER // 2, T)
         for piece, b in enumerate((2, 3, 4, 5, 0)):
             start, stop = edges[piece], edges[piece + 1]
-            acc_h = project(b, 3, start, stop)
+            acc_h = project(b, 0, start, stop)
             if piece == 3:
-                nc.vector.tensor_scalar_max(plane(3, start, stop), acc_h[:, : stop - start], 0.0)
+                nc.vector.tensor_scalar_max(plane(0, start, stop), acc_h[:, : stop - start], 0.0)
             else:
-                nc.scalar.activation(plane(3, start, stop), acc_h[:, : stop - start], RELU)
+                nc.scalar.activation(plane(0, start, stop), acc_h[:, : stop - start], RELU)
         for start, b in ((BANK, 1), (0, 0)):
-            acc_h = project(b, 2, start, start + BANK)
-            nc.scalar.activation(plane(2, start, start + BANK), acc_h[:], RELU)
-        for t, b in ((1, 6), (0, 7)):
+            acc_h = project(b, 1, start, start + BANK)
+            nc.scalar.activation(plane(1, start, start + BANK), acc_h[:], RELU)
+        for t, b in ((2, 6), (3, 7)):
             acc_h = project(b, t, BANK, T)
             nc.scalar.activation(plane(t, BANK, T), acc_h[:], RELU)
-        lower = [(t, project(b, t, 0, BANK)) for t, b in ((1, 1), (0, 0))]
+        lower = [(t, project(b, t, 0, BANK)) for t, b in ((2, 1), (3, 0))]
         for start, stop in ((0, BANK - P), (BANK - P, BANK)):
             for t, acc_h in lower:
                 nc.scalar.activation(plane(t, start, stop), acc_h[:, start:stop], RELU)
@@ -160,8 +160,9 @@ def tile_picked_wsagecat_max_l_kernel(
         def row(r):
             return scratch[:, r * HALF : (r + 1) * HALF]
 
-        diff = {(3, 1): row(0), (2, 1): row(1), (1, 1): row(4), (0, 1): row(5), (3, 0): picked[1][:, (PACK + 2) * SPAN : (PACK + 2) * SPAN + HALF].bitcast(F32)}
-        excess = {(3, 1): row(4), (2, 1): row(5), (1, 1): row(6), (0, 1): row(7), (3, 0): row(2)[:, :QUARTER]}
+        spent = picked[1][:, PACK * SPAN : PACK * SPAN + T].bitcast(F32)
+        diff = {(0, 1): row(0), (1, 1): row(1), (2, 1): row(4), (3, 1): row(5), (0, 0): spent}
+        excess = {(0, 1): row(4), (1, 1): row(5), (2, 1): row(6), (3, 1): row(7), (0, 0): row(2)}
         z_upper = keep.tile([P, PACK * HALF], BF16, align_bytes=64)
         z_lower = [
             keep.tile([P, PACK * QUARTER], BF16, name="z_lower0", tag="late", align_bytes=64),
@@ -173,7 +174,7 @@ def tile_picked_wsagecat_max_l_kernel(
             return values.rearrange("p (u c) -> p u c", c=RUN)
 
         def side(d, t, half):
-            return runs(d, half, t, t + 1)[:, 0, : (1 + half) * per, :]
+            return runs(d, half, t, t + 1)[:, 0]
 
         def subtract(t, half):
             nc.gpsimd.tensor_tensor(in_runs(diff[t, half]), side(0, t, half), side(1, t, half), SUB)
@@ -182,9 +183,14 @@ def tile_picked_wsagecat_max_l_kernel(
             nc.scalar.activation(excess[t, half], diff[t, half], RELU)
 
         def add_back(t, half):
-            n = (1 + half) * QUARTER
-            dst = (z_lower[0], z_upper)[half][:, t * n : (t + 1) * n]
+            dst = z_upper[:, t * HALF : (t + 1) * HALF]
             nc.gpsimd.tensor_tensor(in_runs(dst), in_runs(excess[t, half]), side(1, t, half), ADD)
+
+        def add_back_lower(j):
+            within = slice(j * per, (j + 1) * per)
+            nc.gpsimd.tensor_tensor(
+                in_runs(z_lower[j][:, :QUARTER]), in_runs(excess[0, 0])[:, within], side(1, 0, 0)[:, within], ADD
+            )
 
         def weave_h(j):
             nc.scalar.copy(
@@ -192,35 +198,36 @@ def tile_picked_wsagecat_max_l_kernel(
                 in_=near(h_planes[:, :, j * QUARTER : (j + 1) * QUARTER]),
             )
 
-        for t in (3, 2, 1, 0):
+        for t in range(PACK):
             gather(t, 1)
-        subtract(3, 1)
-        relu(3, 1)
+        subtract(0, 1)
+        relu(0, 1)
         for s in range(2):
             nc.scalar.copy(out=woven(w23_woven[:, s * PACK * N : (s + 1) * PACK * N]), in_=near(w23_raw[:, s]))
         picked[0] = keep.tile([P, 2 * PACK * SPAN], BF16, name="picked_lower", tag="raw", align_bytes=64)
-        for t in (3, 2, 1):
+        for t in range(PACK - 1):
             gather(t, 0)
-        gather_part(0, 0, 0, 0, HALF)
-        gather_part(0, 0, 1, 0, QUARTER)
-        gather_part(0, 0, 1, QUARTER, QUARTER)
-        subtract(2, 1)
-        relu(2, 1)
-        add_back(3, 1)
-        weave_h(3)
-        weave_h(2)
+        gather_part(3, 0, 0, 0, HALF)
+        gather_part(3, 0, 1, 0, QUARTER)
+        gather_part(3, 0, 1, QUARTER, QUARTER)
         subtract(1, 1)
         relu(1, 1)
-        add_back(2, 1)
+        add_back(0, 1)
+        weave_h(3)
+        weave_h(2)
+        subtract(2, 1)
+        relu(2, 1)
+        add_back(1, 1)
         weave_h(1)
         weave_h(0)
-        subtract(0, 1)
-        subtract(3, 0)
-        relu(0, 1)
-        relu(3, 0)
-        add_back(1, 1)
-        add_back(0, 1)
-        add_back(3, 0)
+        subtract(3, 1)
+        subtract(0, 0)
+        relu(3, 1)
+        relu(0, 0)
+        add_back(2, 1)
+        add_back(3, 1)
+        add_back_lower(0)
+        add_back_lower(1)
         woven_upper = keep.tile([P, PACK * HALF], BF16, align_bytes=64)
         woven_lower = z_upper
 
@@ -231,12 +238,12 @@ def tile_picked_wsagecat_max_l_kernel(
         weave_z(z_upper[:], woven_upper, 0, QUARTER)
         weave_z(z_upper[:], woven_upper, QUARTER, QUARTER)
 
-        def largest(planes, j):
+        def largest(j):
             within = slice(j * per, (j + 1) * per)
             nc.vector.tensor_tensor(
-                z_lower[j][:].rearrange("p (t u c) -> p t u c", t=PACK, c=RUN)[:, :planes],
-                runs(0, 0, 0, planes)[:, :, within, :],
-                runs(1, 0, 0, planes)[:, :, within, :],
+                z_lower[j][:].rearrange("p (t u c) -> p t u c", t=PACK, c=RUN)[:, 1:],
+                runs(0, 0, 1, PACK)[:, :, within, :],
+                runs(1, 0, 1, PACK)[:, :, within, :],
                 MAX,
             )
             weave_z(z_lower[j][:], woven_lower[:, j * T : (j + 1) * T], 0, QUARTER)
@@ -269,17 +276,23 @@ def tile_picked_wsagecat_max_l_kernel(
                     stop=(i == len(steps) - 1),
                 )
             copy(out=result[:, base : base + total], in_=acc_o[:, :total])
+
+        def store(base, total):
             nc.sync.dma_start(out=out[:, base : base + total], in_=result[:, base : base + total])
 
-        largest(3, 0)
-        largest(4, 1)
+        largest(0)
+        largest(1)
         quantise(w23_codes, w23_scale, 0, 2 * N, w23_woven[:])
         quantise(h_codes, h_scale, HALF, HALF, h_woven[1][:])
         quantise(z_codes, z_scale, HALF, HALF, woven_upper[:])
         finish(2, HALF, HALF, ((HALF, HALF),), nc.scalar.copy, h_codes)
+        store(HALF, HALF)
         late_codes = keep.tile([P, HALF], U32, tag="late", align_bytes=64)
         quantise(late_codes, h_scale, 0, HALF, h_woven[0][:])
         for first, n in ((0, 2 * P), (2 * P, P), (3 * P, P)):
             quantise(z_codes, z_scale, first, n, woven_lower[:, PACK * first : PACK * (first + n)])
         finish(3, 0, 2 * P, ((0, 2 * P),), nc.scalar.copy, late_codes)
-        finish(4, 2 * P, 2 * P, ((2 * P, P), (3 * P, P)), nc.vector.tensor_copy, late_codes)
+        store(0, 2 * P)
+        finish(4, 2 * P, P, ((2 * P, P),), nc.vector.tensor_copy, late_codes)
+        finish(5, 3 * P, P, ((3 * P, P),), nc.vector.tensor_copy, late_codes)
+        store(2 * P, 2 * P)

@@ -24,6 +24,7 @@ QUARTER = T // 4
 NEAR = 4
 RUN = 64
 GAP = 8
+WINDOW = T + 352
 HALF = T // 2
 SPAN = HALF // RUN * (RUN + GAP)
 
@@ -81,14 +82,14 @@ def tile_picked_wsagecat_max_l_kernel(
                 in_=w1_woven[:, t0:t1, :, :].rearrange("p t m j -> p (t m j)"),
             )
 
-        cast_w1(nc.vector.tensor_copy, 0, 0, 2)
-        cast_w1(nc.scalar.copy, 0, 2, 4)
-        cast_w1(nc.vector.tensor_copy, 1, 0, 1)
-        cast_w1(nc.vector.tensor_copy, 1, 1, 2)
-        cast_w1(nc.scalar.copy, 1, 2, 4)
-        quantise_w1(0, 1)
-        quantise_w1(1, 2)
-        quantise_w1(2, 4)
+        cast_w1(nc.vector.tensor_copy, 0, 2, 4)
+        cast_w1(nc.scalar.copy, 0, 0, 2)
+        cast_w1(nc.vector.tensor_copy, 1, 2, 3)
+        cast_w1(nc.vector.tensor_copy, 1, 3, 4)
+        cast_w1(nc.scalar.copy, 1, 0, 2)
+        quantise_w1(2, 3)
+        quantise_w1(3, 4)
+        quantise_w1(0, 2)
 
         def project(b, t, start, stop):
             acc_h = bank(b, "acc_h")
@@ -112,18 +113,18 @@ def tile_picked_wsagecat_max_l_kernel(
         edges = (0, QUARTER, 2 * QUARTER, 3 * QUARTER, 3 * QUARTER + QUARTER // 2, T)
         for piece, b in enumerate((2, 3, 4, 5, 0)):
             start, stop = edges[piece], edges[piece + 1]
-            acc_h = project(b, 0, start, stop)
+            acc_h = project(b, 2, start, stop)
             if piece == 3:
-                nc.vector.tensor_scalar_max(plane(0, start, stop), acc_h[:, : stop - start], 0.0)
+                nc.vector.tensor_scalar_max(plane(2, start, stop), acc_h[:, : stop - start], 0.0)
             else:
-                nc.scalar.activation(plane(0, start, stop), acc_h[:, : stop - start], RELU)
+                nc.scalar.activation(plane(2, start, stop), acc_h[:, : stop - start], RELU)
         for start, b in ((BANK, 1), (0, 0)):
-            acc_h = project(b, 1, start, start + BANK)
-            nc.scalar.activation(plane(1, start, start + BANK), acc_h[:], RELU)
-        for t, b in ((2, 6), (3, 7)):
+            acc_h = project(b, 3, start, start + BANK)
+            nc.scalar.activation(plane(3, start, start + BANK), acc_h[:], RELU)
+        for t, b in ((1, 6), (0, 7)):
             acc_h = project(b, t, BANK, T)
             nc.scalar.activation(plane(t, BANK, T), acc_h[:], RELU)
-        lower = [(t, project(b, t, 0, BANK)) for t, b in ((2, 1), (3, 0))]
+        lower = [(t, project(b, t, 0, BANK)) for t, b in ((1, 1), (0, 0))]
         for start, stop in ((0, BANK - P), (BANK - P, BANK)):
             for t, acc_h in lower:
                 nc.scalar.activation(plane(t, start, stop), acc_h[:, start:stop], RELU)
@@ -137,60 +138,55 @@ def tile_picked_wsagecat_max_l_kernel(
         w23_woven = keep.tile([P, 2 * PACK * N], BF16, tag="slot", align_bytes=64)
         h_woven = [keep.tile([P, PACK * HALF], BF16, name="h_woven%d" % half, align_bytes=64) for half in range(2)]
         h_planes = h[:].rearrange("p (t c) -> p t c", t=PACK)
-        picked = [None, keep.tile([P, 2 * PACK * SPAN], BF16, name="picked_upper", align_bytes=64)]
-
-        def runs(d, half, t0, t1):
-            base = (d * PACK + t0) * SPAN
-            rows = picked[half][:, base : base + (t1 - t0) * SPAN]
-            return rows.rearrange("p (t u c) -> p t u c", t=t1 - t0, c=RUN + GAP)[:, :, :, :RUN]
-
-        def gather_part(t, half, d, first, n):
-            entry = half * HALF + first
-            nc.vector.tensor_copy(
-                runs(d, half, t, t + 1)[:, 0, first // RUN : (first + n) // RUN, :],
-                plane(t, 0, T).indirect(lists[d][:, entry // 16 : (entry + n) // 16]),
-            )
-
-        def gather(t, half):
-            for d in range(2):
-                gather_part(t, half, d, 0, HALF)
-
-        scratch = keep.tile([P, 8 * HALF], F32, align_bytes=64)
-
-        def row(r):
-            return scratch[:, r * HALF : (r + 1) * HALF]
-
-        spent = picked[1][:, PACK * SPAN : PACK * SPAN + T].bitcast(F32)
-        diff = {(0, 1): row(0), (1, 1): row(1), (2, 1): row(4), (3, 1): row(5), (0, 0): spent}
-        excess = {(0, 1): row(4), (1, 1): row(5), (2, 1): row(6), (3, 1): row(7), (0, 0): row(2)}
-        z_upper = keep.tile([P, PACK * HALF], BF16, align_bytes=64)
-        z_lower = [
-            keep.tile([P, PACK * QUARTER], BF16, name="z_lower0", tag="late", align_bytes=64),
-            keep.tile([P, PACK * QUARTER], BF16, name="z_lower1", align_bytes=64),
-        ]
         per = QUARTER // RUN
+
+        def in_gaps(rows):
+            return rows.rearrange("p (u c) -> p u c", c=RUN + GAP)[:, :, :RUN]
 
         def in_runs(values):
             return values.rearrange("p (u c) -> p u c", c=RUN)
 
-        def side(d, t, half):
-            return runs(d, half, t, t + 1)[:, 0]
+        def gather(dst, t, d, first, n, window=T):
+            nc.vector.tensor_copy(dst, plane(t, 0, window).indirect(lists[d][:, first // 16 : (first + n) // 16]))
 
-        def subtract(t, half):
-            nc.gpsimd.tensor_tensor(in_runs(diff[t, half]), side(0, t, half), side(1, t, half), SUB)
+        early = keep.tile([P, 2 * 3 * SPAN], BF16, align_bytes=64)
 
-        def relu(t, half):
-            nc.scalar.activation(excess[t, half], diff[t, half], RELU)
+        def early_row(d, t):
+            return in_gaps(early[:, (3 * d + t - 1) * SPAN : (3 * d + t) * SPAN])
 
-        def add_back(t, half):
-            dst = z_upper[:, t * HALF : (t + 1) * HALF]
-            nc.gpsimd.tensor_tensor(in_runs(dst), in_runs(excess[t, half]), side(1, t, half), ADD)
+        for t in (2, 3, 1):
+            for d in range(2):
+                gather(early_row(d, t), t, d, 0, HALF)
 
-        def add_back_lower(j):
-            within = slice(j * per, (j + 1) * per)
-            nc.gpsimd.tensor_tensor(
-                in_runs(z_lower[j][:, :QUARTER]), in_runs(excess[0, 0])[:, within], side(1, 0, 0)[:, within], ADD
-            )
+        scratch = keep.tile([P, 8 * HALF], F32, align_bytes=64)
+
+        def row(r, n=HALF):
+            return scratch[:, r * HALF : r * HALF + n]
+
+        diff = {2: row(0), 3: row(1), 1: row(4), 0: scratch[:, 11 * QUARTER : 14 * QUARTER]}
+        excess = {2: row(4), 3: row(5), 1: row(6), 0: row(0, 3 * QUARTER)}
+        z_early = keep.tile([P, PACK * HALF], BF16, align_bytes=64)
+        z_late = [
+            keep.tile([P, PACK * QUARTER], BF16, name="z_late0", tag="late", align_bytes=64),
+            keep.tile([P, PACK * QUARTER], BF16, name="z_late1", align_bytes=64),
+        ]
+
+        def side(d, t):
+            return early_row(d, t) if t else late_rows(d, 0, 2)[:, : 3 * per]
+
+        def subtract(t, j0=0, j1=2):
+            part = slice(j0 * per, j1 * per)
+            nc.gpsimd.tensor_tensor(in_runs(diff[t])[:, part], side(0, t)[:, part], side(1, t)[:, part], SUB)
+
+        def relu(t, j0=0, j1=2):
+            part = slice(j0 * QUARTER, j1 * QUARTER)
+            nc.scalar.activation(excess[t][:, part], diff[t][:, part], RELU)
+
+        def add_back(t, dst, u0, u1):
+            nc.gpsimd.tensor_tensor(in_runs(dst), in_runs(excess[t])[:, u0:u1], side(1, t)[:, u0:u1], ADD)
+
+        def add_early(t):
+            add_back(t, z_early[:, t * HALF : (t + 1) * HALF], 0, 2 * per)
 
         def weave_h(j):
             nc.scalar.copy(
@@ -198,57 +194,65 @@ def tile_picked_wsagecat_max_l_kernel(
                 in_=near(h_planes[:, :, j * QUARTER : (j + 1) * QUARTER]),
             )
 
-        for t in range(PACK):
-            gather(t, 1)
-        subtract(0, 1)
-        relu(0, 1)
+        subtract(2)
+        relu(2)
         for s in range(2):
             nc.scalar.copy(out=woven(w23_woven[:, s * PACK * N : (s + 1) * PACK * N]), in_=near(w23_raw[:, s]))
-        picked[0] = keep.tile([P, 2 * PACK * SPAN], BF16, name="picked_lower", tag="raw", align_bytes=64)
-        for t in range(PACK - 1):
-            gather(t, 0)
-        gather_part(3, 0, 0, 0, HALF)
-        gather_part(3, 0, 1, 0, QUARTER)
-        gather_part(3, 0, 1, QUARTER, QUARTER)
-        subtract(1, 1)
-        relu(1, 1)
-        add_back(0, 1)
-        weave_h(3)
-        weave_h(2)
-        subtract(2, 1)
-        relu(2, 1)
-        add_back(1, 1)
-        weave_h(1)
+        late = keep.tile([P, 2 * 5 * SPAN], BF16, tag="raw", align_bytes=64)
+
+        def late_rows(d, r0, r1):
+            return in_gaps(late[:, (5 * d + r0) * SPAN : (5 * d + r1) * SPAN])
+
+        for d in range(2):
+            gather(late_rows(d, 0, 2), 0, d, 0, T, WINDOW)
+        for t in (1, 2):
+            for d in range(2):
+                gather(late_rows(d, t + 1, t + 2), t, d, HALF, HALF)
+        gather(late_rows(0, 4, 5), 3, 0, HALF, HALF)
+        for j in range(2):
+            gather(late_rows(1, 4, 5)[:, j * per : (j + 1) * per], 3, 1, HALF + j * QUARTER, QUARTER)
+
+        subtract(3)
+        relu(3)
+        add_early(2)
         weave_h(0)
-        subtract(3, 1)
-        subtract(0, 0)
-        relu(3, 1)
-        relu(0, 0)
-        add_back(2, 1)
-        add_back(3, 1)
-        add_back_lower(0)
-        add_back_lower(1)
-        woven_upper = keep.tile([P, PACK * HALF], BF16, align_bytes=64)
-        woven_lower = z_upper
+        weave_h(1)
+        subtract(1)
+        relu(1)
+        add_early(3)
+        weave_h(2)
+        weave_h(3)
+        add_early(1)
+        subtract(0)
+        subtract(0, 2, 3)
+        relu(0)
+        relu(0, 2, 3)
+        add_early(0)
+        add_back(0, z_late[0][:, :QUARTER], 2 * per, 3 * per)
 
-        def weave_z(planes, dst, first, n):
-            rows = planes.rearrange("p (t c) -> p t c", t=PACK)[:, :, first : first + n]
-            nc.scalar.copy(out=woven(dst[:, PACK * first : PACK * (first + n)]), in_=near(rows))
+        woven_early = keep.tile([P, PACK * HALF], BF16, align_bytes=64)
+        woven_late = z_early
 
-        weave_z(z_upper[:], woven_upper, 0, QUARTER)
-        weave_z(z_upper[:], woven_upper, QUARTER, QUARTER)
+        def weave_z(planes, dst):
+            nc.scalar.copy(out=woven(dst), in_=near(planes))
+
+        for j in range(2):
+            weave_z(
+                z_early[:].rearrange("p (t c) -> p t c", t=PACK)[:, :, j * QUARTER : (j + 1) * QUARTER],
+                woven_early[:, j * T : (j + 1) * T],
+            )
 
         def largest(j):
-            within = slice(j * per, (j + 1) * per)
-            nc.vector.tensor_tensor(
-                z_lower[j][:].rearrange("p (t u c) -> p t u c", t=PACK, c=RUN)[:, 1:],
-                runs(0, 0, 1, PACK)[:, :, within, :],
-                runs(1, 0, 1, PACK)[:, :, within, :],
-                MAX,
-            )
-            weave_z(z_lower[j][:], woven_lower[:, j * T : (j + 1) * T], 0, QUARTER)
+            t0 = 1 - j
+            pair = [
+                late_rows(d, 1 + t0, 5).rearrange("p (t u) c -> p t u c", t=PACK - t0)[:, :, j * per : (j + 1) * per]
+                for d in range(2)
+            ]
+            dst = z_late[j][:].rearrange("p (t u c) -> p t u c", t=PACK, c=RUN)[:, t0:]
+            nc.vector.tensor_tensor(dst, pair[0], pair[1], MAX)
+            weave_z(z_late[j][:].rearrange("p (t c) -> p t c", t=PACK), woven_late[:, j * T : (j + 1) * T])
 
-        h_codes = keep.tile([P, T], U32, align_bytes=64)
+        h_codes = keep.tile([P, HALF], U32, align_bytes=64)
         h_scale = keep.tile([P, T], U8, align_bytes=64)
         z_codes = keep.tile([P, T], U32, align_bytes=64)
         z_scale = keep.tile([P, T], U8, align_bytes=64)
@@ -257,20 +261,19 @@ def tile_picked_wsagecat_max_l_kernel(
         result = keep.tile([P, T], F32)
 
         def quantise(codes, scale, first, n, source):
-            nc.vector.quantize_mx(
-                out=codes[:, first : first + n].bitcast(FP8X4), scales=scale[:, first : first + n], in_=source
-            )
+            nc.vector.quantize_mx(out=codes.bitcast(FP8X4), scales=scale[:, first : first + n], in_=source)
 
-        def finish(b, base, total, z_pieces, copy, h_codes):
+        def finish(b, base, total, z_pieces, copy, codes_of_h):
             acc_o = bank(b, "acc_o")
             steps = [(0, base, total)] + [(1, first, n) for first, n in z_pieces]
             for i, (s, first, n) in enumerate(steps):
-                codes, scale = ((h_codes, h_scale), (z_codes, z_scale))[s]
+                codes = (codes_of_h, z_codes[:, first : first + n])[s]
+                scale = (h_scale, z_scale)[s]
                 nc.tensor.matmul_mx(
                     out=acc_o[:, first - base : first - base + n],
                     lhsT=w23_codes[:, s * N : (s + 1) * N].bitcast(FP8X4),
                     lhsT_scale=w23_scale[:, s * N : (s + 1) * N],
-                    rhs=codes[:, first : first + n].bitcast(FP8X4),
+                    rhs=codes.bitcast(FP8X4),
                     rhs_scale=scale[:, first : first + n],
                     start=(i == 0),
                     stop=(i == len(steps) - 1),
@@ -282,17 +285,18 @@ def tile_picked_wsagecat_max_l_kernel(
 
         largest(0)
         largest(1)
-        quantise(w23_codes, w23_scale, 0, 2 * N, w23_woven[:])
-        quantise(h_codes, h_scale, HALF, HALF, h_woven[1][:])
-        quantise(z_codes, z_scale, HALF, HALF, woven_upper[:])
-        finish(2, HALF, HALF, ((HALF, HALF),), nc.scalar.copy, h_codes)
-        store(HALF, HALF)
+        quantise(w23_codes[:], w23_scale, 0, 2 * N, w23_woven[:])
+        quantise(h_codes[:], h_scale, 0, HALF, h_woven[0][:])
+        quantise(z_codes[:, :HALF], z_scale, 0, HALF, woven_early[:])
+        finish(2, 0, HALF, ((0, HALF),), nc.scalar.copy, h_codes[:])
+        store(0, HALF)
         late_codes = keep.tile([P, HALF], U32, tag="late", align_bytes=64)
-        quantise(late_codes, h_scale, 0, HALF, h_woven[0][:])
+        quantise(late_codes[:], h_scale, HALF, HALF, h_woven[1][:])
         for first, n in ((0, 2 * P), (2 * P, P), (3 * P, P)):
-            quantise(z_codes, z_scale, first, n, woven_lower[:, PACK * first : PACK * (first + n)])
-        finish(3, 0, 2 * P, ((0, 2 * P),), nc.scalar.copy, late_codes)
-        store(0, 2 * P)
-        finish(4, 2 * P, P, ((2 * P, P),), nc.vector.tensor_copy, late_codes)
-        finish(5, 3 * P, P, ((3 * P, P),), nc.vector.tensor_copy, late_codes)
-        store(2 * P, 2 * P)
+            cols = slice(HALF + first, HALF + first + n)
+            quantise(z_codes[:, cols], z_scale, HALF + first, n, woven_late[:, PACK * first : PACK * (first + n)])
+        finish(3, 4 * P, 2 * P, ((4 * P, 2 * P),), nc.scalar.copy, late_codes[:, : 2 * P])
+        finish(4, 6 * P, P, ((6 * P, P),), nc.vector.tensor_copy, late_codes[:, 2 * P : 3 * P])
+        store(4 * P, 3 * P)
+        finish(5, 7 * P, P, ((7 * P, P),), nc.vector.tensor_copy, late_codes[:, 3 * P :])
+        store(7 * P, P)

@@ -20,13 +20,14 @@ RELU = mybir.ActivationFunctionType.Relu
 P = 128
 PACK = 4
 BANK = 512
+HALF = T // 2
 QUARTER = T // 4
 NEAR = 4
 RUN = 64
 GAP = 8
-WINDOW = T + 352
-HALF = T // 2
 SPAN = HALF // RUN * (RUN + GAP)
+RUNS = QUARTER // RUN
+WINDOW = T + 352
 
 
 def tile_picked_wsagecat_max_l_kernel(
@@ -57,7 +58,7 @@ def tile_picked_wsagecat_max_l_kernel(
                 in_=x_scales[0, 4 * q : 4 * q + 4, :].bitcast(I32).rearrange("r (a c) -> a r c", a=4),
             )
         x_rows = x_words[0].rearrange("p n t -> p (n t)").bitcast(I32)
-        for nodes in (slice(0, T // 2), slice(T // 2, T - QUARTER), slice(T - QUARTER, T)):
+        for nodes in (slice(0, HALF), slice(HALF, T - QUARTER), slice(T - QUARTER, T)):
             nc.sync.dma_start(out=x_codes[:, nodes].bitcast(I32), in_=x_rows[:, nodes])
         nc.sync.dma_start(lists[0][:], pos1)
         nc.sync.dma_start(lists[1][:], pos2)
@@ -66,7 +67,7 @@ def tile_picked_wsagecat_max_l_kernel(
             nc.sync.dma_start(out=w23_raw[:, s], in_=w.rearrange("(p j) n -> p j n", j=PACK))
 
         w1_woven = keep.tile([P, PACK, P, PACK], BF16, align_bytes=64)
-        w1_codes = keep.tile([P, PACK, P], U32, tag="slot", align_bytes=64)
+        w1_codes = keep.tile([P, PACK, P], U32, tag="weights", align_bytes=64)
         w1_scale = keep.tile([P, PACK, P], U8, align_bytes=64)
 
         def cast_w1(cast, u, t0, t1):
@@ -91,7 +92,10 @@ def tile_picked_wsagecat_max_l_kernel(
         quantise_w1(3, 4)
         quantise_w1(0, 2)
 
-        def project(b, t, start, stop):
+        def plane(t, start, stop):
+            return h[:, t * T + start : t * T + stop]
+
+        def project(b, t, start, stop, on_vector=False):
             acc_h = bank(b, "acc_h")
             for b0 in reversed(range(start, stop, QUARTER)):
                 b1 = min(b0 + QUARTER, stop)
@@ -105,29 +109,18 @@ def tile_picked_wsagecat_max_l_kernel(
                     start=True,
                     stop=True,
                 )
-            return acc_h
-
-        def plane(t, start, stop):
-            return h[:, t * T + start : t * T + stop]
-
-        edges = (0, QUARTER, 2 * QUARTER, 3 * QUARTER, 3 * QUARTER + QUARTER // 2, T)
-        for piece, b in enumerate((2, 3, 4, 5, 0)):
-            start, stop = edges[piece], edges[piece + 1]
-            acc_h = project(b, 2, start, stop)
-            if piece == 3:
-                nc.vector.tensor_scalar_max(plane(2, start, stop), acc_h[:, : stop - start], 0.0)
+            if on_vector:
+                nc.vector.tensor_scalar_max(plane(t, start, stop), acc_h[:, : stop - start], 0.0)
             else:
-                nc.scalar.activation(plane(2, start, stop), acc_h[:, : stop - start], RELU)
-        for start, b in ((BANK, 1), (0, 0)):
-            acc_h = project(b, 3, start, start + BANK)
-            nc.scalar.activation(plane(3, start, start + BANK), acc_h[:], RELU)
-        for t, b in ((1, 6), (0, 7)):
-            acc_h = project(b, t, BANK, T)
-            nc.scalar.activation(plane(t, BANK, T), acc_h[:], RELU)
-        lower = [(t, project(b, t, 0, BANK)) for t, b in ((1, 1), (0, 0))]
-        for start, stop in ((0, BANK - P), (BANK - P, BANK)):
-            for t, acc_h in lower:
-                nc.scalar.activation(plane(t, start, stop), acc_h[:, start:stop], RELU)
+                nc.scalar.activation(plane(t, start, stop), acc_h[:, : stop - start], RELU)
+
+        for a in range(3):
+            project(2 + a, 2, a * QUARTER, (a + 1) * QUARTER)
+        project(5, 2, T - 2 * P, T - P, on_vector=True)
+        project(0, 2, T - P, T)
+        for t, upper_bank, lower_bank in ((3, 1, 0), (1, 6, 1), (0, 7, 0)):
+            project(upper_bank, t, BANK, T)
+            project(lower_bank, t, 0, BANK)
 
         def near(rows):
             return rows.rearrange("p t (c i) -> p c t i", i=NEAR)
@@ -135,19 +128,20 @@ def tile_picked_wsagecat_max_l_kernel(
         def woven(values):
             return values.rearrange("p (c i t) -> p c t i", i=NEAR, t=PACK)
 
-        w23_woven = keep.tile([P, 2 * PACK * N], BF16, tag="slot", align_bytes=64)
-        h_woven = [keep.tile([P, PACK * HALF], BF16, name="h_woven%d" % half, align_bytes=64) for half in range(2)]
-        h_planes = h[:].rearrange("p (t c) -> p t c", t=PACK)
-        per = QUARTER // RUN
+        def by_plane(values):
+            return values.rearrange("p (t c) -> p t c", t=PACK)
 
-        def in_gaps(rows):
-            return rows.rearrange("p (u c) -> p u c", c=RUN + GAP)[:, :, :RUN]
+        def in_gaps(values):
+            return values.rearrange("p (u c) -> p u c", c=RUN + GAP)[:, :, :RUN]
 
         def in_runs(values):
             return values.rearrange("p (u c) -> p u c", c=RUN)
 
         def gather(dst, t, d, first, n, window=T):
             nc.vector.tensor_copy(dst, plane(t, 0, window).indirect(lists[d][:, first // 16 : (first + n) // 16]))
+
+        w23_woven = keep.tile([P, 2 * PACK * N], BF16, tag="weights", align_bytes=64)
+        h_woven = [keep.tile([P, PACK * HALF], BF16, name="h_woven%d" % half, align_bytes=64) for half in range(2)]
 
         early = keep.tile([P, 2 * 3 * SPAN], BF16, align_bytes=64)
 
@@ -158,46 +152,55 @@ def tile_picked_wsagecat_max_l_kernel(
             for d in range(2):
                 gather(early_row(d, t), t, d, 0, HALF)
 
-        scratch = keep.tile([P, 8 * HALF], F32, align_bytes=64)
+        scratch = keep.tile([P, 10 * QUARTER], F32, align_bytes=64)
 
-        def row(r, n=HALF):
-            return scratch[:, r * HALF : r * HALF + n]
+        def quarters(q0, q1):
+            return scratch[:, q0 * QUARTER : q1 * QUARTER]
 
-        diff = {2: row(0), 3: row(1), 1: row(4), 0: scratch[:, 11 * QUARTER : 14 * QUARTER]}
-        excess = {2: row(4), 3: row(5), 1: row(6), 0: row(0, 3 * QUARTER)}
+        diff = {2: quarters(0, 2), 3: quarters(2, 4), 1: quarters(4, 6), 0: quarters(7, 10)}
+        excess = {2: quarters(4, 6), 3: quarters(6, 8), 1: quarters(8, 10), 0: quarters(0, 3)}
         z_early = keep.tile([P, PACK * HALF], BF16, align_bytes=64)
         z_late = [
             keep.tile([P, PACK * QUARTER], BF16, name="z_late0", tag="late", align_bytes=64),
             keep.tile([P, PACK * QUARTER], BF16, name="z_late1", align_bytes=64),
         ]
 
-        def side(d, t):
-            return early_row(d, t) if t else late_rows(d, 0, 2)[:, : 3 * per]
+        def picked(d, t, q0, q1):
+            rows = early_row(d, t) if t else late_rows(d, 0, 2)
+            return rows[:, q0 * RUNS : q1 * RUNS]
 
-        def subtract(t, j0=0, j1=2):
-            part = slice(j0 * per, j1 * per)
-            nc.gpsimd.tensor_tensor(in_runs(diff[t])[:, part], side(0, t)[:, part], side(1, t)[:, part], SUB)
+        def subtract(t, q0, q1):
+            dst = in_runs(diff[t][:, q0 * QUARTER : q1 * QUARTER])
+            nc.gpsimd.tensor_tensor(dst, picked(0, t, q0, q1), picked(1, t, q0, q1), SUB)
 
-        def relu(t, j0=0, j1=2):
-            part = slice(j0 * QUARTER, j1 * QUARTER)
+        def relu(t, q0, q1):
+            part = slice(q0 * QUARTER, q1 * QUARTER)
             nc.scalar.activation(excess[t][:, part], diff[t][:, part], RELU)
 
-        def add_back(t, dst, u0, u1):
-            nc.gpsimd.tensor_tensor(in_runs(dst), in_runs(excess[t])[:, u0:u1], side(1, t)[:, u0:u1], ADD)
+        def add_back(dst, t, q0, q1):
+            above = in_runs(excess[t][:, q0 * QUARTER : q1 * QUARTER])
+            nc.gpsimd.tensor_tensor(in_runs(dst), above, picked(1, t, q0, q1), ADD)
 
         def add_early(t):
-            add_back(t, z_early[:, t * HALF : (t + 1) * HALF], 0, 2 * per)
+            add_back(by_plane(z_early[:])[:, t], t, 0, 2)
 
-        def weave_h(j):
-            nc.scalar.copy(
-                out=woven(h_woven[j // 2][:, j % 2 * T : (j % 2 + 1) * T]),
-                in_=near(h_planes[:, :, j * QUARTER : (j + 1) * QUARTER]),
-            )
+        def weave(planes, q, dst):
+            nc.scalar.copy(out=woven(dst), in_=near(by_plane(planes)[:, :, q * QUARTER : (q + 1) * QUARTER]))
 
-        subtract(2)
-        relu(2)
-        for s in range(2):
-            nc.scalar.copy(out=woven(w23_woven[:, s * PACK * N : (s + 1) * PACK * N]), in_=near(w23_raw[:, s]))
+        def woven_quarter(values, q):
+            return values[:, q * PACK * QUARTER : (q + 1) * PACK * QUARTER]
+
+        def weave_h(half):
+            for q in range(2):
+                weave(h[:], 2 * half + q, woven_quarter(h_woven[half], q))
+
+        subtract(2, 0, 2)
+        relu(2, 0, 2)
+        nc.scalar.copy(
+            out=w23_woven[:].rearrange("p (s c i t) -> p s c t i", s=2, i=NEAR, t=PACK),
+            in_=w23_raw[:].rearrange("p s t (c i) -> p s c t i", i=NEAR),
+        )
+
         late = keep.tile([P, 2 * 5 * SPAN], BF16, tag="raw", align_bytes=64)
 
         def late_rows(d, r0, r1):
@@ -209,50 +212,40 @@ def tile_picked_wsagecat_max_l_kernel(
             for d in range(2):
                 gather(late_rows(d, t + 1, t + 2), t, d, HALF, HALF)
         gather(late_rows(0, 4, 5), 3, 0, HALF, HALF)
-        for j in range(2):
-            gather(late_rows(1, 4, 5)[:, j * per : (j + 1) * per], 3, 1, HALF + j * QUARTER, QUARTER)
+        for q in range(2):
+            gather(late_rows(1, 4, 5)[:, q * RUNS : (q + 1) * RUNS], 3, 1, HALF + q * QUARTER, QUARTER)
 
-        subtract(3)
-        relu(3)
+        subtract(3, 0, 2)
+        relu(3, 0, 2)
         add_early(2)
         weave_h(0)
-        weave_h(1)
-        subtract(1)
-        relu(1)
+        subtract(1, 0, 2)
+        relu(1, 0, 2)
         add_early(3)
-        weave_h(2)
-        weave_h(3)
+        weave_h(1)
         add_early(1)
-        subtract(0)
+        subtract(0, 0, 2)
         subtract(0, 2, 3)
-        relu(0)
+        relu(0, 0, 2)
         relu(0, 2, 3)
         add_early(0)
-        add_back(0, z_late[0][:, :QUARTER], 2 * per, 3 * per)
+        add_back(by_plane(z_late[0][:])[:, 0], 0, 2, 3)
 
         woven_early = keep.tile([P, PACK * HALF], BF16, align_bytes=64)
+        for q in range(2):
+            weave(z_early[:], q, woven_quarter(woven_early, q))
         woven_late = z_early
 
-        def weave_z(planes, dst):
-            nc.scalar.copy(out=woven(dst), in_=near(planes))
-
-        for j in range(2):
-            weave_z(
-                z_early[:].rearrange("p (t c) -> p t c", t=PACK)[:, :, j * QUARTER : (j + 1) * QUARTER],
-                woven_early[:, j * T : (j + 1) * T],
-            )
-
-        def largest(j):
-            t0 = 1 - j
-            pair = [
-                late_rows(d, 1 + t0, 5).rearrange("p (t u) c -> p t u c", t=PACK - t0)[:, :, j * per : (j + 1) * per]
+        for q in range(2):
+            t0 = 1 - q
+            a, b = [
+                late_rows(d, 1 + t0, 5).rearrange("p (t u) c -> p t u c", t=PACK - t0)[:, :, q * RUNS : (q + 1) * RUNS]
                 for d in range(2)
             ]
-            dst = z_late[j][:].rearrange("p (t u c) -> p t u c", t=PACK, c=RUN)[:, t0:]
-            nc.vector.tensor_tensor(dst, pair[0], pair[1], MAX)
-            weave_z(z_late[j][:].rearrange("p (t c) -> p t c", t=PACK), woven_late[:, j * T : (j + 1) * T])
+            nc.vector.tensor_tensor(z_late[q][:].rearrange("p (t u c) -> p t u c", t=PACK, c=RUN)[:, t0:], a, b, MAX)
+            weave(z_late[q][:], 0, woven_quarter(woven_late, q))
 
-        h_codes = keep.tile([P, HALF], U32, align_bytes=64)
+        early_codes = keep.tile([P, HALF], U32, align_bytes=64)
         h_scale = keep.tile([P, T], U8, align_bytes=64)
         z_codes = keep.tile([P, T], U32, align_bytes=64)
         z_scale = keep.tile([P, T], U8, align_bytes=64)
@@ -260,43 +253,40 @@ def tile_picked_wsagecat_max_l_kernel(
         w23_scale = keep.tile([P, 2 * N], U8, align_bytes=64)
         result = keep.tile([P, T], F32)
 
-        def quantise(codes, scale, first, n, source):
-            nc.vector.quantize_mx(out=codes.bitcast(FP8X4), scales=scale[:, first : first + n], in_=source)
+        def quantise(codes, scale, values):
+            nc.vector.quantize_mx(out=codes.bitcast(FP8X4), scales=scale, in_=values)
 
-        def finish(b, base, total, z_pieces, copy, codes_of_h):
+        def finish(b, first, n, h_codes, copy):
             acc_o = bank(b, "acc_o")
-            steps = [(0, base, total)] + [(1, first, n) for first, n in z_pieces]
-            for i, (s, first, n) in enumerate(steps):
-                codes = (codes_of_h, z_codes[:, first : first + n])[s]
-                scale = (h_scale, z_scale)[s]
+            targets = slice(first, first + n)
+            for s, (codes, scale) in enumerate(((h_codes, h_scale), (z_codes[:, targets], z_scale))):
                 nc.tensor.matmul_mx(
-                    out=acc_o[:, first - base : first - base + n],
+                    out=acc_o[:, :n],
                     lhsT=w23_codes[:, s * N : (s + 1) * N].bitcast(FP8X4),
                     lhsT_scale=w23_scale[:, s * N : (s + 1) * N],
                     rhs=codes.bitcast(FP8X4),
-                    rhs_scale=scale[:, first : first + n],
-                    start=(i == 0),
-                    stop=(i == len(steps) - 1),
+                    rhs_scale=scale[:, targets],
+                    start=(s == 0),
+                    stop=(s == 1),
                 )
-            copy(out=result[:, base : base + total], in_=acc_o[:, :total])
+            copy(out=result[:, targets], in_=acc_o[:, :n])
 
-        def store(base, total):
-            nc.sync.dma_start(out=out[:, base : base + total], in_=result[:, base : base + total])
+        def store(first, stop):
+            nc.sync.dma_start(out=out[:, first:stop], in_=result[:, first:stop])
 
-        largest(0)
-        largest(1)
-        quantise(w23_codes[:], w23_scale, 0, 2 * N, w23_woven[:])
-        quantise(h_codes[:], h_scale, 0, HALF, h_woven[0][:])
-        quantise(z_codes[:, :HALF], z_scale, 0, HALF, woven_early[:])
-        finish(2, 0, HALF, ((0, HALF),), nc.scalar.copy, h_codes[:])
+        quantise(w23_codes[:], w23_scale[:], w23_woven[:])
+        quantise(early_codes[:], h_scale[:, :HALF], h_woven[0][:])
+        quantise(z_codes[:, :HALF], z_scale[:, :HALF], woven_early[:])
+        finish(2, 0, HALF, early_codes[:], nc.scalar.copy)
         store(0, HALF)
         late_codes = keep.tile([P, HALF], U32, tag="late", align_bytes=64)
-        quantise(late_codes[:], h_scale, HALF, HALF, h_woven[1][:])
-        for first, n in ((0, 2 * P), (2 * P, P), (3 * P, P)):
-            cols = slice(HALF + first, HALF + first + n)
-            quantise(z_codes[:, cols], z_scale, HALF + first, n, woven_late[:, PACK * first : PACK * (first + n)])
-        finish(3, 4 * P, 2 * P, ((4 * P, 2 * P),), nc.scalar.copy, late_codes[:, : 2 * P])
-        finish(4, 6 * P, P, ((6 * P, P),), nc.vector.tensor_copy, late_codes[:, 2 * P : 3 * P])
-        store(4 * P, 3 * P)
-        finish(5, 7 * P, P, ((7 * P, P),), nc.vector.tensor_copy, late_codes[:, 3 * P :])
-        store(7 * P, P)
+        quantise(late_codes[:], h_scale[:, HALF:], h_woven[1][:])
+        pieces = ((0, 2 * P), (2 * P, 3 * P), (3 * P, 4 * P))
+        for start, stop in pieces:
+            targets = slice(HALF + start, HALF + stop)
+            quantise(z_codes[:, targets], z_scale[:, targets], woven_late[:, PACK * start : PACK * stop])
+        finish(3, HALF, 2 * P, late_codes[:, : 2 * P], nc.scalar.copy)
+        finish(4, T - 2 * P, P, late_codes[:, 2 * P : 3 * P], nc.vector.tensor_copy)
+        store(HALF, T - P)
+        finish(5, T - P, P, late_codes[:, 3 * P :], nc.vector.tensor_copy)
+        store(T - P, T)

@@ -23,6 +23,7 @@ BANK = 512
 HALF = T // 2
 QUARTER = T // 4
 NEAR = 4
+NEAR_BF16 = 8
 RUN = 64
 GAP = 8
 SPAN = HALF // RUN * (RUN + GAP)
@@ -122,11 +123,11 @@ def tile_picked_wsagecat_max_l_kernel(
             project(upper_bank, t, BANK, T)
             project(lower_bank, t, 0, BANK)
 
-        def near(rows):
-            return rows.rearrange("p t (c i) -> p c t i", i=NEAR)
+        def near(rows, width):
+            return rows.rearrange("p t (c i) -> p c t i", i=width)
 
-        def woven(values):
-            return values.rearrange("p (c i t) -> p c t i", i=NEAR, t=PACK)
+        def woven(values, width):
+            return values.rearrange("p (c i t) -> p c t i", i=width, t=PACK)
 
         def by_plane(values):
             return values.rearrange("p (t c) -> p t c", t=PACK)
@@ -184,15 +185,16 @@ def tile_picked_wsagecat_max_l_kernel(
         def add_early(t):
             add_back(by_plane(z_early[:])[:, t], t, 0, 2)
 
-        def weave(planes, q, dst):
-            nc.scalar.copy(out=woven(dst), in_=near(by_plane(planes)[:, :, q * QUARTER : (q + 1) * QUARTER]))
+        def weave(planes, q, dst, width):
+            columns = by_plane(planes)[:, :, q * QUARTER : (q + 1) * QUARTER]
+            nc.scalar.copy(out=woven(dst, width), in_=near(columns, width))
 
         def woven_quarter(values, q):
             return values[:, q * PACK * QUARTER : (q + 1) * PACK * QUARTER]
 
         def weave_h(half):
             for q in range(2):
-                weave(h[:], 2 * half + q, woven_quarter(h_woven[half], q))
+                weave(h[:], 2 * half + q, woven_quarter(h_woven[half], q), NEAR)
 
         subtract(2, 0, 2)
         relu(2, 0, 2)
@@ -233,7 +235,7 @@ def tile_picked_wsagecat_max_l_kernel(
 
         woven_early = keep.tile([P, PACK * HALF], BF16, align_bytes=64)
         for q in range(2):
-            weave(z_early[:], q, woven_quarter(woven_early, q))
+            weave(z_early[:], q, woven_quarter(woven_early, q), NEAR_BF16)
         woven_late = z_early
 
         for q in range(2):
@@ -243,7 +245,7 @@ def tile_picked_wsagecat_max_l_kernel(
                 for d in range(2)
             ]
             nc.vector.tensor_tensor(z_late[q][:].rearrange("p (t u c) -> p t u c", t=PACK, c=RUN)[:, t0:], a, b, MAX)
-            weave(z_late[q][:], 0, woven_quarter(woven_late, q))
+            weave(z_late[q][:], 0, woven_quarter(woven_late, q), NEAR_BF16)
 
         early_codes = keep.tile([P, HALF], U32, align_bytes=64)
         h_scale = keep.tile([P, T], U8, align_bytes=64)

@@ -14,8 +14,9 @@ U8 = mybir.dt.uint8
 FP8X4 = mybir.dt.float8_e4m3fn_x4
 MAX = mybir.AluOpType.max
 ADD = mybir.AluOpType.add
-SUB = mybir.AluOpType.subtract
+MULT = mybir.AluOpType.mult
 RELU = mybir.ActivationFunctionType.Relu
+COPY = mybir.ActivationFunctionType.Copy
 
 P = 128
 PACK = 4
@@ -23,12 +24,8 @@ BANK = 512
 HALF = T // 2
 QUARTER = T // 4
 NEAR = 4
-NEAR_BF16 = 8
-RUN = 64
-GAP = 8
-SPAN = HALF // RUN * (RUN + GAP)
-RUNS = QUARTER // RUN
-WINDOW = T + 352
+PAIR = 2
+PIECES = ((0, HALF), (HALF, QUARTER), (T - 2 * P, P), (T - P, P))
 
 
 def tile_picked_wsagecat_max_l_kernel(
@@ -63,12 +60,12 @@ def tile_picked_wsagecat_max_l_kernel(
             nc.sync.dma_start(out=x_codes[:, nodes].bitcast(I32), in_=x_rows[:, nodes])
         nc.sync.dma_start(lists[0][:], pos1)
         nc.sync.dma_start(lists[1][:], pos2)
-        w23_raw = keep.tile([P, 2, PACK, N], F32, tag="raw", align_bytes=64)
+        w23_raw = keep.tile([P, 2, PACK, N], F32, align_bytes=64)
         for s, w in enumerate((w2, w3)):
             nc.sync.dma_start(out=w23_raw[:, s], in_=w.rearrange("(p j) n -> p j n", j=PACK))
 
         w1_woven = keep.tile([P, PACK, P, PACK], BF16, align_bytes=64)
-        w1_codes = keep.tile([P, PACK, P], U32, tag="weights", align_bytes=64)
+        w1_codes = keep.tile([P, PACK, P], U32, align_bytes=64)
         w1_scale = keep.tile([P, PACK, P], U8, align_bytes=64)
 
         def cast_w1(cast, u, t0, t1):
@@ -119,9 +116,10 @@ def tile_picked_wsagecat_max_l_kernel(
             project(2 + a, 2, a * QUARTER, (a + 1) * QUARTER)
         project(5, 2, T - 2 * P, T - P, on_vector=True)
         project(0, 2, T - P, T)
-        for t, upper_bank, lower_bank in ((3, 1, 0), (1, 6, 1), (0, 7, 0)):
-            project(upper_bank, t, BANK, T)
-            project(lower_bank, t, 0, BANK)
+        later = ((3, 1), (1, 6), (0, 7))
+        for start in (BANK, 0):
+            for t, b in later:
+                project(b, t, start, start + BANK, on_vector=True)
 
         def near(rows, width):
             return rows.rearrange("p t (c i) -> p c t i", i=width)
@@ -129,144 +127,71 @@ def tile_picked_wsagecat_max_l_kernel(
         def woven(values, width):
             return values.rearrange("p (c i t) -> p c t i", i=width, t=PACK)
 
-        def by_plane(values):
-            return values.rearrange("p (t c) -> p t c", t=PACK)
+        def weave(dst, rows):
+            nc.gpsimd.tensor_scalar(dst.rearrange("p (c t) -> p c t", t=PACK), rows.rearrange("p t c -> p c t"), 1.0, 0.0, MULT, ADD)
 
-        def in_gaps(values):
-            return values.rearrange("p (u c) -> p u c", c=RUN + GAP)[:, :, :RUN]
-
-        def in_runs(values):
-            return values.rearrange("p (u c) -> p u c", c=RUN)
-
-        def gather(dst, t, d, first, n, window=T):
-            nc.vector.tensor_copy(dst, plane(t, 0, window).indirect(lists[d][:, first // 16 : (first + n) // 16]))
-
-        w23_woven = keep.tile([P, 2 * PACK * N], BF16, tag="weights", align_bytes=64)
-        h_woven = [keep.tile([P, PACK * HALF], BF16, name="h_woven%d" % half, align_bytes=64) for half in range(2)]
-
-        early = keep.tile([P, 2 * 3 * SPAN], BF16, align_bytes=64)
-
-        def early_row(d, t):
-            return in_gaps(early[:, (3 * d + t - 1) * SPAN : (3 * d + t) * SPAN])
-
-        for t in (2, 3, 1):
-            for d in range(2):
-                gather(early_row(d, t), t, d, 0, HALF)
-
-        scratch = keep.tile([P, 10 * QUARTER], F32, align_bytes=64)
-
-        def quarters(q0, q1):
-            return scratch[:, q0 * QUARTER : q1 * QUARTER]
-
-        diff = {2: quarters(0, 2), 3: quarters(2, 4), 1: quarters(4, 6), 0: quarters(7, 10)}
-        excess = {2: quarters(4, 6), 3: quarters(6, 8), 1: quarters(8, 10), 0: quarters(0, 3)}
-        z_early = keep.tile([P, PACK * HALF], BF16, align_bytes=64)
-        z_late = [
-            keep.tile([P, PACK * QUARTER], BF16, name="z_late0", tag="late", align_bytes=64),
-            keep.tile([P, PACK * QUARTER], BF16, name="z_late1", align_bytes=64),
-        ]
-
-        def picked(d, t, q0, q1):
-            rows = early_row(d, t) if t else late_rows(d, 0, 2)
-            return rows[:, q0 * RUNS : q1 * RUNS]
-
-        def subtract(t, q0, q1):
-            dst = in_runs(diff[t][:, q0 * QUARTER : q1 * QUARTER])
-            nc.gpsimd.tensor_tensor(dst, picked(0, t, q0, q1), picked(1, t, q0, q1), SUB)
-
-        def relu(t, q0, q1):
-            part = slice(q0 * QUARTER, q1 * QUARTER)
-            nc.scalar.activation(excess[t][:, part], diff[t][:, part], RELU)
-
-        def add_back(dst, t, q0, q1):
-            above = in_runs(excess[t][:, q0 * QUARTER : q1 * QUARTER])
-            nc.gpsimd.tensor_tensor(in_runs(dst), above, picked(1, t, q0, q1), ADD)
-
-        def add_early(t):
-            add_back(by_plane(z_early[:])[:, t], t, 0, 2)
-
-        def weave(planes, q, dst, width):
-            columns = by_plane(planes)[:, :, q * QUARTER : (q + 1) * QUARTER]
-            nc.scalar.copy(out=woven(dst, width), in_=near(columns, width))
-
-        def woven_quarter(values, q):
-            return values[:, q * PACK * QUARTER : (q + 1) * PACK * QUARTER]
-
-        def weave_h(half):
-            for q in range(2):
-                weave(h[:], 2 * half + q, woven_quarter(h_woven[half], q), NEAR)
-
-        subtract(2, 0, 2)
-        relu(2, 0, 2)
-        nc.scalar.copy(
-            out=w23_woven[:].rearrange("p (s c i t) -> p s c t i", s=2, i=NEAR, t=PACK),
-            in_=w23_raw[:].rearrange("p s t (c i) -> p s c t i", i=NEAR),
-        )
-
-        late = keep.tile([P, 2 * 5 * SPAN], BF16, tag="raw", align_bytes=64)
-
-        def late_rows(d, r0, r1):
-            return in_gaps(late[:, (5 * d + r0) * SPAN : (5 * d + r1) * SPAN])
-
-        for d in range(2):
-            gather(late_rows(d, 0, 2), 0, d, 0, T, WINDOW)
-        for t in (1, 2):
-            for d in range(2):
-                gather(late_rows(d, t + 1, t + 2), t, d, HALF, HALF)
-        gather(late_rows(0, 4, 5), 3, 0, HALF, HALF)
-        for q in range(2):
-            gather(late_rows(1, 4, 5)[:, q * RUNS : (q + 1) * RUNS], 3, 1, HALF + q * QUARTER, QUARTER)
-
-        subtract(3, 0, 2)
-        relu(3, 0, 2)
-        add_early(2)
-        weave_h(0)
-        subtract(1, 0, 2)
-        relu(1, 0, 2)
-        add_early(3)
-        weave_h(1)
-        add_early(1)
-        subtract(0, 0, 2)
-        subtract(0, 2, 3)
-        relu(0, 0, 2)
-        relu(0, 2, 3)
-        add_early(0)
-        add_back(by_plane(z_late[0][:])[:, 0], 0, 2, 3)
-
-        woven_early = keep.tile([P, PACK * HALF], BF16, align_bytes=64)
-        for q in range(2):
-            weave(z_early[:], q, woven_quarter(woven_early, q), NEAR_BF16)
-        woven_late = z_early
-
-        for q in range(2):
-            t0 = 1 - q
-            a, b = [
-                late_rows(d, 1 + t0, 5).rearrange("p (t u) c -> p t u c", t=PACK - t0)[:, :, q * RUNS : (q + 1) * RUNS]
-                for d in range(2)
-            ]
-            nc.vector.tensor_tensor(z_late[q][:].rearrange("p (t u c) -> p t u c", t=PACK, c=RUN)[:, t0:], a, b, MAX)
-            weave(z_late[q][:], 0, woven_quarter(woven_late, q), NEAR_BF16)
-
-        early_codes = keep.tile([P, HALF], U32, align_bytes=64)
-        h_scale = keep.tile([P, T], U8, align_bytes=64)
+        h_codes = keep.tile([P, T + 2 * N], U32, align_bytes=64)
+        h_scale = keep.tile([P, T + 2 * N], U8, align_bytes=64)
+        w23_codes = h_codes[:, T:]
+        w23_scale = h_scale[:, T:]
         z_codes = keep.tile([P, T], U32, align_bytes=64)
         z_scale = keep.tile([P, T], U8, align_bytes=64)
-        w23_codes = keep.tile([P, 2 * N], U32, align_bytes=64)
-        w23_scale = keep.tile([P, 2 * N], U8, align_bytes=64)
         result = keep.tile([P, T], F32)
 
         def quantise(codes, scale, values):
             nc.vector.quantize_mx(out=codes.bitcast(FP8X4), scales=scale, in_=values)
 
-        def finish(b, first, n, h_codes, copy):
+        h_woven = keep.tile([P, PACK * (T + 2 * N)], BF16, align_bytes=64)
+        w23_woven = h_woven[:, PACK * T :]
+        for s in range(2):
+            weave(w23_woven[:, s * PACK * N : (s + 1) * PACK * N], w23_raw[:, s])
+        h_planes = h[:].rearrange("p (t c) -> p t c", t=PACK)
+        for q in reversed(range(4)):
+            weave(h_woven[:, q * PACK * QUARTER : (q + 1) * PACK * QUARTER], h_planes[:, :, q * QUARTER : (q + 1) * QUARTER])
+
+        picked = [keep.tile([P, 2, PACK, n], F32, name="picked%d" % u, align_bytes=64) for u, (first, n) in enumerate(PIECES)]
+
+        def gather(t, u, on_vector=False):
+            first, n = PIECES[u]
+            for d in range(2):
+                window = plane(t, 0, T).indirect(lists[d][:, first // 16 : (first + n) // 16])
+                if on_vector:
+                    nc.vector.tensor_copy(picked[u][:, d, t, :], window)
+                else:
+                    nc.scalar.activation(picked[u][:, d, t, :], window, COPY)
+
+        for u in range(4):
+            gather(2, u)
+        gather(3, 0)
+        gather(1, 0, on_vector=True)
+        gather(0, 0, on_vector=True)
+        gather(0, 1, on_vector=True)
+        for u in range(1, 4):
+            for t in (3, 1, 0)[: 2 if u == 1 else 3]:
+                gather(t, u)
+
+        z_woven = keep.tile([P, PACK * T], BF16, align_bytes=64)
+
+        def neighbours(u):
+            first, n = PIECES[u]
+            values = z_woven[:, PACK * first : PACK * (first + n)]
+            nc.vector.tensor_tensor(woven(values, PAIR), near(picked[u][:, 0], PAIR), near(picked[u][:, 1], PAIR), MAX)
+
+        def quantise_z(u):
+            first, n = PIECES[u]
+            targets = slice(first, first + n)
+            quantise(z_codes[:, targets], z_scale[:, targets], z_woven[:, PACK * first : PACK * (first + n)])
+
+        def finish(b, u, copy):
+            first, n = PIECES[u]
             acc_o = bank(b, "acc_o")
             targets = slice(first, first + n)
-            for s, (codes, scale) in enumerate(((h_codes, h_scale), (z_codes[:, targets], z_scale))):
+            for s, (codes, scale) in enumerate(((h_codes, h_scale), (z_codes, z_scale))):
                 nc.tensor.matmul_mx(
                     out=acc_o[:, :n],
                     lhsT=w23_codes[:, s * N : (s + 1) * N].bitcast(FP8X4),
                     lhsT_scale=w23_scale[:, s * N : (s + 1) * N],
-                    rhs=codes.bitcast(FP8X4),
+                    rhs=codes[:, targets].bitcast(FP8X4),
                     rhs_scale=scale[:, targets],
                     start=(s == 0),
                     stop=(s == 1),
@@ -276,19 +201,20 @@ def tile_picked_wsagecat_max_l_kernel(
         def store(first, stop):
             nc.sync.dma_start(out=out[:, first:stop], in_=result[:, first:stop])
 
-        quantise(w23_codes[:], w23_scale[:], w23_woven[:])
-        quantise(early_codes[:], h_scale[:, :HALF], h_woven[0][:])
-        quantise(z_codes[:, :HALF], z_scale[:, :HALF], woven_early[:])
-        finish(2, 0, HALF, early_codes[:], nc.scalar.copy)
+        neighbours(0)
+        quantise(h_codes[:, QUARTER:], h_scale[:, QUARTER:], h_woven[:, PACK * QUARTER :])
+        quantise(h_codes[:, :QUARTER], h_scale[:, :QUARTER], h_woven[:, : PACK * QUARTER])
+        quantise_z(0)
+        finish(2, 0, nc.scalar.copy)
         store(0, HALF)
-        late_codes = keep.tile([P, HALF], U32, tag="late", align_bytes=64)
-        quantise(late_codes[:], h_scale[:, HALF:], h_woven[1][:])
-        pieces = ((0, 2 * P), (2 * P, 3 * P), (3 * P, 4 * P))
-        for start, stop in pieces:
-            targets = slice(HALF + start, HALF + stop)
-            quantise(z_codes[:, targets], z_scale[:, targets], woven_late[:, PACK * start : PACK * stop])
-        finish(3, HALF, 2 * P, late_codes[:, : 2 * P], nc.scalar.copy)
-        finish(4, T - 2 * P, P, late_codes[:, 2 * P : 3 * P], nc.vector.tensor_copy)
+        neighbours(1)
+        neighbours(2)
+        quantise_z(1)
+        quantise_z(2)
+        neighbours(3)
+        quantise_z(3)
+        finish(3, 1, nc.scalar.copy)
+        finish(4, 2, nc.scalar.copy)
         store(HALF, T - P)
-        finish(5, T - P, P, late_codes[:, 3 * P :], nc.vector.tensor_copy)
+        finish(5, 3, nc.vector.tensor_copy)
         store(T - P, T)

@@ -25,6 +25,7 @@ HALF = T // 2
 QUARTER = T // 4
 NEAR = 4
 PAIR = 2
+WINDOW = T + 352
 PIECES = ((0, HALF), (HALF, QUARTER), (T - 2 * P, P), (T - P, P))
 
 
@@ -58,14 +59,14 @@ def tile_picked_wsagecat_max_l_kernel(
         x_rows = x_words[0].rearrange("p n t -> p (n t)").bitcast(I32)
         for nodes in (slice(0, HALF), slice(HALF, T - QUARTER), slice(T - QUARTER, T)):
             nc.sync.dma_start(out=x_codes[:, nodes].bitcast(I32), in_=x_rows[:, nodes])
-        nc.sync.dma_start(lists[0][:], pos1)
         nc.sync.dma_start(lists[1][:], pos2)
-        w23_raw = keep.tile([P, 2, PACK, N], F32, align_bytes=64)
+        nc.sync.dma_start(lists[0][:], pos1)
+        w23_raw = keep.tile([P, 2, PACK, N], F32, tag="raw", align_bytes=64)
         for s, w in enumerate((w2, w3)):
             nc.sync.dma_start(out=w23_raw[:, s], in_=w.rearrange("(p j) n -> p j n", j=PACK))
 
         w1_woven = keep.tile([P, PACK, P, PACK], BF16, align_bytes=64)
-        w1_codes = keep.tile([P, PACK, P], U32, align_bytes=64)
+        w1_codes = keep.tile([P, PACK, P], U32, tag="weights", align_bytes=64)
         w1_scale = keep.tile([P, PACK, P], U8, align_bytes=64)
 
         def cast_w1(cast, u, t0, t1):
@@ -81,14 +82,14 @@ def tile_picked_wsagecat_max_l_kernel(
                 in_=w1_woven[:, t0:t1, :, :].rearrange("p t m j -> p (t m j)"),
             )
 
-        cast_w1(nc.vector.tensor_copy, 0, 2, 4)
-        cast_w1(nc.scalar.copy, 0, 0, 2)
-        cast_w1(nc.vector.tensor_copy, 1, 2, 3)
-        cast_w1(nc.vector.tensor_copy, 1, 3, 4)
-        cast_w1(nc.scalar.copy, 1, 0, 2)
-        quantise_w1(2, 3)
-        quantise_w1(3, 4)
-        quantise_w1(0, 2)
+        cast_w1(nc.vector.tensor_copy, 0, 0, 2)
+        cast_w1(nc.scalar.copy, 0, 2, 4)
+        cast_w1(nc.vector.tensor_copy, 1, 0, 1)
+        cast_w1(nc.vector.tensor_copy, 1, 1, 2)
+        cast_w1(nc.scalar.copy, 1, 2, 4)
+        quantise_w1(0, 1)
+        quantise_w1(1, 2)
+        quantise_w1(2, 4)
 
         def plane(t, start, stop):
             return h[:, t * T + start : t * T + stop]
@@ -113,13 +114,13 @@ def tile_picked_wsagecat_max_l_kernel(
                 nc.scalar.activation(plane(t, start, stop), acc_h[:, : stop - start], RELU)
 
         for a in range(3):
-            project(2 + a, 2, a * QUARTER, (a + 1) * QUARTER)
-        project(5, 2, T - 2 * P, T - P, on_vector=True)
-        project(0, 2, T - P, T)
-        later = ((3, 1), (1, 6), (0, 7))
+            project(2 + a, 0, a * QUARTER, (a + 1) * QUARTER)
+        project(5, 0, T - 2 * P, T - P, on_vector=True)
+        project(0, 0, T - P, T)
+        later = ((1, 1), (2, 6), (3, 7))
         for start in (BANK, 0):
             for t, b in later:
-                project(b, t, start, start + BANK, on_vector=True)
+                project(b, t, start, start + BANK)
 
         def near(rows, width):
             return rows.rearrange("p t (c i) -> p c t i", i=width)
@@ -130,52 +131,54 @@ def tile_picked_wsagecat_max_l_kernel(
         def weave(dst, rows):
             nc.gpsimd.tensor_scalar(dst.rearrange("p (c t) -> p c t", t=PACK), rows.rearrange("p t c -> p c t"), 1.0, 0.0, MULT, ADD)
 
-        h_codes = keep.tile([P, T + 2 * N], U32, align_bytes=64)
-        h_scale = keep.tile([P, T + 2 * N], U8, align_bytes=64)
-        w23_codes = h_codes[:, T:]
-        w23_scale = h_scale[:, T:]
+        codes = keep.tile([P, 2 * N + T], U32, align_bytes=64)
+        scale = keep.tile([P, 2 * N + T], U8, align_bytes=64)
+        w23_codes, h_codes = codes[:, : 2 * N], codes[:, 2 * N :]
+        w23_scale, h_scale = scale[:, : 2 * N], scale[:, 2 * N :]
         z_codes = keep.tile([P, T], U32, align_bytes=64)
         z_scale = keep.tile([P, T], U8, align_bytes=64)
         result = keep.tile([P, T], F32)
 
-        def quantise(codes, scale, values):
-            nc.vector.quantize_mx(out=codes.bitcast(FP8X4), scales=scale, in_=values)
+        def quantise(words, scales, values):
+            nc.vector.quantize_mx(out=words.bitcast(FP8X4), scales=scales, in_=values)
 
-        h_woven = keep.tile([P, PACK * (T + 2 * N)], BF16, align_bytes=64)
-        w23_woven = h_woven[:, PACK * T :]
-        for s in range(2):
-            weave(w23_woven[:, s * PACK * N : (s + 1) * PACK * N], w23_raw[:, s])
+        lower_woven = keep.tile([P, PACK * (2 * N + HALF)], BF16, align_bytes=64)
+        w23_woven = lower_woven[:, : PACK * 2 * N]
+        nc.gpsimd.tensor_scalar(
+            w23_woven.rearrange("p (s n j) -> p s n j", s=2, j=PACK), w23_raw[:].rearrange("p s j n -> p s n j"), 1.0, 0.0, MULT, ADD
+        )
         h_planes = h[:].rearrange("p (t c) -> p t c", t=PACK)
-        for q in reversed(range(4)):
-            weave(h_woven[:, q * PACK * QUARTER : (q + 1) * PACK * QUARTER], h_planes[:, :, q * QUARTER : (q + 1) * QUARTER])
+        upper_woven = keep.tile([P, PACK * HALF], BF16, tag="raw", align_bytes=64)
+        weave(upper_woven[:], h_planes[:, :, HALF:])
+        weave(lower_woven[:, PACK * 2 * N :], h_planes[:, :, :HALF])
 
-        picked = [keep.tile([P, 2, PACK, n], F32, name="picked%d" % u, align_bytes=64) for u, (first, n) in enumerate(PIECES)]
+        second = keep.tile([P, PACK, T], F32, align_bytes=64)
+        for t, first in ((0, 0), (0, HALF), (1, 0), (1, HALF)):
+            offsets = lists[1][:, first // 16 : (first + HALF) // 16]
+            nc.vector.tensor_copy(second[:, t, first : first + HALF], plane(t, 0, T).indirect(offsets))
+        nc.vector.tensor_copy(second[:, 2, :], plane(2, 0, WINDOW).indirect(lists[1][:]))
+        nc.vector.tensor_copy(second[:, 3, :HALF], plane(3, 0, T).indirect(lists[1][:, : HALF // 16]))
 
-        def gather(t, u, on_vector=False):
+        first_values = keep.tile([P, PACK * T], F32, tag="weights", align_bytes=64)
+
+        def piece(u):
             first, n = PIECES[u]
-            for d in range(2):
-                window = plane(t, 0, T).indirect(lists[d][:, first // 16 : (first + n) // 16])
-                if on_vector:
-                    nc.vector.tensor_copy(picked[u][:, d, t, :], window)
-                else:
-                    nc.scalar.activation(picked[u][:, d, t, :], window, COPY)
+            return first_values[:, PACK * first : PACK * (first + n)].rearrange("p (t c) -> p t c", t=PACK)
 
-        for u in range(4):
-            gather(2, u)
-        gather(3, 0)
-        gather(1, 0, on_vector=True)
-        gather(0, 0, on_vector=True)
-        gather(0, 1, on_vector=True)
-        for u in range(1, 4):
-            for t in (3, 1, 0)[: 2 if u == 1 else 3]:
-                gather(t, u)
+        for u, (first, n) in enumerate(PIECES):
+            for t in range(PACK):
+                offsets = lists[0][:, first // 16 : (first + n) // 16]
+                nc.scalar.activation(piece(u)[:, t], plane(t, 0, T).indirect(offsets), COPY)
+            if u:
+                offsets = lists[1][:, first // 16 : (first + n) // 16]
+                nc.scalar.activation(second[:, 3, first : first + n], plane(3, 0, T).indirect(offsets), COPY)
 
         z_woven = keep.tile([P, PACK * T], BF16, align_bytes=64)
 
         def neighbours(u):
             first, n = PIECES[u]
             values = z_woven[:, PACK * first : PACK * (first + n)]
-            nc.vector.tensor_tensor(woven(values, PAIR), near(picked[u][:, 0], PAIR), near(picked[u][:, 1], PAIR), MAX)
+            nc.vector.tensor_tensor(woven(values, PAIR), near(piece(u), PAIR), near(second[:, :, first : first + n], PAIR), MAX)
 
         def quantise_z(u):
             first, n = PIECES[u]
@@ -186,13 +189,13 @@ def tile_picked_wsagecat_max_l_kernel(
             first, n = PIECES[u]
             acc_o = bank(b, "acc_o")
             targets = slice(first, first + n)
-            for s, (codes, scale) in enumerate(((h_codes, h_scale), (z_codes, z_scale))):
+            for s, (words, scales) in enumerate(((h_codes, h_scale), (z_codes, z_scale))):
                 nc.tensor.matmul_mx(
                     out=acc_o[:, :n],
                     lhsT=w23_codes[:, s * N : (s + 1) * N].bitcast(FP8X4),
                     lhsT_scale=w23_scale[:, s * N : (s + 1) * N],
-                    rhs=codes[:, targets].bitcast(FP8X4),
-                    rhs_scale=scale[:, targets],
+                    rhs=words[:, targets].bitcast(FP8X4),
+                    rhs_scale=scales[:, targets],
                     start=(s == 0),
                     stop=(s == 1),
                 )
@@ -202,12 +205,14 @@ def tile_picked_wsagecat_max_l_kernel(
             nc.sync.dma_start(out=out[:, first:stop], in_=result[:, first:stop])
 
         neighbours(0)
-        quantise(h_codes[:, QUARTER:], h_scale[:, QUARTER:], h_woven[:, PACK * QUARTER :])
-        quantise(h_codes[:, :QUARTER], h_scale[:, :QUARTER], h_woven[:, : PACK * QUARTER])
+        both = (2 * N + HALF) // 2
+        for start in (0, both):
+            quantise(codes[:, start : start + both], scale[:, start : start + both], lower_woven[:, PACK * start : PACK * (start + both)])
         quantise_z(0)
         finish(2, 0, nc.scalar.copy)
         store(0, HALF)
         neighbours(1)
+        quantise(h_codes[:, HALF:], h_scale[:, HALF:], upper_woven[:])
         neighbours(2)
         quantise_z(1)
         quantise_z(2)

@@ -24,9 +24,11 @@ BANK = 512
 HALF = T // 2
 QUARTER = T // 4
 NEAR = 4
-PAIR = 2
 WINDOW = T + 352
-PIECES = ((0, HALF), (HALF, QUARTER), (T - 2 * P, P), (T - P, P))
+SHARE = HALF - 32
+LAST = 96
+PIECES = ((HALF, HALF), (QUARTER, QUARTER), (LAST, QUARTER - LAST), (0, LAST))
+GROUPS = ((HALF, HALF), (QUARTER, QUARTER), (P, P), (0, P))
 
 
 def tile_picked_wsagecat_max_l_kernel(
@@ -51,13 +53,14 @@ def tile_picked_wsagecat_max_l_kernel(
         w1_raw = [keep.tile([P, 2, H], F32, name="w1_raw%d" % u) for u in range(2)]
         for u in range(2):
             nc.sync.dma_start(out=w1_raw[u][:], in_=w1_rows[:, 2 * u : 2 * u + 2, :])
+        x_rows = x_words[0].rearrange("p n t -> p (n t)").bitcast(I32)
+        nc.sync.dma_start(out=x_codes[:, :QUARTER].bitcast(I32), in_=x_rows[:, :QUARTER])
         for q in range(4):
             nc.sync.dma_start(
                 out=x_scale[32 * q : 32 * q + 16, :].bitcast(I32),
                 in_=x_scales[0, 4 * q : 4 * q + 4, :].bitcast(I32).rearrange("r (a c) -> a r c", a=4),
             )
-        x_rows = x_words[0].rearrange("p n t -> p (n t)").bitcast(I32)
-        for nodes in (slice(0, HALF), slice(HALF, T - QUARTER), slice(T - QUARTER, T)):
+        for nodes in (slice(QUARTER, T - QUARTER), slice(T - QUARTER, T)):
             nc.sync.dma_start(out=x_codes[:, nodes].bitcast(I32), in_=x_rows[:, nodes])
         nc.sync.dma_start(lists[1][:], pos2)
         nc.sync.dma_start(lists[0][:], pos1)
@@ -82,14 +85,14 @@ def tile_picked_wsagecat_max_l_kernel(
                 in_=w1_woven[:, t0:t1, :, :].rearrange("p t m j -> p (t m j)"),
             )
 
-        cast_w1(nc.vector.tensor_copy, 0, 0, 2)
-        cast_w1(nc.scalar.copy, 0, 2, 4)
-        cast_w1(nc.vector.tensor_copy, 1, 0, 1)
-        cast_w1(nc.vector.tensor_copy, 1, 1, 2)
-        cast_w1(nc.scalar.copy, 1, 2, 4)
-        quantise_w1(0, 1)
-        quantise_w1(1, 2)
-        quantise_w1(2, 4)
+        cast_w1(nc.vector.tensor_copy, 0, 2, 4)
+        cast_w1(nc.scalar.copy, 0, 0, 2)
+        cast_w1(nc.vector.tensor_copy, 1, 3, 4)
+        cast_w1(nc.vector.tensor_copy, 1, 2, 3)
+        cast_w1(nc.scalar.copy, 1, 0, 2)
+        quantise_w1(3, 4)
+        quantise_w1(2, 3)
+        quantise_w1(0, 2)
 
         def plane(t, start, stop):
             return h[:, t * T + start : t * T + stop]
@@ -114,10 +117,10 @@ def tile_picked_wsagecat_max_l_kernel(
                 nc.scalar.activation(plane(t, start, stop), acc_h[:, : stop - start], RELU)
 
         for a in range(3):
-            project(2 + a, 0, a * QUARTER, (a + 1) * QUARTER)
-        project(5, 0, T - 2 * P, T - P, on_vector=True)
-        project(0, 0, T - P, T)
-        later = ((1, 1), (2, 6), (3, 7))
+            project(2 + a, 3, a * QUARTER, (a + 1) * QUARTER)
+        project(5, 3, T - 2 * P, T - P, on_vector=True)
+        project(0, 3, T - P, T)
+        later = ((2, 1), (1, 6), (0, 7))
         for start in (BANK, 0):
             for t, b in later:
                 project(b, t, start, start + BANK)
@@ -142,7 +145,9 @@ def tile_picked_wsagecat_max_l_kernel(
         def quantise(words, scales, values):
             nc.vector.quantize_mx(out=words.bitcast(FP8X4), scales=scales, in_=values)
 
-        lower_woven = keep.tile([P, PACK * (2 * N + HALF)], BF16, align_bytes=64)
+        both = (2 * N + HALF) // 2
+        shared_woven = keep.tile([P, PACK * T], BF16, align_bytes=64)
+        lower_woven = shared_woven[:, : PACK * 2 * both]
         w23_woven = lower_woven[:, : PACK * 2 * N]
         nc.gpsimd.tensor_scalar(
             w23_woven.rearrange("p (s n j) -> p s n j", s=2, j=PACK), w23_raw[:].rearrange("p s j n -> p s n j"), 1.0, 0.0, MULT, ADD
@@ -153,11 +158,12 @@ def tile_picked_wsagecat_max_l_kernel(
         weave(lower_woven[:, PACK * 2 * N :], h_planes[:, :, :HALF])
 
         second = keep.tile([P, PACK, T], F32, align_bytes=64)
-        for t, first in ((0, 0), (0, HALF), (1, 0), (1, HALF)):
+        for first in (0, HALF):
             offsets = lists[1][:, first // 16 : (first + HALF) // 16]
-            nc.vector.tensor_copy(second[:, t, first : first + HALF], plane(t, 0, T).indirect(offsets))
-        nc.vector.tensor_copy(second[:, 2, :], plane(2, 0, WINDOW).indirect(lists[1][:]))
-        nc.vector.tensor_copy(second[:, 3, :HALF], plane(3, 0, T).indirect(lists[1][:, : HALF // 16]))
+            nc.vector.tensor_copy(second[:, 3, first : first + HALF], plane(3, 0, T).indirect(offsets))
+        for t in (2, 1):
+            nc.vector.tensor_copy(second[:, t, :], plane(t, 0, WINDOW).indirect(lists[1][:]))
+        nc.vector.tensor_copy(second[:, 0, SHARE:], plane(0, 0, T).indirect(lists[1][:, SHARE // 16 :]))
 
         first_values = keep.tile([P, PACK * T], F32, tag="weights", align_bytes=64)
 
@@ -166,27 +172,27 @@ def tile_picked_wsagecat_max_l_kernel(
             return first_values[:, PACK * first : PACK * (first + n)].rearrange("p (t c) -> p t c", t=PACK)
 
         for u, (first, n) in enumerate(PIECES):
-            for t in range(PACK):
+            for t in reversed(range(PACK)):
                 offsets = lists[0][:, first // 16 : (first + n) // 16]
                 nc.scalar.activation(piece(u)[:, t], plane(t, 0, T).indirect(offsets), COPY)
-            if u:
-                offsets = lists[1][:, first // 16 : (first + n) // 16]
-                nc.scalar.activation(second[:, 3, first : first + n], plane(3, 0, T).indirect(offsets), COPY)
+            if u == 0:
+                nc.scalar.activation(second[:, 0, :SHARE], plane(0, 0, T).indirect(lists[1][:, : SHARE // 16]), COPY)
 
-        z_woven = keep.tile([P, PACK * T], BF16, align_bytes=64)
+        def z_woven(u):
+            first, n = PIECES[u]
+            return shared_woven[:, PACK * first : PACK * (first + n)]
 
         def neighbours(u):
             first, n = PIECES[u]
-            values = z_woven[:, PACK * first : PACK * (first + n)]
-            nc.vector.tensor_tensor(woven(values, PAIR), near(piece(u), PAIR), near(second[:, :, first : first + n], PAIR), MAX)
+            nc.vector.tensor_tensor(woven(z_woven(u), NEAR), near(piece(u), NEAR), near(second[:, :, first : first + n], NEAR), MAX)
 
         def quantise_z(u):
-            first, n = PIECES[u]
+            first, n = GROUPS[u]
             targets = slice(first, first + n)
-            quantise(z_codes[:, targets], z_scale[:, targets], z_woven[:, PACK * first : PACK * (first + n)])
+            quantise(z_codes[:, targets], z_scale[:, targets], shared_woven[:, PACK * first : PACK * (first + n)])
 
         def finish(b, u, copy):
-            first, n = PIECES[u]
+            first, n = GROUPS[u]
             acc_o = bank(b, "acc_o")
             targets = slice(first, first + n)
             for s, (words, scales) in enumerate(((h_codes, h_scale), (z_codes, z_scale))):
@@ -204,22 +210,21 @@ def tile_picked_wsagecat_max_l_kernel(
         def store(first, stop):
             nc.sync.dma_start(out=out[:, first:stop], in_=result[:, first:stop])
 
-        neighbours(0)
-        both = (2 * N + HALF) // 2
-        for start in (0, both):
-            quantise(codes[:, start : start + both], scale[:, start : start + both], lower_woven[:, PACK * start : PACK * (start + both)])
-        quantise_z(0)
-        finish(2, 0, nc.scalar.copy)
-        store(0, HALF)
-        neighbours(1)
         quantise(h_codes[:, HALF:], h_scale[:, HALF:], upper_woven[:])
+        for start in (both, 0):
+            quantise(codes[:, start : start + both], scale[:, start : start + both], lower_woven[:, PACK * start : PACK * (start + both)])
+        neighbours(0)
+        neighbours(1)
+        quantise_z(0)
         neighbours(2)
         quantise_z(1)
-        quantise_z(2)
         neighbours(3)
+        quantise_z(2)
         quantise_z(3)
+        finish(2, 0, nc.scalar.copy)
+        store(HALF, T)
         finish(3, 1, nc.scalar.copy)
+        store(QUARTER, HALF)
         finish(4, 2, nc.scalar.copy)
-        store(HALF, T - P)
         finish(5, 3, nc.vector.tensor_copy)
-        store(T - P, T)
+        store(0, QUARTER)

@@ -25,7 +25,7 @@ HALF = T // 2
 QUARTER = T // 4
 NEAR = 4
 WINDOW = T + 352
-SHARE = HALF - 32
+SHARE = HALF - 96
 LAST = 96
 PIECES = ((HALF, HALF), (QUARTER, QUARTER), (LAST, QUARTER - LAST), (0, LAST))
 GROUPS = ((HALF, HALF), (QUARTER, QUARTER), (P, P), (0, P))

@@ -25,7 +25,7 @@ HALF = T // 2
 QUARTER = T // 4
 NEAR = 4
 WINDOW = T + 352
-SHARE = HALF - 96
+SHARE = HALF - 64
 LAST = 96
 PIECES = ((HALF, HALF), (QUARTER, QUARTER), (LAST, QUARTER - LAST), (0, LAST))
 GROUPS = ((HALF, HALF), (QUARTER, QUARTER), (P, P), (0, P))
@@ -226,5 +226,6 @@ def tile_picked_wsagecat_max_l_kernel(
         finish(3, 1, nc.scalar.copy)
         store(QUARTER, HALF)
         finish(4, 2, nc.scalar.copy)
+        store(P, QUARTER)
         finish(5, 3, nc.vector.tensor_copy)
-        store(0, QUARTER)
+        store(0, P)

@@ -207,8 +207,8 @@ def tile_picked_wsagecat_max_l_kernel(
                 )
             copy(out=result[:, targets], in_=acc_o[:, :n])
 
-        def store(first, stop):
-            nc.sync.dma_start(out=out[:, first:stop], in_=result[:, first:stop])
+        def store(queue, first, stop):
+            queue.dma_start(out=out[:, first:stop], in_=result[:, first:stop])
 
         quantise(h_codes[:, HALF:], h_scale[:, HALF:], upper_woven[:])
         for start in (both, 0):
@@ -222,10 +222,9 @@ def tile_picked_wsagecat_max_l_kernel(
         quantise_z(2)
         quantise_z(3)
         finish(2, 0, nc.scalar.copy)
-        store(HALF, T)
+        store(nc.scalar, HALF, T)
         finish(3, 1, nc.scalar.copy)
-        store(QUARTER, HALF)
+        store(nc.scalar, QUARTER, HALF)
         finish(4, 2, nc.scalar.copy)
-        store(P, QUARTER)
         finish(5, 3, nc.vector.tensor_copy)
-        store(0, P)
+        store(nc.sync, 0, QUARTER)

@@ -120,10 +120,9 @@ def tile_picked_wsagecat_max_l_kernel(
             project(2 + a, 3, a * QUARTER, (a + 1) * QUARTER)
         project(5, 3, T - 2 * P, T - P, on_vector=True)
         project(0, 3, T - P, T)
-        later = ((2, 1), (1, 6), (0, 7))
-        for start in (BANK, 0):
-            for t, b in later:
-                project(b, t, start, start + BANK)
+        for start, stop, banks in ((T - QUARTER, T, (1, 6, 7)), (HALF, T - QUARTER, (5, 0, 4)), (0, HALF, (1, 6, 7))):
+            for t, b in zip((2, 1, 0), banks):
+                project(b, t, start, stop)
 
         def near(rows, width):
             return rows.rearrange("p t (c i) -> p c t i", i=width)
@@ -149,12 +148,12 @@ def tile_picked_wsagecat_max_l_kernel(
         shared_woven = keep.tile([P, PACK * T], BF16, align_bytes=64)
         lower_woven = shared_woven[:, : PACK * 2 * both]
         w23_woven = lower_woven[:, : PACK * 2 * N]
-        nc.gpsimd.tensor_scalar(
-            w23_woven.rearrange("p (s n j) -> p s n j", s=2, j=PACK), w23_raw[:].rearrange("p s j n -> p s n j"), 1.0, 0.0, MULT, ADD
-        )
+        for s in range(2):
+            weave(w23_woven[:, s * PACK * N : (s + 1) * PACK * N], w23_raw[:, s])
         h_planes = h[:].rearrange("p (t c) -> p t c", t=PACK)
         upper_woven = keep.tile([P, PACK * HALF], BF16, tag="raw", align_bytes=64)
-        weave(upper_woven[:], h_planes[:, :, HALF:])
+        for start in (T - QUARTER, HALF):
+            weave(upper_woven[:, PACK * (start - HALF) : PACK * (start - HALF + QUARTER)], h_planes[:, :, start : start + QUARTER])
         weave(lower_woven[:, PACK * 2 * N :], h_planes[:, :, :HALF])
 
         second = keep.tile([P, PACK, T], F32, align_bytes=64)

@@ -25,7 +25,7 @@ HALF = T // 2
 QUARTER = T // 4
 NEAR = 4
 WINDOW = T + 352
-SHARE = HALF - 64
+SHARE = HALF
 LAST = 96
 PIECES = ((HALF, HALF), (QUARTER, QUARTER), (LAST, QUARTER - LAST), (0, LAST))
 GROUPS = ((HALF, HALF), (QUARTER, QUARTER), (P, P), (0, P))
@@ -122,7 +122,7 @@ def tile_picked_wsagecat_max_l_kernel(
         project(0, 3, T - P, T)
         for start, stop, banks in ((T - QUARTER, T, (1, 6, 7)), (HALF, T - QUARTER, (5, 0, 4)), (0, HALF, (1, 6, 7))):
             for t, b in zip((2, 1, 0), banks):
-                project(b, t, start, stop)
+                project(b, t, start, stop, on_vector=(b, stop) == (1, T))
 
         def near(rows, width):
             return rows.rearrange("p t (c i) -> p c t i", i=width)

@@ -26,6 +26,7 @@ QUARTER = T // 4
 NEAR = 4
 WINDOW = T + 352
 SHARE = HALF
+WARM = 6
 LAST = 96
 PIECES = ((HALF, HALF), (QUARTER, QUARTER), (LAST, QUARTER - LAST), (0, LAST))
 GROUPS = ((HALF, HALF), (QUARTER, QUARTER), (P, P), (0, P))
@@ -85,7 +86,23 @@ def tile_picked_wsagecat_max_l_kernel(
                 in_=w1_woven[:, t0:t1, :, :].rearrange("p t m j -> p (t m j)"),
             )
 
+        warm_values = keep.tile([P, H], BF16, align_bytes=64)
+        warm_codes = keep.tile([P, P], U32, align_bytes=64)
+        warm_scale = keep.tile([P, P], U8, align_bytes=64)
+        nc.vector.tensor_copy(out=warm_values[:], in_=w1_raw[0][:, 0, :])
         cast_w1(nc.vector.tensor_copy, 0, 2, 4)
+        nc.vector.quantize_mx(out=warm_codes[:].bitcast(FP8X4), scales=warm_scale[:], in_=warm_values[:])
+        acc_warm = bank(1, "acc_warm")
+        for n in range(WARM):
+            nc.tensor.matmul_mx(
+                out=acc_warm[:32, (n % PACK) * P : (n % PACK + 1) * P],
+                lhsT=warm_codes[:, :32].bitcast(FP8X4),
+                lhsT_scale=warm_scale[:, :32],
+                rhs=warm_codes[:].bitcast(FP8X4),
+                rhs_scale=warm_scale[:],
+                start=True,
+                stop=True,
+            )
         cast_w1(nc.scalar.copy, 0, 0, 2)
         cast_w1(nc.vector.tensor_copy, 1, 3, 4)
         cast_w1(nc.vector.tensor_copy, 1, 2, 3)

@@ -26,7 +26,8 @@ QUARTER = T // 4
 NEAR = 4
 WINDOW = T + 352
 SHARE = HALF
-WARM = 6
+SEED = P
+WARM_NARROW, WARM_WIDE = 3, 3
 LAST = 96
 PIECES = ((HALF, HALF), (QUARTER, QUARTER), (LAST, QUARTER - LAST), (0, LAST))
 GROUPS = ((HALF, HALF), (QUARTER, QUARTER), (P, P), (0, P))
@@ -50,33 +51,33 @@ def tile_picked_wsagecat_max_l_kernel(
 
         nc.vector.memset(x_scale[:].bitcast(I32), 0)
 
-        w1_rows = w1.rearrange("(p j) c -> p j c", j=PACK)
-        w1_raw = [keep.tile([P, 2, H], F32, name="w1_raw%d" % u) for u in range(2)]
-        for u in range(2):
-            nc.sync.dma_start(out=w1_raw[u][:], in_=w1_rows[:, 2 * u : 2 * u + 2, :])
+        w1_rows = w1.rearrange("(p j) c -> p (j c)", j=PACK)
+        w1_raw = [keep.tile([P, 2 * H], F32, name="w1_raw%d" % u) for u in range(2)]
+        nc.sync.dma_start(out=w1_raw[0][:, :SEED], in_=w1_rows[:, :SEED])
+        nc.sync.dma_start(out=w1_raw[0][:, SEED:], in_=w1_rows[:, SEED : 2 * H])
+        nc.sync.dma_start(out=w1_raw[1][:], in_=w1_rows[:, 2 * H :])
         x_rows = x_words[0].rearrange("p n t -> p (n t)").bitcast(I32)
-        nc.sync.dma_start(out=x_codes[:, :QUARTER].bitcast(I32), in_=x_rows[:, :QUARTER])
         for q in range(4):
             nc.sync.dma_start(
                 out=x_scale[32 * q : 32 * q + 16, :].bitcast(I32),
                 in_=x_scales[0, 4 * q : 4 * q + 4, :].bitcast(I32).rearrange("r (a c) -> a r c", a=4),
             )
-        for nodes in (slice(QUARTER, T - QUARTER), slice(T - QUARTER, T)):
+        for nodes in (slice(0, HALF), slice(HALF, T)):
             nc.sync.dma_start(out=x_codes[:, nodes].bitcast(I32), in_=x_rows[:, nodes])
-        nc.sync.dma_start(lists[1][:], pos2)
-        nc.sync.dma_start(lists[0][:], pos1)
         w23_raw = keep.tile([P, 2, PACK, N], F32, tag="raw", align_bytes=64)
-        for s, w in enumerate((w2, w3)):
-            nc.sync.dma_start(out=w23_raw[:, s], in_=w.rearrange("(p j) n -> p j n", j=PACK))
+        nc.sync.dma_start(out=w23_raw[:, 0], in_=w2.rearrange("(p j) n -> p j n", j=PACK))
+        nc.sync.dma_start(lists[1][:], pos2)
+        nc.sync.dma_start(out=w23_raw[:, 1], in_=w3.rearrange("(p j) n -> p j n", j=PACK))
+        nc.sync.dma_start(lists[0][:], pos1)
 
         w1_woven = keep.tile([P, PACK, P, PACK], BF16, align_bytes=64)
         w1_codes = keep.tile([P, PACK, P], U32, tag="weights", align_bytes=64)
         w1_scale = keep.tile([P, PACK, P], U8, align_bytes=64)
 
-        def cast_w1(cast, u, t0, t1):
+        def cast_w1(cast, u, t0, t1, m0=0, m1=P):
             cast(
-                out=w1_woven[:, t0:t1, :, 2 * u : 2 * u + 2].rearrange("p t m j -> p m j t"),
-                in_=w1_raw[u][:].rearrange("p j (m t) -> p m j t", t=PACK)[:, :, :, t0:t1],
+                out=w1_woven[:, t0:t1, m0:m1, 2 * u : 2 * u + 2].rearrange("p t m j -> p m j t"),
+                in_=w1_raw[u][:].rearrange("p (j m t) -> p m j t", j=2, t=PACK)[:, m0:m1, :, t0:t1],
             )
 
         def quantise_w1(t0, t1):
@@ -86,24 +87,30 @@ def tile_picked_wsagecat_max_l_kernel(
                 in_=w1_woven[:, t0:t1, :, :].rearrange("p t m j -> p (t m j)"),
             )
 
-        warm_values = keep.tile([P, H], BF16, align_bytes=64)
-        warm_codes = keep.tile([P, P], U32, align_bytes=64)
-        warm_scale = keep.tile([P, P], U8, align_bytes=64)
-        nc.vector.tensor_copy(out=warm_values[:], in_=w1_raw[0][:, 0, :])
-        cast_w1(nc.vector.tensor_copy, 0, 2, 4)
-        nc.vector.quantize_mx(out=warm_codes[:].bitcast(FP8X4), scales=warm_scale[:], in_=warm_values[:])
+        warm_values = keep.tile([P, PACK, SEED], BF16, align_bytes=64)
+        warm_codes = keep.tile([P, BANK], U32, align_bytes=64)
+        warm_scale = keep.tile([P, BANK], U8, align_bytes=64)
+        nc.vector.tensor_copy(out=warm_values[:], in_=w1_raw[0][:, :SEED].unsqueeze(1).to_broadcast([P, PACK, SEED]))
+        for c in range(0, BANK, P):
+            nc.vector.quantize_mx(
+                out=warm_codes[:, c : c + P].bitcast(FP8X4),
+                scales=warm_scale[:, c : c + P],
+                in_=warm_values[:].rearrange("p r c -> p (r c)"),
+            )
         acc_warm = bank(1, "acc_warm")
-        for n in range(WARM):
+        for n in (P,) * WARM_NARROW + (BANK,) * WARM_WIDE:
             nc.tensor.matmul_mx(
-                out=acc_warm[:32, (n % PACK) * P : (n % PACK + 1) * P],
+                out=acc_warm[:32, :n],
                 lhsT=warm_codes[:, :32].bitcast(FP8X4),
                 lhsT_scale=warm_scale[:, :32],
-                rhs=warm_codes[:].bitcast(FP8X4),
-                rhs_scale=warm_scale[:],
+                rhs=warm_codes[:, :n].bitcast(FP8X4),
+                rhs_scale=warm_scale[:, :n],
                 start=True,
                 stop=True,
             )
-        cast_w1(nc.scalar.copy, 0, 0, 2)
+        cast_w1(nc.vector.tensor_copy, 0, 2, 4)
+        cast_w1(nc.vector.tensor_copy, 0, 0, 2, 0, SEED // PACK)
+        cast_w1(nc.scalar.copy, 0, 0, 2, SEED // PACK, P)
         cast_w1(nc.vector.tensor_copy, 1, 3, 4)
         cast_w1(nc.vector.tensor_copy, 1, 2, 3)
         cast_w1(nc.scalar.copy, 1, 0, 2)

@@ -25,7 +25,7 @@ HALF = T // 2
 QUARTER = T // 4
 NEAR = 4
 WINDOW = T + 352
-SHARE = HALF
+SHARE = 608
 SEED = P
 WARM_NARROW, WARM_WIDE = 3, 3
 LAST = 96
@@ -140,10 +140,8 @@ def tile_picked_wsagecat_max_l_kernel(
             else:
                 nc.scalar.activation(plane(t, start, stop), acc_h[:, : stop - start], RELU)
 
-        for a in range(3):
-            project(2 + a, 3, a * QUARTER, (a + 1) * QUARTER)
-        project(5, 3, T - 2 * P, T - P, on_vector=True)
-        project(0, 3, T - P, T)
+        for a, b in enumerate((2, 3, 4, 5)):
+            project(b, 3, a * QUARTER, (a + 1) * QUARTER, on_vector=a % 2 == 1)
         for start, stop, banks in ((T - QUARTER, T, (1, 6, 7)), (HALF, T - QUARTER, (5, 0, 4)), (0, HALF, (1, 6, 7))):
             for t, b in zip((2, 1, 0), banks):
                 project(b, t, start, stop, on_vector=(b, stop) == (1, T))
@@ -199,7 +197,7 @@ def tile_picked_wsagecat_max_l_kernel(
                 offsets = lists[0][:, first // 16 : (first + n) // 16]
                 nc.scalar.activation(piece(u)[:, t], plane(t, 0, T).indirect(offsets), COPY)
             if u == 0:
-                nc.scalar.activation(second[:, 0, :SHARE], plane(0, 0, T).indirect(lists[1][:, : SHARE // 16]), COPY)
+                nc.scalar.activation(second[:, 0, :SHARE], plane(0, 0, WINDOW).indirect(lists[1][:, : SHARE // 16]), COPY)
 
         def z_woven(u):
             first, n = PIECES[u]

from contextlib import ExitStack

import concourse.mybir as mybir

K, T, H, N = 512, 1024, 512, 128
FLOPS = 2 * K * H * T + 2 * 2 * H * N * T

F32 = mybir.dt.float32
BF16 = mybir.dt.bfloat16
I32 = mybir.dt.int32
U32 = mybir.dt.uint32
U16 = mybir.dt.uint16
U8 = mybir.dt.uint8
FP8X4 = mybir.dt.float8_e4m3fn_x4
MAX = mybir.AluOpType.max
ADD = mybir.AluOpType.add
MULT = mybir.AluOpType.mult
RELU = mybir.ActivationFunctionType.Relu
COPY = mybir.ActivationFunctionType.Copy

P = 128
PACK = 4
BANK = 512
HALF = T // 2
QUARTER = T // 4
NEAR = 4
WINDOW = T + 352
SHARE = 608
SEED = P
WARM_NARROW, WARM_WIDE = 3, 3
LAST = 96
PIECES = ((HALF, HALF), (QUARTER, QUARTER), (LAST, QUARTER - LAST), (0, LAST))
GROUPS = ((HALF, HALF), (QUARTER, QUARTER), (P, P), (0, P))


def tile_picked_wsagecat_max_l_kernel(
    tc, x_words, x_scales, w1, w2, w3, pos1, pos2, out
):
    nc = tc.nc
    with ExitStack() as ctx:
        keep = ctx.enter_context(tc.tile_pool(name="keep", bufs=1))
        psum = ctx.enter_context(tc.psum_pool(name="psum", bufs=1))

        def bank(b, role):
            return psum.tile([P, BANK], F32, name=role, tag="bank%d" % b)

        lists = [keep.tile([P, T // 16], U16, name="list%d" % d) for d in range(2)]
        x_codes = keep.tile([P, T], U32, align_bytes=64)
        x_scale = keep.tile([P, QUARTER], U8, align_bytes=64)
        h = keep.tile([P, PACK * T], F32, align_bytes=64)

        nc.vector.memset(x_scale[:].bitcast(I32), 0)

        w1_rows = w1.rearrange("(p j) c -> p (j c)", j=PACK)
        w1_raw = [keep.tile([P, 2 * H], F32, name="w1_raw%d" % u) for u in range(2)]
        nc.sync.dma_start(out=w1_raw[0][:, :SEED], in_=w1_rows[:, :SEED])
        nc.sync.dma_start(out=w1_raw[0][:, SEED:], in_=w1_rows[:, SEED : 2 * H])
        nc.sync.dma_start(out=w1_raw[1][:], in_=w1_rows[:, 2 * H :])
        x_rows = x_words[0].rearrange("p n t -> p (n t)").bitcast(I32)
        for q in range(4):
            nc.sync.dma_start(
                out=x_scale[32 * q : 32 * q + 16, :].bitcast(I32),
                in_=x_scales[0, 4 * q : 4 * q + 4, :].bitcast(I32).rearrange("r (a c) -> a r c", a=4),
            )
        for nodes in (slice(0, HALF), slice(HALF, T)):
            nc.sync.dma_start(out=x_codes[:, nodes].bitcast(I32), in_=x_rows[:, nodes])
        w23_raw = keep.tile([P, 2, PACK, N], F32, tag="raw", align_bytes=64)
        nc.sync.dma_start(out=w23_raw[:, 0], in_=w2.rearrange("(p j) n -> p j n", j=PACK))
        nc.sync.dma_start(lists[1][:], pos2)
        nc.sync.dma_start(out=w23_raw[:, 1], in_=w3.rearrange("(p j) n -> p j n", j=PACK))
        nc.sync.dma_start(lists[0][:], pos1)

        w1_woven = keep.tile([P, PACK, P, PACK], BF16, align_bytes=64)
        w1_codes = keep.tile([P, PACK, P], U32, tag="weights", align_bytes=64)
        w1_scale = keep.tile([P, PACK, P], U8, align_bytes=64)

        def cast_w1(cast, u, t0, t1, m0=0, m1=P):
            cast(
                out=w1_woven[:, t0:t1, m0:m1, 2 * u : 2 * u + 2].rearrange("p t m j -> p m j t"),
                in_=w1_raw[u][:].rearrange("p (j m t) -> p m j t", j=2, t=PACK)[:, m0:m1, :, t0:t1],
            )

        def quantise_w1(t0, t1):
            nc.vector.quantize_mx(
                out=w1_codes[:, t0:t1, :].rearrange("p t m -> p (t m)").bitcast(FP8X4),
                scales=w1_scale[:, t0:t1, :].rearrange("p t m -> p (t m)"),
                in_=w1_woven[:, t0:t1, :, :].rearrange("p t m j -> p (t m j)"),
            )

        warm_values = keep.tile([P, PACK, SEED], BF16, align_bytes=64)
        warm_codes = keep.tile([P, BANK], U32, align_bytes=64)
        warm_scale = keep.tile([P, BANK], U8, align_bytes=64)
        nc.vector.tensor_copy(out=warm_values[:], in_=w1_raw[0][:, :SEED].unsqueeze(1).to_broadcast([P, PACK, SEED]))
        for c in range(0, BANK, P):
            nc.vector.quantize_mx(
                out=warm_codes[:, c : c + P].bitcast(FP8X4),
                scales=warm_scale[:, c : c + P],
                in_=warm_values[:].rearrange("p r c -> p (r c)"),
            )
        acc_warm = bank(1, "acc_warm")
        for n in (P,) * WARM_NARROW + (BANK,) * WARM_WIDE:
            nc.tensor.matmul_mx(
                out=acc_warm[:32, :n],
                lhsT=warm_codes[:, :32].bitcast(FP8X4),
                lhsT_scale=warm_scale[:, :32],
                rhs=warm_codes[:, :n].bitcast(FP8X4),
                rhs_scale=warm_scale[:, :n],
                start=True,
                stop=True,
            )
        cast_w1(nc.vector.tensor_copy, 0, 2, 4)
        cast_w1(nc.vector.tensor_copy, 0, 0, 2, 0, SEED // PACK)
        cast_w1(nc.scalar.copy, 0, 0, 2, SEED // PACK, P)
        cast_w1(nc.vector.tensor_copy, 1, 3, 4)
        cast_w1(nc.vector.tensor_copy, 1, 2, 3)
        cast_w1(nc.scalar.copy, 1, 0, 2)
        quantise_w1(3, 4)
        quantise_w1(2, 3)
        quantise_w1(0, 2)

        def plane(t, start, stop):
            return h[:, t * T + start : t * T + stop]

        def project(b, t, start, stop, on_vector=False):
            acc_h = bank(b, "acc_h")
            for b0 in reversed(range(start, stop, QUARTER)):
                b1 = min(b0 + QUARTER, stop)
                a, within = divmod(b0, QUARTER)
                nc.tensor.matmul_mx(
                    out=acc_h[:, b0 - start : b1 - start],
                    lhsT=w1_codes[:, t, :].bitcast(FP8X4),
                    lhsT_scale=w1_scale[:, t, :],
                    rhs=x_codes[:, b0:b1].bitcast(FP8X4),
                    rhs_scale=x_scale[4 * a :, within : within + b1 - b0],
                    start=True,
                    stop=True,
                )
            if on_vector:
                nc.vector.tensor_scalar_max(plane(t, start, stop), acc_h[:, : stop - start], 0.0)
            else:
                nc.scalar.activation(plane(t, start, stop), acc_h[:, : stop - start], RELU)

        for a, b in enumerate((2, 3, 4, 5)):
            project(b, 3, a * QUARTER, (a + 1) * QUARTER, on_vector=a % 2 == 1)
        for start, stop, banks in ((T - QUARTER, T, (1, 6, 7)), (HALF, T - QUARTER, (5, 0, 4)), (0, HALF, (1, 6, 7))):
            for t, b in zip((2, 1, 0), banks):
                project(b, t, start, stop, on_vector=(b, stop) == (1, T))

        def near(rows, width):
            return rows.rearrange("p t (c i) -> p c t i", i=width)

        def woven(values, width):
            return values.rearrange("p (c i t) -> p c t i", i=width, t=PACK)

        def weave(dst, rows):
            nc.gpsimd.tensor_scalar(dst.rearrange("p (c t) -> p c t", t=PACK), rows.rearrange("p t c -> p c t"), 1.0, 0.0, MULT, ADD)

        codes = keep.tile([P, 2 * N + T], U32, align_bytes=64)
        scale = keep.tile([P, 2 * N + T], U8, align_bytes=64)
        w23_codes, h_codes = codes[:, : 2 * N], codes[:, 2 * N :]
        w23_scale, h_scale = scale[:, : 2 * N], scale[:, 2 * N :]
        z_codes = keep.tile([P, T], U32, align_bytes=64)
        z_scale = keep.tile([P, T], U8, align_bytes=64)
        result = keep.tile([P, T], F32)

        def quantise(words, scales, values):
            nc.vector.quantize_mx(out=words.bitcast(FP8X4), scales=scales, in_=values)

        both = (2 * N + HALF) // 2
        shared_woven = keep.tile([P, PACK * T], BF16, align_bytes=64)
        lower_woven = shared_woven[:, : PACK * 2 * both]
        w23_woven = lower_woven[:, : PACK * 2 * N]
        for s in range(2):
            weave(w23_woven[:, s * PACK * N : (s + 1) * PACK * N], w23_raw[:, s])
        h_planes = h[:].rearrange("p (t c) -> p t c", t=PACK)
        upper_woven = keep.tile([P, PACK * HALF], BF16, tag="raw", align_bytes=64)
        for start in (T - QUARTER, HALF):
            weave(upper_woven[:, PACK * (start - HALF) : PACK * (start - HALF + QUARTER)], h_planes[:, :, start : start + QUARTER])
        weave(lower_woven[:, PACK * 2 * N :], h_planes[:, :, :HALF])

        second = keep.tile([P, PACK, T], F32, align_bytes=64)
        for first in (0, HALF):
            offsets = lists[1][:, first // 16 : (first + HALF) // 16]
            nc.vector.tensor_copy(second[:, 3, first : first + HALF], plane(3, 0, T).indirect(offsets))
        for t in (2, 1):
            nc.vector.tensor_copy(second[:, t, :], plane(t, 0, WINDOW).indirect(lists[1][:]))
        nc.vector.tensor_copy(second[:, 0, SHARE:], plane(0, 0, T).indirect(lists[1][:, SHARE // 16 :]))

        first_values = keep.tile([P, PACK * T], F32, tag="weights", align_bytes=64)

        def piece(u):
            first, n = PIECES[u]
            return first_values[:, PACK * first : PACK * (first + n)].rearrange("p (t c) -> p t c", t=PACK)

        for u, (first, n) in enumerate(PIECES):
            for t in reversed(range(PACK)):
                offsets = lists[0][:, first // 16 : (first + n) // 16]
                nc.scalar.activation(piece(u)[:, t], plane(t, 0, T).indirect(offsets), COPY)
            if u == 0:
                nc.scalar.activation(second[:, 0, :SHARE], plane(0, 0, WINDOW).indirect(lists[1][:, : SHARE // 16]), COPY)

        def z_woven(u):
            first, n = PIECES[u]
            return shared_woven[:, PACK * first : PACK * (first + n)]

        def neighbours(u):
            first, n = PIECES[u]
            nc.vector.tensor_tensor(woven(z_woven(u), NEAR), near(piece(u), NEAR), near(second[:, :, first : first + n], NEAR), MAX)

        def quantise_z(u):
            first, n = GROUPS[u]
            targets = slice(first, first + n)
            quantise(z_codes[:, targets], z_scale[:, targets], shared_woven[:, PACK * first : PACK * (first + n)])

        def finish(b, u, copy):
            first, n = GROUPS[u]
            acc_o = bank(b, "acc_o")
            targets = slice(first, first + n)
            for s, (words, scales) in enumerate(((h_codes, h_scale), (z_codes, z_scale))):
                nc.tensor.matmul_mx(
                    out=acc_o[:, :n],
                    lhsT=w23_codes[:, s * N : (s + 1) * N].bitcast(FP8X4),
                    lhsT_scale=w23_scale[:, s * N : (s + 1) * N],
                    rhs=words[:, targets].bitcast(FP8X4),
                    rhs_scale=scales[:, targets],
                    start=(s == 0),
                    stop=(s == 1),
                )
            copy(out=result[:, targets], in_=acc_o[:, :n])

        def store(queue, first, stop):
            queue.dma_start(out=out[:, first:stop], in_=result[:, first:stop])

        quantise(h_codes[:, HALF:], h_scale[:, HALF:], upper_woven[:])
        for start in (both, 0):
            quantise(codes[:, start : start + both], scale[:, start : start + both], lower_woven[:, PACK * start : PACK * (start + both)])
        neighbours(0)
        neighbours(1)
        quantise_z(0)
        neighbours(2)
        quantise_z(1)
        neighbours(3)
        quantise_z(2)
        quantise_z(3)
        finish(2, 0, nc.scalar.copy)
        store(nc.scalar, HALF, T)
        finish(3, 1, nc.scalar.copy)
        store(nc.scalar, QUARTER, HALF)
        finish(4, 2, nc.scalar.copy)
        finish(5, 3, nc.vector.tensor_copy)
        store(nc.sync, 0, QUARTER)
